import numpy as np
import ml_dtypes


def mxq(x, axis, fmt="e4m3"):
    dtype, down = {"e4m3": (ml_dtypes.float8_e4m3fn, 7), "e5m2": (ml_dtypes.float8_e5m2, 14)}[fmt]
    v = np.moveaxis(np.asarray(x, np.float32).astype(ml_dtypes.bfloat16).astype(np.float64), axis, -1)
    blocks = v.reshape(v.shape[:-1] + (-1, 32))
    amax = np.abs(blocks).max(-1, keepdims=True)
    byte = np.maximum(np.where(amax > 0, np.frexp(amax)[1] - 1 + 127, 0) - down, 1)
    scale = np.exp2(byte - 127.0)
    codes = (blocks / scale).astype(np.float32).astype(dtype).astype(np.float64)
    return np.moveaxis((codes * scale).reshape(v.shape), -1, axis)


WIDE = False


def mx_kscale(k):
    if not WIDE:
        return np.ones(k)
    levels = np.array([10, -10, 5, -5, 0])
    if k % 512:
        return np.exp2(np.random.permutation(np.resize(levels, k // 32))).repeat(32)
    a = np.empty((k // 512, 16))
    for p in range(k // 512):
        a[p, :8] = np.random.permutation(np.resize(levels, 8))
        for g in range(8):
            far = levels[np.abs(levels - a[p, g]) >= 10]
            a[p, g + 8] = far[np.random.randint(len(far))]
    return np.exp2(a.ravel()).repeat(32)


def f64(x):
    return np.asarray(x).astype(np.float64)


def striped(idx):
    return np.tile(idx.reshape(-1, 16).T, (8, 1)).astype(np.uint16)


def unstriped(offs):
    return offs[:16].T.reshape(-1).astype(np.int64)


def striped8(idx):
    return np.concatenate([x.reshape(-1, 16).T for x in idx]).astype(np.uint16)


def runs(offs, k):
    lists = np.stack([offs[16 * r : 16 * r + 16].T.reshape(-1) for r in range(8)]).astype(np.int64)
    return lists[np.arange(k) % 512 // 64]


def pack_weight(w):
    k, n = w.shape
    w = f64(np.asarray(w, np.float32).astype(ml_dtypes.bfloat16)).reshape(k // 32, 32, n)
    amax = np.abs(w).max(1)
    byte = np.clip(np.where(amax > 0, np.frexp(amax)[1] - 1 + 127 - 7, 1), 1, 254)
    scaled = (w * np.exp2(127.0 - byte)[:, None, :]).reshape(k, n).astype(np.float32)
    words = np.ascontiguousarray(scaled.reshape(k // 512, 128, 4, n).transpose(0, 1, 3, 2)).astype(ml_dtypes.float8_e4m3fn).view(np.uint8)
    return words, np.ascontiguousarray(byte.astype(np.uint8).reshape(k // 512, 16, n))


def unpack_weight(words, scales):
    g, p, n, _ = words.shape
    vals = np.ascontiguousarray(words).view(ml_dtypes.float8_e4m3fn).astype(np.float64) * np.repeat(np.exp2(scales.astype(np.float64) - 127.0), 8, axis=1)[..., None]
    return vals.transpose(0, 1, 3, 2).reshape(g * 512, n)


def sigmoid(v):
    return 1.0 / (1.0 + np.exp(-np.maximum(v, -700.0)))


K, T, S, V, N, H = 512, 2048, 1024, 512, 512, 512


def setup_inputs():
    n = np.random.standard_normal
    s = mx_kscale(K)[:, None]
    u = mx_kscale(H)
    packed_xT = pack_weight(n((K, T)) * s)
    return {
        "x_words": packed_xT[0],
        "x_scales": packed_xT[1],
        "w1": (n((K, H)) / np.sqrt(K) / s).astype(np.float32),
        "w2": (n((K, H)) / np.sqrt(K) / s * u).astype(np.float32),
        "w3": (n((H, N)) / np.sqrt(H) / u[:, None]).astype(np.float32),
        "offs": striped(np.random.permutation(T)[:S]),
        "left": striped8(np.stack([np.random.permutation(S)[:V] for _ in range(8)])),
        "right": striped8(np.stack([np.random.permutation(S)[:V] for _ in range(8)])),
    }


def reference(x_words, x_scales, w1, w2, w3, offs, left, right):
    xq = unpack_weight(x_words, x_scales)[:, unstriped(offs)]
    val = mxq(f64(w2), 0, "e4m3").T @ xq
    vr = val[np.arange(H)[:, None], runs(right, H)]
    s = mxq(f64(w1), 0, "e4m3").T @ xq
    q = sigmoid(s[np.arange(H)[:, None], runs(left, H)] - (s[np.arange(H)[:, None], runs(right, H)]))
    z = vr + q * (val[np.arange(H)[:, None], runs(left, H)] - vr)
    return mxq(f64(w3), 0, "e4m3").T @ mxq(z, 0, "e4m3")

@@ -1,0 +1,206 @@
+from contextlib import ExitStack
+
+import concourse.mybir as mybir
+
+K, T, S, V, N, H = 512, 2048, 1024, 512, 512, 512
+FLOPS = 2 * K * H * S * 2 + 2 * H * N * V
+
+F32 = mybir.dt.float32
+BF16 = mybir.dt.bfloat16
+I32 = mybir.dt.int32
+U32 = mybir.dt.uint32
+U16 = mybir.dt.uint16
+U8 = mybir.dt.uint8
+FP8X4 = mybir.dt.float8_e4m3fn_x4
+ALU = mybir.AluOpType
+SIGMOID = mybir.ActivationFunctionType.Sigmoid
+
+P = 128
+PACK = 4
+BANK = 512
+PIECES = ((0, 256), (256, 384), (384, 512))
+
+
+def tile_picked_tourney_none_p_kernel(
+    tc, x_words, x_scales, w1, w2, w3, offs, left, right, out
+):
+    nc = tc.nc
+    with ExitStack() as ctx:
+        lists = ctx.enter_context(tc.tile_pool(name="lists", bufs=1))
+        keep = ctx.enter_context(tc.tile_pool(name="keep", bufs=1))
+        psum = ctx.enter_context(tc.psum_pool(name="psum", bufs=8))
+
+        offs_sb = lists.tile([P, S // 16], U16, name="offs_sb")
+        left_sb = lists.tile([P, V // 16], U16, name="left_sb")
+        right_sb = lists.tile([P, V // 16], U16, name="right_sb")
+
+        shared = ctx.enter_context(tc.tile_pool(name="shared", bufs=1))
+        scale_table = shared.tile([P, T], U8, name="scale_table", offset=7168)
+        word_table = keep.tile([P, T], I32, name="word_table", tag="words_then_w3")
+        warm = keep.tile([P, 2], F32, name="warm", tag="warm_then_w1")
+
+        nc.vector.memset(scale_table[:].bitcast(I32), 0)
+        nc.gpsimd.memset(warm[:, 0:1], 0.0)
+        nc.sync.dma_start(offs_sb[:], offs)
+        nc.scalar.dma_start(word_table[:], x_words[0].rearrange("p n r -> p (n r)").bitcast(I32))
+        for q in range(4):
+            nc.sync.dma_start(
+                scale_table[32 * q : 32 * q + 4, :].bitcast(I32),
+                x_scales[0, 4 * q : 4 * q + 4, :].bitcast(I32),
+            )
+        nc.sync.dma_start(right_sb[:], right)
+        nc.sync.dma_start(left_sb[:], left)
+        nc.scalar.activation(warm[:, 1:2], warm[:, 0:1], SIGMOID)
+        w1_raw = keep.tile([P, PACK, H], F32, name="w1_raw", tag="warm_then_w1")
+        nc.sync.dma_start(w1_raw[:], w1.rearrange("(p j) c -> p j c", j=PACK))
+
+        x_scale = keep.tile([P, S], U8, name="x_scale", align_bytes=64)
+        nc.vector.tensor_copy(x_scale[:], scale_table[:].indirect(offs_sb[:]))
+        w2_raw = shared.tile([P, PACK, H], F32, name="w2_raw", offset=0)
+        nc.sync.dma_start(w2_raw[:], w2.rearrange("(p j) c -> p j c", j=PACK))
+
+        x_codes = shared.tile([P, S], U32, name="x_codes", offset=8192, align_bytes=64)
+        for h in range(S // BANK):
+            nc.vector.tensor_copy(
+                x_codes[:, h * BANK : (h + 1) * BANK],
+                word_table[:].bitcast(U32).indirect(offs_sb[:, h * BANK // 16 : (h + 1) * BANK // 16]),
+            )
+        w3_raw = keep.tile([P, PACK, N], F32, name="w3_raw", tag="words_then_w3")
+        w3_rows = w3.rearrange("(b t r) n -> t b r n", t=PACK, r=8)
+        for t in range(PACK):
+            nc.sync.dma_start(w3_raw[:, t, :], w3_rows[t])
+
+        def interleave(copy, grouped, raw, t):
+            copy(
+                grouped.rearrange("p (b h i) j -> p b h j i", h=2, i=4),
+                raw[:].rearrange("p j (b t h i) -> p t b h j i", t=PACK, h=2, i=4)[:, t],
+            )
+
+        def quantize(grouped, name):
+            width = grouped.shape[1]
+            codes = keep.tile([P, width], U32, name=name + "_codes", align_bytes=64)
+            scale = keep.tile([P, width], U8, name=name + "_scale", align_bytes=64)
+            nc.vector.quantize_mx(
+                out=codes[:].bitcast(FP8X4), scales=scale[:], in_=grouped.rearrange("p c j -> p (c j)")
+            )
+            return codes, scale
+
+        def project(weight, name):
+            codes, scale = weight
+            rows = keep.tile([P, S], F32, name=name)
+            for h in range(S // BANK):
+                cols = slice(h * BANK, (h + 1) * BANK)
+                bank = psum.tile([P, BANK], F32, name="bank")
+                nc.tensor.matmul_mx(
+                    out=bank[:],
+                    lhsT=codes[:].bitcast(FP8X4),
+                    lhsT_scale=scale[:],
+                    rhs=x_codes[:, cols].bitcast(FP8X4),
+                    rhs_scale=x_scale[:, cols],
+                    start=True,
+                    stop=True,
+                )
+                nc.scalar.copy(rows[:, cols], bank[:])
+            return rows
+
+        def w2_tile(t):
+            grouped = keep.tile([P, P, PACK], BF16, name="w2_grouped%d" % t, align_bytes=64)
+            interleave(nc.scalar.copy, grouped[:], w2_raw, t)
+            return quantize(grouped[:], "w2_%d" % t)
+
+        w3_grouped = keep.tile([P, N, PACK], BF16, name="w3_grouped", align_bytes=64)
+
+        def w3_interleave(m):
+            cols = slice(m * P, (m + 1) * P)
+            nc.scalar.copy(
+                w3_grouped[:, cols, :].rearrange("p (c i) t -> p c t i", i=4),
+                w3_raw[:, :, cols].rearrange("p t (c i) -> p c t i", i=4),
+            )
+
+        def score_difference(s_rows, t):
+            s_right = keep.tile([P, V], F32, name="s_right%d" % t)
+            diff = keep.tile([P, V], F32, name="diff%d" % t)
+            nc.vector.tensor_copy(s_right[:], s_rows[:].indirect(right_sb[:]))
+            nc.vector.tensor_tensor(diff[:], s_rows[:].indirect(left_sb[:]), s_right[:], ALU.subtract)
+            return diff
+
+        def gates(diff, t):
+            q_left = keep.tile([P, V], F32, name="q_left%d" % t)
+            q_right = keep.tile([P, V], F32, name="q_right%d" % t)
+            nc.scalar.activation(q_left[:], diff[:], SIGMOID)
+            nc.scalar.activation(q_right[:], diff[:], SIGMOID, scale=-1.0)
+            return q_left, q_right
+
+        part_left = keep.tile([P, PACK, V], F32, name="part_left")
+        part_right = keep.tile([P, PACK, V], F32, name="part_right")
+
+        def weigh(part, val_rows, offsets, gate, t, lo, hi):
+            nc.vector.tensor_tensor(
+                part[:, t, lo:hi],
+                val_rows[:].indirect(offsets[:, lo // 16 : hi // 16]),
+                gate[:, lo:hi],
+                ALU.mult,
+            )
+
+        first = keep.tile([P, P, PACK], BF16, name="w1_first", tag="w1_grouped", align_bytes=64)
+        interleave(nc.scalar.copy, first[:], w1_raw, 0)
+        w1_q = [quantize(first[:], "w1_0")]
+        s_rows = [project(w1_q[0], "s0")]
+        rest = keep.tile([P, PACK - 1, P, PACK], BF16, name="w1_rest", tag="w1_grouped", align_bytes=64)
+        for t in range(1, PACK):
+            interleave(nc.vector.tensor_copy, rest[:, t - 1], w1_raw, t)
+        for t in range(1, PACK):
+            w1_q.append(quantize(rest[:, t - 1], "w1_%d" % t))
+
+        diffs = [score_difference(s_rows[0], 0)]
+        w2_q = [w2_tile(0)]
+        s_rows.append(project(w1_q[1], "s1"))
+        diffs.append(score_difference(s_rows[1], 1))
+        for t in range(PACK - 1):
+            w2_q.append(w2_tile(t + 1))
+            q_left, q_right = gates(diffs[t], t)
+            val_rows = project(w2_q[t], "val%d" % t)
+            weigh(part_left, val_rows, left_sb, q_left, t, 0, V)
+            weigh(part_right, val_rows, right_sb, q_right, t, 0, V)
+            if t + 2 < PACK:
+                s_rows.append(project(w1_q[t + 2], "s%d" % (t + 2)))
+                diffs.append(score_difference(s_rows[t + 2], t + 2))
+            w3_interleave(t)
+        t = PACK - 1
+        q_left, q_right = gates(diffs[t], t)
+        val_rows = project(w2_q[t], "val%d" % t)
+        w3_interleave(t)
+        w3_codes, w3_scale = quantize(w3_grouped[:], "w3")
+
+        out_rows = out.rearrange("(a p) v -> p a v", p=P)
+        for lo, hi in PIECES:
+            width = hi - lo
+            weigh(part_left, val_rows, left_sb, q_left, t, lo, hi)
+            weigh(part_right, val_rows, right_sb, q_right, t, lo, hi)
+            z = keep.tile([P, width, PACK], BF16, name="z%d" % lo, align_bytes=64)
+            nc.vector.tensor_tensor(
+                z[:].rearrange("p (c i) t -> p c t i", i=4),
+                part_left[:, :, lo:hi].rearrange("p t (c i) -> p c t i", i=4),
+                part_right[:, :, lo:hi].rearrange("p t (c i) -> p c t i", i=4),
+                ALU.add,
+            )
+            z_codes, z_scale = quantize(z[:], "z%d" % lo)
+            for pair in range(2):
+                bank = psum.tile([P, 2, width], F32, name="bank")
+                for a in range(2):
+                    cols = slice((2 * pair + a) * P, (2 * pair + a + 1) * P)
+                    nc.tensor.matmul_mx(
+                        out=bank[:, a, :],
+                        lhsT=w3_codes[:, cols].bitcast(FP8X4),
+                        lhsT_scale=w3_scale[:, cols],
+                        rhs=z_codes[:].bitcast(FP8X4),
+                        rhs_scale=z_scale[:],
+                        start=True,
+                        stop=True,
+                    )
+                result = keep.tile([P, 2, width], F32, name="result%d_%d" % (lo, pair))
+                if hi == V and pair == 1:
+                    nc.vector.tensor_copy(result[:], bank[:])
+                else:
+                    nc.scalar.copy(result[:], bank[:])
+                nc.sync.dma_start(out_rows[:, 2 * pair : 2 * pair + 2, lo:hi], result[:])

@@ -18,6 +18,7 @@ SIGMOID = mybir.ActivationFunctionType.Sigmoid
 P = 128
 PACK = 4
 BANK = 512
+HEAD = 768
 PIECES = ((0, 256), (256, 384), (384, 512))
 
 
@@ -34,46 +35,42 @@ def tile_picked_tourney_none_p_kernel(
         left_sb = lists.tile([P, V // 16], U16, name="left_sb")
         right_sb = lists.tile([P, V // 16], U16, name="right_sb")
 
-        shared = ctx.enter_context(tc.tile_pool(name="shared", bufs=1))
-        scale_table = shared.tile([P, T], U8, name="scale_table", offset=7168)
+        scale_table = keep.tile([P, T], U8, name="scale_table")
         word_table = keep.tile([P, T], I32, name="word_table", tag="words_then_w3")
-        warm = keep.tile([P, 2], F32, name="warm", tag="warm_then_w1")
+        w1_parts = ((0, 3 * H // 4), (3 * H // 4, H))
+        w1_raw = [keep.tile([P, PACK, hi - lo], F32, name="w1_raw%d" % lo) for lo, hi in w1_parts]
 
-        nc.vector.memset(scale_table[:].bitcast(I32), 0)
-        nc.gpsimd.memset(warm[:, 0:1], 0.0)
+        nc.vector.memset(scale_table[:, : 3 * T // 4].bitcast(I32), 0)
+        nc.gpsimd.memset(scale_table[:, 3 * T // 4 :].bitcast(I32), 0)
         nc.sync.dma_start(offs_sb[:], offs)
-        nc.scalar.dma_start(word_table[:], x_words[0].rearrange("p n r -> p (n r)").bitcast(I32))
+        words = x_words[0].rearrange("p n r -> p (n r)").bitcast(I32)
+        nc.sync.dma_start(word_table[:, : T // 4], words[:, : T // 4])
+        nc.sync.dma_start(right_sb[:], right)
         for q in range(4):
-            nc.sync.dma_start(
+            queue = nc.scalar if q % 2 else nc.sync
+            queue.dma_start(
                 scale_table[32 * q : 32 * q + 4, :].bitcast(I32),
                 x_scales[0, 4 * q : 4 * q + 4, :].bitcast(I32),
             )
-        nc.sync.dma_start(right_sb[:], right)
+        nc.sync.dma_start(word_table[:, T // 4 :], words[:, T // 4 :])
+        for raw, (lo, hi) in zip(w1_raw, w1_parts):
+            nc.sync.dma_start(raw[:], w1[:, lo:hi].rearrange("(p j) c -> p j c", j=PACK))
         nc.sync.dma_start(left_sb[:], left)
-        nc.scalar.activation(warm[:, 1:2], warm[:, 0:1], SIGMOID)
-        w1_raw = keep.tile([P, PACK, H], F32, name="w1_raw", tag="warm_then_w1")
-        nc.sync.dma_start(w1_raw[:], w1.rearrange("(p j) c -> p j c", j=PACK))
+        w2_raw = keep.tile([P, PACK, H], F32, name="w2_raw")
+        nc.sync.dma_start(w2_raw[:], w2.rearrange("(p j) c -> p j c", j=PACK))
 
         x_scale = keep.tile([P, S], U8, name="x_scale", align_bytes=64)
         nc.vector.tensor_copy(x_scale[:], scale_table[:].indirect(offs_sb[:]))
-        w2_raw = shared.tile([P, PACK, H], F32, name="w2_raw", offset=0)
-        nc.sync.dma_start(w2_raw[:], w2.rearrange("(p j) c -> p j c", j=PACK))
 
-        x_codes = shared.tile([P, S], U32, name="x_codes", offset=8192, align_bytes=64)
-        for h in range(S // BANK):
-            nc.vector.tensor_copy(
-                x_codes[:, h * BANK : (h + 1) * BANK],
-                word_table[:].bitcast(U32).indirect(offs_sb[:, h * BANK // 16 : (h + 1) * BANK // 16]),
-            )
-        w3_raw = keep.tile([P, PACK, N], F32, name="w3_raw", tag="words_then_w3")
-        w3_rows = w3.rearrange("(b t r) n -> t b r n", t=PACK, r=8)
-        for t in range(PACK):
-            nc.sync.dma_start(w3_raw[:, t, :], w3_rows[t])
+        staged = ctx.enter_context(tc.tile_pool(name="staged", bufs=1))
+        word_window = word_table[:].bitcast(U32)
+        x_head = keep.tile([P, HEAD], U32, name="x_head", align_bytes=64)
+        nc.vector.tensor_copy(x_head[:], word_window.indirect(offs_sb[:, : HEAD // 16]))
 
         def interleave(copy, grouped, raw, t):
             copy(
-                grouped.rearrange("p (b h i) j -> p b h j i", h=2, i=4),
-                raw[:].rearrange("p j (b t h i) -> p t b h j i", t=PACK, h=2, i=4)[:, t],
+                grouped.rearrange("p (b h i) j -> p b h j i", h=4, i=2),
+                raw[:].rearrange("p j (b t h i) -> p t b h j i", t=PACK, h=4, i=2)[:, t],
             )
 
         def quantize(grouped, name):
@@ -83,24 +80,42 @@ def tile_picked_tourney_none_p_kernel(
             nc.vector.quantize_mx(
                 out=codes[:].bitcast(FP8X4), scales=scale[:], in_=grouped.rearrange("p c j -> p (c j)")
             )
-            return codes, scale
+            return codes[:], scale[:]
 
-        def project(weight, name):
+        first = staged.tile([P, P, PACK], BF16, name="w1_first", offset=1536, align_bytes=64)
+        second = keep.tile([P, P, PACK], BF16, name="w1_second", align_bytes=64)
+        for t, grouped in enumerate((first, second)):
+            for raw, (lo, hi) in zip(w1_raw, w1_parts):
+                interleave(nc.scalar.copy, grouped[:, lo // PACK : hi // PACK], raw, t)
+        w1_q = [quantize(first[:], "w1_0")]
+        x_tail = staged.tile([P, S - HEAD], U32, name="x_tail", offset=2048, align_bytes=64)
+        nc.vector.tensor_copy(x_tail[:], word_window.indirect(offs_sb[:, HEAD // 16 :]))
+
+        w3_raw = keep.tile([P, PACK, N], F32, name="w3_raw", tag="words_then_w3")
+        w3_rows = w3.rearrange("(b t r) n -> t b r n", t=PACK, r=8)
+        for t in range(PACK):
+            nc.sync.dma_start(w3_raw[:, t, :], w3_rows[t])
+
+        def x_codes(lo, hi):
+            return x_head[:, lo:hi] if hi <= HEAD else x_tail[:, lo - HEAD : hi - HEAD]
+
+        def project(weight, name, width=BANK):
             codes, scale = weight
             rows = keep.tile([P, S], F32, name=name)
-            for h in range(S // BANK):
-                cols = slice(h * BANK, (h + 1) * BANK)
-                bank = psum.tile([P, BANK], F32, name="bank")
-                nc.tensor.matmul_mx(
-                    out=bank[:],
-                    lhsT=codes[:].bitcast(FP8X4),
-                    lhsT_scale=scale[:],
-                    rhs=x_codes[:, cols].bitcast(FP8X4),
-                    rhs_scale=x_scale[:, cols],
-                    start=True,
-                    stop=True,
-                )
-                nc.scalar.copy(rows[:, cols], bank[:])
+            for lo in range(0, S, width):
+                bank = psum.tile([P, width], F32, name="bank")
+                cuts = sorted({lo, lo + width} | ({HEAD} if lo < HEAD < lo + width else set()))
+                for a, b in zip(cuts, cuts[1:]):
+                    nc.tensor.matmul_mx(
+                        out=bank[:, a - lo : b - lo],
+                        lhsT=codes.bitcast(FP8X4),
+                        lhsT_scale=scale,
+                        rhs=x_codes(a, b).bitcast(FP8X4),
+                        rhs_scale=x_scale[:, a:b],
+                        start=True,
+                        stop=True,
+                    )
+                nc.scalar.copy(rows[:, lo : lo + width], bank[:])
             return rows
 
         def w2_tile(t):
@@ -113,23 +128,31 @@ def tile_picked_tourney_none_p_kernel(
         def w3_interleave(m):
             cols = slice(m * P, (m + 1) * P)
             nc.scalar.copy(
-                w3_grouped[:, cols, :].rearrange("p (c i) t -> p c t i", i=4),
-                w3_raw[:, :, cols].rearrange("p t (c i) -> p c t i", i=4),
+                w3_grouped[:, cols, :].rearrange("p (c i) t -> p c t i", i=2),
+                w3_raw[:, :, cols].rearrange("p t (c i) -> p c t i", i=2),
             )
 
         def score_difference(s_rows, t):
             s_right = keep.tile([P, V], F32, name="s_right%d" % t)
             diff = keep.tile([P, V], F32, name="diff%d" % t)
-            nc.vector.tensor_copy(s_right[:], s_rows[:].indirect(right_sb[:]))
-            nc.vector.tensor_tensor(diff[:], s_rows[:].indirect(left_sb[:]), s_right[:], ALU.subtract)
+            halves = ((0, V // 2), (V // 2, V))
+            for lo, hi in halves:
+                nc.vector.tensor_copy(s_right[:, lo:hi], s_rows[:].indirect(right_sb[:, lo // 16 : hi // 16]))
+            for lo, hi in halves:
+                nc.vector.tensor_tensor(
+                    diff[:, lo:hi],
+                    s_rows[:].indirect(left_sb[:, lo // 16 : hi // 16]),
+                    s_right[:, lo:hi],
+                    ALU.subtract,
+                )
             return diff
 
-        def gates(diff, t):
-            q_left = keep.tile([P, V], F32, name="q_left%d" % t)
-            q_right = keep.tile([P, V], F32, name="q_right%d" % t)
-            nc.scalar.activation(q_left[:], diff[:], SIGMOID)
-            nc.scalar.activation(q_right[:], diff[:], SIGMOID, scale=-1.0)
-            return q_left, q_right
+        q_left = [keep.tile([P, V], F32, name="q_left%d" % t) for t in range(PACK)]
+        q_right = [keep.tile([P, V], F32, name="q_right%d" % t) for t in range(PACK)]
+
+        def gates(diff, t, lo, hi):
+            nc.scalar.activation(q_left[t][:, lo:hi], diff[:, lo:hi], SIGMOID)
+            nc.scalar.activation(q_right[t][:, lo:hi], diff[:, lo:hi], SIGMOID, scale=-1.0)
 
         part_left = keep.tile([P, PACK, V], F32, name="part_left")
         part_right = keep.tile([P, PACK, V], F32, name="part_right")
@@ -138,52 +161,64 @@ def tile_picked_tourney_none_p_kernel(
             nc.vector.tensor_tensor(
                 part[:, t, lo:hi],
                 val_rows[:].indirect(offsets[:, lo // 16 : hi // 16]),
-                gate[:, lo:hi],
+                gate[t][:, lo:hi],
                 ALU.mult,
             )
 
-        first = keep.tile([P, P, PACK], BF16, name="w1_first", tag="w1_grouped", align_bytes=64)
-        interleave(nc.scalar.copy, first[:], w1_raw, 0)
-        w1_q = [quantize(first[:], "w1_0")]
-        s_rows = [project(w1_q[0], "s0")]
-        rest = keep.tile([P, PACK - 1, P, PACK], BF16, name="w1_rest", tag="w1_grouped", align_bytes=64)
-        for t in range(1, PACK):
-            interleave(nc.vector.tensor_copy, rest[:, t - 1], w1_raw, t)
-        for t in range(1, PACK):
-            w1_q.append(quantize(rest[:, t - 1], "w1_%d" % t))
+        s_rows = [project(w1_q[0], "s0", BANK // 2)]
+        rest = staged.tile([P, 2, P, PACK], BF16, name="w1_rest", offset=0, align_bytes=64)
+        for raw, (lo, hi) in zip(w1_raw, w1_parts):
+            nc.vector.tensor_copy(
+                rest[:, :, lo // PACK : hi // PACK].rearrange("p t (b r) j -> p b t r j", r=8),
+                raw[:].rearrange("p j (b t r) -> p b t r j", t=PACK, r=8)[:, :, 2:],
+            )
+        w1_q.append(quantize(second[:], "w1_1"))
+        codes, scale = quantize(rest[:].rearrange("p t c j -> p (t c) j"), "w1_23")
+        w1_q.extend((codes[:, u * P : (u + 1) * P], scale[:, u * P : (u + 1) * P]) for u in range(2))
 
         diffs = [score_difference(s_rows[0], 0)]
-        w2_q = [w2_tile(0)]
         s_rows.append(project(w1_q[1], "s1"))
+        w2_q = [w2_tile(0)]
         diffs.append(score_difference(s_rows[1], 1))
-        for t in range(PACK - 1):
-            w2_q.append(w2_tile(t + 1))
-            q_left, q_right = gates(diffs[t], t)
-            val_rows = project(w2_q[t], "val%d" % t)
+        s_rows.append(project(w1_q[2], "s2"))
+        diffs.append(score_difference(s_rows[2], 2))
+        gates(diffs[0], 0, 0, V)
+        w2_q.append(w2_tile(1))
+        w2_q.append(w2_tile(2))
+
+        def weigh_all(val_rows, t):
             weigh(part_left, val_rows, left_sb, q_left, t, 0, V)
             weigh(part_right, val_rows, right_sb, q_right, t, 0, V)
-            if t + 2 < PACK:
-                s_rows.append(project(w1_q[t + 2], "s%d" % (t + 2)))
-                diffs.append(score_difference(s_rows[t + 2], t + 2))
-            w3_interleave(t)
-        t = PACK - 1
-        q_left, q_right = gates(diffs[t], t)
-        val_rows = project(w2_q[t], "val%d" % t)
-        w3_interleave(t)
+
+        weigh_all(project(w2_q[0], "val0"), 0)
+        s_rows.append(project(w1_q[3], "s3"))
+        diffs.append(score_difference(s_rows[3], 3))
+        gates(diffs[1], 1, 0, V)
+        weigh_all(project(w2_q[1], "val1"), 1)
+        w2_q.append(w2_tile(3))
+        w3_interleave(0)
+        gates(diffs[2], 2, 0, V)
+        weigh_all(project(w2_q[2], "val2"), 2)
+        gates(diffs[3], 3, 0, V)
+        val_rows = project(w2_q[3], "val3")
+        for m in range(1, PACK):
+            w3_interleave(m)
         w3_codes, w3_scale = quantize(w3_grouped[:], "w3")
 
         out_rows = out.rearrange("(a p) v -> p a v", p=P)
-        for lo, hi in PIECES:
-            width = hi - lo
-            weigh(part_left, val_rows, left_sb, q_left, t, lo, hi)
-            weigh(part_right, val_rows, right_sb, q_right, t, lo, hi)
-            z = keep.tile([P, width, PACK], BF16, name="z%d" % lo, align_bytes=64)
+
+        def blend(part_left, part_right, lo, hi):
+            z = keep.tile([P, hi - lo, PACK], BF16, name="z%d" % hi, align_bytes=64)
             nc.vector.tensor_tensor(
-                z[:].rearrange("p (c i) t -> p c t i", i=4),
-                part_left[:, :, lo:hi].rearrange("p t (c i) -> p c t i", i=4),
-                part_right[:, :, lo:hi].rearrange("p t (c i) -> p c t i", i=4),
+                z[:].rearrange("p (c i) t -> p c t i", i=2),
+                part_left[:, :, lo:hi].rearrange("p t (c i) -> p c t i", i=2),
+                part_right[:, :, lo:hi].rearrange("p t (c i) -> p c t i", i=2),
                 ALU.add,
             )
+            return z
+
+        def finish(z, lo, hi):
+            width = hi - lo
             z_codes, z_scale = quantize(z[:], "z%d" % lo)
             for pair in range(2):
                 bank = psum.tile([P, 2, width], F32, name="bank")
@@ -193,14 +228,31 @@ def tile_picked_tourney_none_p_kernel(
                         out=bank[:, a, :],
                         lhsT=w3_codes[:, cols].bitcast(FP8X4),
                         lhsT_scale=w3_scale[:, cols],
-                        rhs=z_codes[:].bitcast(FP8X4),
-                        rhs_scale=z_scale[:],
+                        rhs=z_codes.bitcast(FP8X4),
+                        rhs_scale=z_scale,
                         start=True,
                         stop=True,
                     )
                 result = keep.tile([P, 2, width], F32, name="result%d_%d" % (lo, pair))
+                rows = out_rows[:, 2 * pair : 2 * pair + 2, lo:hi]
                 if hi == V and pair == 1:
                     nc.vector.tensor_copy(result[:], bank[:])
+                    nc.sync.dma_start(rows, result[:])
+                elif hi == V:
+                    nc.scalar.copy(result[:], bank[:])
+                    nc.scalar.dma_start(rows, result[:])
                 else:
                     nc.scalar.copy(result[:], bank[:])
-                nc.sync.dma_start(out_rows[:, 2 * pair : 2 * pair + 2, lo:hi], result[:])
+                    nc.sync.dma_start(rows, result[:])
+
+        t = PACK - 1
+        before = None
+        for lo, hi in PIECES:
+            weigh(part_left, val_rows, left_sb, q_left, t, lo, hi)
+            if before is not None:
+                z = blend(part_left, part_right, *before)
+            weigh(part_right, val_rows, right_sb, q_right, t, lo, hi)
+            if before is not None:
+                finish(z, *before)
+            before = (lo, hi)
+        finish(blend(part_left, part_right, *before), *before)

@@ -42,6 +42,8 @@ def tile_picked_tourney_none_p_kernel(
 
         nc.vector.memset(scale_table[:, : 3 * T // 4].bitcast(I32), 0)
         nc.gpsimd.memset(scale_table[:, 3 * T // 4 :].bitcast(I32), 0)
+        warm = keep.tile([P, 2], F32, name="warm")
+        nc.vector.memset(warm[:, 0:1], 0.0)
         nc.sync.dma_start(offs_sb[:], offs)
         words = x_words[0].rearrange("p n r -> p (n r)").bitcast(I32)
         nc.sync.dma_start(word_table[:, : T // 4], words[:, : T // 4])
@@ -53,6 +55,7 @@ def tile_picked_tourney_none_p_kernel(
                 x_scales[0, 4 * q : 4 * q + 4, :].bitcast(I32),
             )
         nc.sync.dma_start(word_table[:, T // 4 :], words[:, T // 4 :])
+        nc.scalar.activation(warm[:, 1:2], warm[:, 0:1], SIGMOID)
         for raw, (lo, hi) in zip(w1_raw, w1_parts):
             nc.sync.dma_start(raw[:], w1[:, lo:hi].rearrange("(p j) c -> p j c", j=PACK))
         nc.sync.dma_start(left_sb[:], left)
@@ -184,7 +187,6 @@ def tile_picked_tourney_none_p_kernel(
         diffs.append(score_difference(s_rows[2], 2))
         gates(diffs[0], 0, 0, V)
         w2_q.append(w2_tile(1))
-        w2_q.append(w2_tile(2))
 
         def weigh_all(val_rows, t):
             weigh(part_left, val_rows, left_sb, q_left, t, 0, V)
@@ -193,6 +195,7 @@ def tile_picked_tourney_none_p_kernel(
         weigh_all(project(w2_q[0], "val0"), 0)
         s_rows.append(project(w1_q[3], "s3"))
         diffs.append(score_difference(s_rows[3], 3))
+        w2_q.append(w2_tile(2))
         gates(diffs[1], 1, 0, V)
         weigh_all(project(w2_q[1], "val1"), 1)
         w2_q.append(w2_tile(3))

@@ -49,8 +49,7 @@ def tile_picked_tourney_none_p_kernel(
         nc.sync.dma_start(word_table[:, : T // 4], words[:, : T // 4])
         nc.sync.dma_start(right_sb[:], right)
         for q in range(4):
-            queue = nc.scalar if q % 2 else nc.sync
-            queue.dma_start(
+            nc.sync.dma_start(
                 scale_table[32 * q : 32 * q + 4, :].bitcast(I32),
                 x_scales[0, 4 * q : 4 * q + 4, :].bitcast(I32),
             )

@@ -48,11 +48,8 @@ def tile_picked_tourney_none_p_kernel(
         words = x_words[0].rearrange("p n r -> p (n r)").bitcast(I32)
         nc.sync.dma_start(word_table[:, : T // 4], words[:, : T // 4])
         nc.sync.dma_start(right_sb[:], right)
-        for q in range(4):
-            nc.sync.dma_start(
-                scale_table[32 * q : 32 * q + 4, :].bitcast(I32),
-                x_scales[0, 4 * q : 4 * q + 4, :].bitcast(I32),
-            )
+        for r in range(4):
+            nc.sync.dma_start(scale_table[r:P:32, :].bitcast(I32), x_scales[0, r:16:4, :].bitcast(I32))
         nc.sync.dma_start(word_table[:, T // 4 :], words[:, T // 4 :])
         nc.scalar.activation(warm[:, 1:2], warm[:, 0:1], SIGMOID)
         for raw, (lo, hi) in zip(w1_raw, w1_parts):

@@ -219,10 +219,11 @@ def tile_picked_tourney_none_p_kernel(
         def finish(z, lo, hi):
             width = hi - lo
             z_codes, z_scale = quantize(z[:], "z%d" % lo)
-            for pair in range(2):
-                bank = psum.tile([P, 2, width], F32, name="bank")
-                for a in range(2):
-                    cols = slice((2 * pair + a) * P, (2 * pair + a + 1) * P)
+            blocks = 1 if lo == 0 else 2
+            for first in range(0, PACK, blocks):
+                bank = psum.tile([P, blocks, width], F32, name="bank")
+                for a in range(blocks):
+                    cols = slice((first + a) * P, (first + a + 1) * P)
                     nc.tensor.matmul_mx(
                         out=bank[:, a, :],
                         lhsT=w3_codes[:, cols].bitcast(FP8X4),
@@ -232,9 +233,9 @@ def tile_picked_tourney_none_p_kernel(
                         start=True,
                         stop=True,
                     )
-                result = keep.tile([P, 2, width], F32, name="result%d_%d" % (lo, pair))
-                rows = out_rows[:, 2 * pair : 2 * pair + 2, lo:hi]
-                if hi == V and pair == 1:
+                result = keep.tile([P, blocks, width], F32, name="result%d_%d" % (lo, first))
+                rows = out_rows[:, first : first + blocks, lo:hi]
+                if hi == V and first > 0:
                     nc.vector.tensor_copy(result[:], bank[:])
                     nc.sync.dma_start(rows, result[:])
                 elif hi == V:

@@ -42,8 +42,6 @@ def tile_picked_tourney_none_p_kernel(
 
         nc.vector.memset(scale_table[:, : 3 * T // 4].bitcast(I32), 0)
         nc.gpsimd.memset(scale_table[:, 3 * T // 4 :].bitcast(I32), 0)
-        warm = keep.tile([P, 2], F32, name="warm")
-        nc.vector.memset(warm[:, 0:1], 0.0)
         nc.sync.dma_start(offs_sb[:], offs)
         words = x_words[0].rearrange("p n r -> p (n r)").bitcast(I32)
         nc.sync.dma_start(word_table[:, : T // 4], words[:, : T // 4])
@@ -51,7 +49,6 @@ def tile_picked_tourney_none_p_kernel(
         for r in range(4):
             nc.sync.dma_start(scale_table[r:P:32, :].bitcast(I32), x_scales[0, r:16:4, :].bitcast(I32))
         nc.sync.dma_start(word_table[:, T // 4 :], words[:, T // 4 :])
-        nc.scalar.activation(warm[:, 1:2], warm[:, 0:1], SIGMOID)
         for raw, (lo, hi) in zip(w1_raw, w1_parts):
             nc.sync.dma_start(raw[:], w1[:, lo:hi].rearrange("(p j) c -> p j c", j=PACK))
         nc.sync.dma_start(left_sb[:], left)

@@ -18,7 +18,7 @@ SIGMOID = mybir.ActivationFunctionType.Sigmoid
 P = 128
 PACK = 4
 BANK = 512
-HEAD = 768
+X_CUTS = (0, 640, 1024)
 PIECES = ((0, 256), (256, 384), (384, 512))
 
 
@@ -37,20 +37,24 @@ def tile_picked_tourney_none_p_kernel(
 
         scale_table = keep.tile([P, T], U8, name="scale_table")
         word_table = keep.tile([P, T], I32, name="word_table", tag="words_then_w3")
-        w1_parts = ((0, 3 * H // 4), (3 * H // 4, H))
+        w1_parts = ((0, 192), (192, H))
         w1_raw = [keep.tile([P, PACK, hi - lo], F32, name="w1_raw%d" % lo) for lo, hi in w1_parts]
 
         nc.vector.memset(scale_table[:, : 3 * T // 4].bitcast(I32), 0)
         nc.gpsimd.memset(scale_table[:, 3 * T // 4 :].bitcast(I32), 0)
         nc.sync.dma_start(offs_sb[:], offs)
         words = x_words[0].rearrange("p n r -> p (n r)").bitcast(I32)
-        nc.sync.dma_start(word_table[:, : T // 4], words[:, : T // 4])
+
+        def load_w1(part):
+            lo, hi = w1_parts[part]
+            nc.sync.dma_start(w1_raw[part][:], w1[:, lo:hi].rearrange("(p j) c -> p j c", j=PACK))
+
+        load_w1(0)
         nc.sync.dma_start(right_sb[:], right)
         for r in range(4):
             nc.sync.dma_start(scale_table[r:P:32, :].bitcast(I32), x_scales[0, r:16:4, :].bitcast(I32))
-        nc.sync.dma_start(word_table[:, T // 4 :], words[:, T // 4 :])
-        for raw, (lo, hi) in zip(w1_raw, w1_parts):
-            nc.sync.dma_start(raw[:], w1[:, lo:hi].rearrange("(p j) c -> p j c", j=PACK))
+        nc.sync.dma_start(word_table[:], words)
+        load_w1(1)
         nc.sync.dma_start(left_sb[:], left)
         w2_raw = keep.tile([P, PACK, H], F32, name="w2_raw")
         nc.sync.dma_start(w2_raw[:], w2.rearrange("(p j) c -> p j c", j=PACK))
@@ -60,8 +64,8 @@ def tile_picked_tourney_none_p_kernel(
 
         staged = ctx.enter_context(tc.tile_pool(name="staged", bufs=1))
         word_window = word_table[:].bitcast(U32)
-        x_head = keep.tile([P, HEAD], U32, name="x_head", align_bytes=64)
-        nc.vector.tensor_copy(x_head[:], word_window.indirect(offs_sb[:, : HEAD // 16]))
+        x_head = keep.tile([P, X_CUTS[1]], U32, name="x_head", align_bytes=64)
+        nc.vector.tensor_copy(x_head[:], word_window.indirect(offs_sb[:, : X_CUTS[1] // 16]))
 
         def interleave(copy, grouped, raw, t):
             copy(
@@ -78,14 +82,26 @@ def tile_picked_tourney_none_p_kernel(
             )
             return codes[:], scale[:]
 
-        first = staged.tile([P, P, PACK], BF16, name="w1_first", offset=1536, align_bytes=64)
+        first = staged.tile([P, P, PACK], BF16, name="w1_first", offset=512, align_bytes=64)
         second = keep.tile([P, P, PACK], BF16, name="w1_second", align_bytes=64)
-        for t, grouped in enumerate((first, second)):
-            for raw, (lo, hi) in zip(w1_raw, w1_parts):
-                interleave(nc.scalar.copy, grouped[:, lo // PACK : hi // PACK], raw, t)
+        rest = keep.tile([P, 2, P, PACK], BF16, name="w1_rest", align_bytes=64)
+        w1_grouped = (first[:], second[:], rest[:, 0], rest[:, 1])
+
+        def w1_interleave(part, t):
+            lo, hi = w1_parts[part]
+            interleave(nc.scalar.copy, w1_grouped[t][:, lo // PACK : hi // PACK], w1_raw[part], t)
+
+        for t in range(PACK):
+            w1_interleave(0, t)
+        w1_interleave(1, 0)
         w1_q = [quantize(first[:], "w1_0")]
-        x_tail = staged.tile([P, S - HEAD], U32, name="x_tail", offset=2048, align_bytes=64)
-        nc.vector.tensor_copy(x_tail[:], word_window.indirect(offs_sb[:, HEAD // 16 :]))
+        x_parts = [x_head]
+        for lo, hi in zip(X_CUTS[1:], X_CUTS[2:]):
+            part = staged.tile([P, hi - lo], U32, name="x%d" % lo, offset=0, align_bytes=64)
+            nc.vector.tensor_copy(part[:], word_window.indirect(offs_sb[:, lo // 16 : hi // 16]))
+            x_parts.append(part)
+        for t in range(1, PACK):
+            w1_interleave(1, t)
 
         w3_raw = keep.tile([P, PACK, N], F32, name="w3_raw", tag="words_then_w3")
         w3_rows = w3.rearrange("(b t r) n -> t b r n", t=PACK, r=8)
@@ -93,14 +109,15 @@ def tile_picked_tourney_none_p_kernel(
             nc.sync.dma_start(w3_raw[:, t, :], w3_rows[t])
 
         def x_codes(lo, hi):
-            return x_head[:, lo:hi] if hi <= HEAD else x_tail[:, lo - HEAD : hi - HEAD]
+            part = max(i for i in range(len(x_parts)) if X_CUTS[i] <= lo)
+            return x_parts[part][:, lo - X_CUTS[part] : hi - X_CUTS[part]]
 
-        def project(weight, name, width=BANK):
+        def project(weight, name, banks=(0, BANK, S), last=nc.scalar.copy):
             codes, scale = weight
             rows = keep.tile([P, S], F32, name=name)
-            for lo in range(0, S, width):
-                bank = psum.tile([P, width], F32, name="bank")
-                cuts = sorted({lo, lo + width} | ({HEAD} if lo < HEAD < lo + width else set()))
+            for lo, hi in zip(banks, banks[1:]):
+                bank = psum.tile([P, hi - lo], F32, name="bank")
+                cuts = sorted({lo, hi} | {cut for cut in (BANK, 640, 896) if lo < cut < hi})
                 for a, b in zip(cuts, cuts[1:]):
                     nc.tensor.matmul_mx(
                         out=bank[:, a - lo : b - lo],
@@ -111,7 +128,7 @@ def tile_picked_tourney_none_p_kernel(
                         start=True,
                         stop=True,
                     )
-                nc.scalar.copy(rows[:, lo : lo + width], bank[:])
+                (last if hi == S else nc.scalar.copy)(rows[:, lo:hi], bank[:])
             return rows
 
         def w2_tile(t):
@@ -161,13 +178,7 @@ def tile_picked_tourney_none_p_kernel(
                 ALU.mult,
             )
 
-        s_rows = [project(w1_q[0], "s0", BANK // 2)]
-        rest = staged.tile([P, 2, P, PACK], BF16, name="w1_rest", offset=0, align_bytes=64)
-        for raw, (lo, hi) in zip(w1_raw, w1_parts):
-            nc.vector.tensor_copy(
-                rest[:, :, lo // PACK : hi // PACK].rearrange("p t (b r) j -> p b t r j", r=8),
-                raw[:].rearrange("p j (b t r) -> p b t r j", t=PACK, r=8)[:, :, 2:],
-            )
+        s_rows = [project(w1_q[0], "s0", (0, 256, 640, 896, S), nc.vector.tensor_copy)]
         w1_q.append(quantize(second[:], "w1_1"))
         codes, scale = quantize(rest[:].rearrange("p t c j -> p (t c) j"), "w1_23")
         w1_q.extend((codes[:, u * P : (u + 1) * P], scale[:, u * P : (u + 1) * P]) for u in range(2))

@@ -1,6 +1,7 @@
 from contextlib import ExitStack
 
 import concourse.mybir as mybir
+from concourse.masks import make_identity
 
 K, T, S, V, N, H = 512, 2048, 1024, 512, 512, 512
 FLOPS = 2 * K * H * S * 2 + 2 * H * N * V
@@ -18,8 +19,10 @@ SIGMOID = mybir.ActivationFunctionType.Sigmoid
 P = 128
 PACK = 4
 BANK = 512
-X_CUTS = (0, 640, 1024)
-PIECES = ((0, 256), (256, 384), (384, 512))
+HEAD = 768
+EARLY = 256
+PIECES = ((256, 384), (384, 512))
+W3_CUTS = (0, 192, 384, 512)
 
 
 def tile_picked_tourney_none_p_kernel(
@@ -29,7 +32,8 @@ def tile_picked_tourney_none_p_kernel(
     with ExitStack() as ctx:
         lists = ctx.enter_context(tc.tile_pool(name="lists", bufs=1))
         keep = ctx.enter_context(tc.tile_pool(name="keep", bufs=1))
-        psum = ctx.enter_context(tc.psum_pool(name="psum", bufs=8))
+        psum = ctx.enter_context(tc.psum_pool(name="psum", bufs=6))
+        sums = ctx.enter_context(tc.psum_pool(name="sums", bufs=1))
 
         offs_sb = lists.tile([P, S // 16], U16, name="offs_sb")
         left_sb = lists.tile([P, V // 16], U16, name="left_sb")
@@ -37,24 +41,22 @@ def tile_picked_tourney_none_p_kernel(
 
         scale_table = keep.tile([P, T], U8, name="scale_table")
         word_table = keep.tile([P, T], I32, name="word_table", tag="words_then_w3")
-        w1_parts = ((0, 192), (192, H))
+        w1_parts = ((0, 3 * H // 4), (3 * H // 4, H))
         w1_raw = [keep.tile([P, PACK, hi - lo], F32, name="w1_raw%d" % lo) for lo, hi in w1_parts]
 
         nc.vector.memset(scale_table[:, : 3 * T // 4].bitcast(I32), 0)
         nc.gpsimd.memset(scale_table[:, 3 * T // 4 :].bitcast(I32), 0)
+        identity = keep.tile([P, P], F32, name="identity")
+        make_identity(nc, identity[:])
         nc.sync.dma_start(offs_sb[:], offs)
         words = x_words[0].rearrange("p n r -> p (n r)").bitcast(I32)
-
-        def load_w1(part):
-            lo, hi = w1_parts[part]
-            nc.sync.dma_start(w1_raw[part][:], w1[:, lo:hi].rearrange("(p j) c -> p j c", j=PACK))
-
-        load_w1(0)
+        nc.sync.dma_start(word_table[:, : T // 4], words[:, : T // 4])
         nc.sync.dma_start(right_sb[:], right)
         for r in range(4):
             nc.sync.dma_start(scale_table[r:P:32, :].bitcast(I32), x_scales[0, r:16:4, :].bitcast(I32))
-        nc.sync.dma_start(word_table[:], words)
-        load_w1(1)
+        nc.sync.dma_start(word_table[:, T // 4 :], words[:, T // 4 :])
+        for raw, (lo, hi) in zip(w1_raw, w1_parts):
+            nc.sync.dma_start(raw[:], w1[:, lo:hi].rearrange("(p j) c -> p j c", j=PACK))
         nc.sync.dma_start(left_sb[:], left)
         w2_raw = keep.tile([P, PACK, H], F32, name="w2_raw")
         nc.sync.dma_start(w2_raw[:], w2.rearrange("(p j) c -> p j c", j=PACK))
@@ -64,8 +66,8 @@ def tile_picked_tourney_none_p_kernel(
 
         staged = ctx.enter_context(tc.tile_pool(name="staged", bufs=1))
         word_window = word_table[:].bitcast(U32)
-        x_head = keep.tile([P, X_CUTS[1]], U32, name="x_head", align_bytes=64)
-        nc.vector.tensor_copy(x_head[:], word_window.indirect(offs_sb[:, : X_CUTS[1] // 16]))
+        x_head = keep.tile([P, HEAD], U32, name="x_head", align_bytes=64)
+        nc.vector.tensor_copy(x_head[:], word_window.indirect(offs_sb[:, : HEAD // 16]))
 
         def interleave(copy, grouped, raw, t):
             copy(
@@ -82,26 +84,14 @@ def tile_picked_tourney_none_p_kernel(
             )
             return codes[:], scale[:]
 
-        first = staged.tile([P, P, PACK], BF16, name="w1_first", offset=512, align_bytes=64)
+        first = staged.tile([P, P, PACK], BF16, name="w1_first", offset=1536, align_bytes=64)
         second = keep.tile([P, P, PACK], BF16, name="w1_second", align_bytes=64)
-        rest = keep.tile([P, 2, P, PACK], BF16, name="w1_rest", align_bytes=64)
-        w1_grouped = (first[:], second[:], rest[:, 0], rest[:, 1])
-
-        def w1_interleave(part, t):
-            lo, hi = w1_parts[part]
-            interleave(nc.scalar.copy, w1_grouped[t][:, lo // PACK : hi // PACK], w1_raw[part], t)
-
-        for t in range(PACK):
-            w1_interleave(0, t)
-        w1_interleave(1, 0)
+        for t, grouped in enumerate((first, second)):
+            for raw, (lo, hi) in zip(w1_raw, w1_parts):
+                interleave(nc.scalar.copy, grouped[:, lo // PACK : hi // PACK], raw, t)
         w1_q = [quantize(first[:], "w1_0")]
-        x_parts = [x_head]
-        for lo, hi in zip(X_CUTS[1:], X_CUTS[2:]):
-            part = staged.tile([P, hi - lo], U32, name="x%d" % lo, offset=0, align_bytes=64)
-            nc.vector.tensor_copy(part[:], word_window.indirect(offs_sb[:, lo // 16 : hi // 16]))
-            x_parts.append(part)
-        for t in range(1, PACK):
-            w1_interleave(1, t)
+        x_tail = staged.tile([P, S - HEAD], U32, name="x_tail", offset=2048, align_bytes=64)
+        nc.vector.tensor_copy(x_tail[:], word_window.indirect(offs_sb[:, HEAD // 16 :]))
 
         w3_raw = keep.tile([P, PACK, N], F32, name="w3_raw", tag="words_then_w3")
         w3_rows = w3.rearrange("(b t r) n -> t b r n", t=PACK, r=8)
@@ -109,15 +99,14 @@ def tile_picked_tourney_none_p_kernel(
             nc.sync.dma_start(w3_raw[:, t, :], w3_rows[t])
 
         def x_codes(lo, hi):
-            part = max(i for i in range(len(x_parts)) if X_CUTS[i] <= lo)
-            return x_parts[part][:, lo - X_CUTS[part] : hi - X_CUTS[part]]
+            return x_head[:, lo:hi] if hi <= HEAD else x_tail[:, lo - HEAD : hi - HEAD]
 
-        def project(weight, name, banks=(0, BANK, S), last=nc.scalar.copy):
+        def project(weight, name, width=BANK):
             codes, scale = weight
             rows = keep.tile([P, S], F32, name=name)
-            for lo, hi in zip(banks, banks[1:]):
-                bank = psum.tile([P, hi - lo], F32, name="bank")
-                cuts = sorted({lo, hi} | {cut for cut in (BANK, 640, 896) if lo < cut < hi})
+            for lo in range(0, S, width):
+                bank = psum.tile([P, width], F32, name="bank")
+                cuts = sorted({lo, lo + width} | ({HEAD} if lo < HEAD < lo + width else set()))
                 for a, b in zip(cuts, cuts[1:]):
                     nc.tensor.matmul_mx(
                         out=bank[:, a - lo : b - lo],
@@ -128,105 +117,144 @@ def tile_picked_tourney_none_p_kernel(
                         start=True,
                         stop=True,
                     )
-                (last if hi == S else nc.scalar.copy)(rows[:, lo:hi], bank[:])
+                nc.scalar.copy(rows[:, lo : lo + width], bank[:])
             return rows
 
-        def w2_tile(t):
-            grouped = keep.tile([P, P, PACK], BF16, name="w2_grouped%d" % t, align_bytes=64)
-            interleave(nc.scalar.copy, grouped[:], w2_raw, t)
-            return quantize(grouped[:], "w2_%d" % t)
+        def w2_pair(u):
+            grouped = keep.tile([P, 2, P, PACK], BF16, name="w2_grouped%d" % u, align_bytes=64)
+            for e in range(2):
+                interleave(nc.scalar.copy, grouped[:, e], w2_raw, 2 * u + e)
+            return split(quantize(grouped[:].rearrange("p t c j -> p (t c) j"), "w2_%d" % u))
 
-        w3_grouped = keep.tile([P, N, PACK], BF16, name="w3_grouped", align_bytes=64)
+        def split(weight):
+            codes, scale = weight
+            return [(codes[:, u * P : (u + 1) * P], scale[:, u * P : (u + 1) * P]) for u in range(2)]
 
-        def w3_interleave(m):
-            cols = slice(m * P, (m + 1) * P)
-            nc.scalar.copy(
-                w3_grouped[:, cols, :].rearrange("p (c i) t -> p c t i", i=2),
-                w3_raw[:, :, cols].rearrange("p t (c i) -> p c t i", i=2),
+        w3_grouped = keep.tile([P, N * PACK], BF16, name="w3_grouped", align_bytes=64)
+
+        def w3_interleave(part):
+            lo, hi = W3_CUTS[part], W3_CUTS[part + 1]
+            nc.gpsimd.tensor_scalar(
+                w3_grouped[:, lo * PACK : hi * PACK].rearrange("p (c i t) -> p c t i", i=2, t=PACK),
+                w3_raw[:, :, lo:hi].rearrange("p t (c i) -> p c t i", i=2),
+                1.0,
+                0.0,
+                ALU.mult,
+                ALU.add,
             )
 
         def score_difference(s_rows, t):
-            s_right = keep.tile([P, V], F32, name="s_right%d" % t)
+            low = keep.tile([P, V // 2], F32, name="s_right_low%d" % t)[:]
+            if t in (1, 2):
+                high = w3_grouped[:, W3_CUTS[t - 1] * PACK : W3_CUTS[t - 1] * PACK + V].bitcast(F32)
+            else:
+                high = keep.tile([P, V // 2], F32, name="s_right_high%d" % t)[:]
             diff = keep.tile([P, V], F32, name="diff%d" % t)
-            halves = ((0, V // 2), (V // 2, V))
-            for lo, hi in halves:
-                nc.vector.tensor_copy(s_right[:, lo:hi], s_rows[:].indirect(right_sb[:, lo // 16 : hi // 16]))
-            for lo, hi in halves:
+            halves = ((0, V // 2, low), (V // 2, V, high))
+            for lo, hi, s_right in halves:
+                nc.vector.tensor_copy(s_right, s_rows[:].indirect(right_sb[:, lo // 16 : hi // 16]))
+            for lo, hi, s_right in halves:
                 nc.vector.tensor_tensor(
-                    diff[:, lo:hi],
-                    s_rows[:].indirect(left_sb[:, lo // 16 : hi // 16]),
-                    s_right[:, lo:hi],
-                    ALU.subtract,
+                    diff[:, lo:hi], s_rows[:].indirect(left_sb[:, lo // 16 : hi // 16]), s_right, ALU.subtract
                 )
+            if t in (1, 2):
+                w3_interleave(t - 1)
             return diff
 
         q_left = [keep.tile([P, V], F32, name="q_left%d" % t) for t in range(PACK)]
         q_right = [keep.tile([P, V], F32, name="q_right%d" % t) for t in range(PACK)]
 
-        def gates(diff, t, lo, hi):
-            nc.scalar.activation(q_left[t][:, lo:hi], diff[:, lo:hi], SIGMOID)
-            nc.scalar.activation(q_right[t][:, lo:hi], diff[:, lo:hi], SIGMOID, scale=-1.0)
+        def gates(t, lo, hi):
+            nc.scalar.activation(q_left[t][:, lo:hi], diffs[t][:, lo:hi], SIGMOID)
+            nc.scalar.activation(q_right[t][:, lo:hi], diffs[t][:, lo:hi], SIGMOID, scale=-1.0)
 
-        part_left = keep.tile([P, PACK, V], F32, name="part_left")
-        part_right = keep.tile([P, PACK, V], F32, name="part_right")
-
-        def weigh(part, val_rows, offsets, gate, t, lo, hi):
+        def weigh(part, offsets, gate, t, lo, hi):
             nc.vector.tensor_tensor(
-                part[:, t, lo:hi],
-                val_rows[:].indirect(offsets[:, lo // 16 : hi // 16]),
-                gate[t][:, lo:hi],
-                ALU.mult,
+                part, val_rows[t][:].indirect(offsets[:, lo // 16 : hi // 16]), gate[t][:, lo:hi], ALU.mult
             )
 
-        s_rows = [project(w1_q[0], "s0", (0, 256, 640, 896, S), nc.vector.tensor_copy)]
+        s_rows = [project(w1_q[0], "s0", BANK // 2)]
+        rest = staged.tile([P, 2, P, PACK], BF16, name="w1_rest", offset=0, align_bytes=64)
+        for raw, (lo, hi) in zip(w1_raw, w1_parts):
+            nc.vector.tensor_copy(
+                rest[:, :, lo // PACK : hi // PACK].rearrange("p t (b r) j -> p b t r j", r=8),
+                raw[:].rearrange("p j (b t r) -> p b t r j", t=PACK, r=8)[:, :, 2:],
+            )
         w1_q.append(quantize(second[:], "w1_1"))
-        codes, scale = quantize(rest[:].rearrange("p t c j -> p (t c) j"), "w1_23")
-        w1_q.extend((codes[:, u * P : (u + 1) * P], scale[:, u * P : (u + 1) * P]) for u in range(2))
+        w1_q.extend(split(quantize(rest[:].rearrange("p t c j -> p (t c) j"), "w1_23")))
 
         diffs = [score_difference(s_rows[0], 0)]
         s_rows.append(project(w1_q[1], "s1"))
-        w2_q = [w2_tile(0)]
         diffs.append(score_difference(s_rows[1], 1))
+        w2_q = w2_pair(0)
         s_rows.append(project(w1_q[2], "s2"))
         diffs.append(score_difference(s_rows[2], 2))
-        gates(diffs[0], 0, 0, V)
-        w2_q.append(w2_tile(1))
-
-        def weigh_all(val_rows, t):
-            weigh(part_left, val_rows, left_sb, q_left, t, 0, V)
-            weigh(part_right, val_rows, right_sb, q_right, t, 0, V)
-
-        weigh_all(project(w2_q[0], "val0"), 0)
+        w2_q.extend(w2_pair(1))
         s_rows.append(project(w1_q[3], "s3"))
         diffs.append(score_difference(s_rows[3], 3))
-        w2_q.append(w2_tile(2))
-        gates(diffs[1], 1, 0, V)
-        weigh_all(project(w2_q[1], "val1"), 1)
-        w2_q.append(w2_tile(3))
-        w3_interleave(0)
-        gates(diffs[2], 2, 0, V)
-        weigh_all(project(w2_q[2], "val2"), 2)
-        gates(diffs[3], 3, 0, V)
-        val_rows = project(w2_q[3], "val3")
-        for m in range(1, PACK):
-            w3_interleave(m)
-        w3_codes, w3_scale = quantize(w3_grouped[:], "w3")
+
+        turned = [sums.tile([P, PACK, P], F32, name="turned%d" % block) for block in range(EARLY // P)]
+        val_rows = []
+        for t in range(PACK):
+            gates(t, 0, EARLY)
+            val_rows.append(project(w2_q[t], "val%d" % t))
+        nc.scalar.copy(
+            w3_grouped[:, W3_CUTS[2] * PACK :].rearrange("p (c i t) -> p c t i", i=2, t=PACK),
+            w3_raw[:, :, W3_CUTS[2] :].rearrange("p t (c i) -> p c t i", i=2),
+        )
+        for t in range(PACK):
+            terms = [keep.tile([P, EARLY], F32, name="term%d_%d" % (t, side)) for side in range(2)]
+            weigh(terms[0][:], left_sb, q_left, t, 0, EARLY)
+            weigh(terms[1][:], right_sb, q_right, t, 0, EARLY)
+            for block, bank in enumerate(turned):
+                for side, term in enumerate(terms):
+                    nc.tensor.matmul(
+                        bank[:, t, :],
+                        term[:, block * P : (block + 1) * P],
+                        identity[:],
+                        start=side == 0,
+                        stop=side == 1,
+                        is_transpose=True,
+                    )
+
+        w3_codes, w3_scale = quantize(w3_grouped[:].rearrange("p (c t) -> p c t", t=PACK), "w3")
+        late = V - EARLY
+        parts = keep.tile([P, PACK * 2 * late], F32, name="parts", align_bytes=64)
+        sides = parts[:].rearrange("p (t s v) -> p s t v", s=2, v=late)
+        part_left, part_right = sides[:, 0], sides[:, 1]
+        for t in range(PACK):
+            gates(t, EARLY, V)
+        for t in range(PACK - 1):
+            weigh(part_left[:, t, :], left_sb, q_left, t, EARLY, V)
+            weigh(part_right[:, t, :], right_sb, q_right, t, EARLY, V)
+
+        words_back = psum.tile([P, EARLY // P, 2, P], F32, name="bank")
+        for block, bank in enumerate(turned):
+            rounded = keep.tile([P, 2, P, 2], BF16, name="rounded%d" % block)
+            nc.scalar.copy(rounded[:], bank[:].rearrange("v (u e) p -> v u p e", e=2))
+            pairs = rounded[:].rearrange("v u p e -> v u (p e)").bitcast(F32)
+            for u in range(2):
+                nc.tensor.transpose(words_back[:, block, u, :], pairs[:, u, :], identity[:])
+        z_early = parts[:, (PACK - 1) * 2 * late :]
+        nc.scalar.copy(
+            z_early.rearrange("p (b v u) -> p b v u", v=P, u=2), words_back[:].rearrange("p b u v -> p b v u")
+        )
 
         out_rows = out.rearrange("(a p) v -> p a v", p=P)
 
-        def blend(part_left, part_right, lo, hi):
+        def blend(lo, hi):
             z = keep.tile([P, hi - lo, PACK], BF16, name="z%d" % hi, align_bytes=64)
             nc.vector.tensor_tensor(
                 z[:].rearrange("p (c i) t -> p c t i", i=2),
-                part_left[:, :, lo:hi].rearrange("p t (c i) -> p c t i", i=2),
-                part_right[:, :, lo:hi].rearrange("p t (c i) -> p c t i", i=2),
+                part_left[:, :, lo - EARLY : hi - EARLY].rearrange("p t (c i) -> p c t i", i=2),
+                part_right[:, :, lo - EARLY : hi - EARLY].rearrange("p t (c i) -> p c t i", i=2),
                 ALU.add,
             )
-            return z
+            return z[:]
 
         def finish(z, lo, hi):
             width = hi - lo
-            z_codes, z_scale = quantize(z[:], "z%d" % lo)
+            z_codes, z_scale = quantize(z, "z%d" % lo)
             blocks = 1 if lo == 0 else 2
             for first in range(0, PACK, blocks):
                 bank = psum.tile([P, blocks, width], F32, name="bank")
@@ -253,14 +281,15 @@ def tile_picked_tourney_none_p_kernel(
                     nc.scalar.copy(result[:], bank[:])
                     nc.sync.dma_start(rows, result[:])
 
+        finish(z_early.bitcast(BF16).rearrange("p (v t) -> p v t", t=PACK), 0, EARLY)
         t = PACK - 1
         before = None
         for lo, hi in PIECES:
-            weigh(part_left, val_rows, left_sb, q_left, t, lo, hi)
+            weigh(part_left[:, t, lo - EARLY : hi - EARLY], left_sb, q_left, t, lo, hi)
             if before is not None:
-                z = blend(part_left, part_right, *before)
-            weigh(part_right, val_rows, right_sb, q_right, t, lo, hi)
+                z = blend(*before)
+            weigh(part_right[:, t, lo - EARLY : hi - EARLY], right_sb, q_right, t, lo, hi)
             if before is not None:
                 finish(z, *before)
             before = (lo, hi)
-        finish(blend(part_left, part_right, *before), *before)
+        finish(blend(*before), *before)

@@ -22,7 +22,7 @@ BANK = 512
 HEAD = 768
 EARLY = 256
 PIECES = ((256, 384), (384, 512))
-W3_CUTS = (0, 192, 384, 512)
+W3_CUTS = (0, 128, 256, 512)
 
 
 def tile_picked_tourney_none_p_kernel(
@@ -173,13 +173,12 @@ def tile_picked_tourney_none_p_kernel(
                 part, val_rows[t][:].indirect(offsets[:, lo // 16 : hi // 16]), gate[t][:, lo:hi], ALU.mult
             )
 
-        s_rows = [project(w1_q[0], "s0", BANK // 2)]
         rest = staged.tile([P, 2, P, PACK], BF16, name="w1_rest", offset=0, align_bytes=64)
         for raw, (lo, hi) in zip(w1_raw, w1_parts):
-            nc.vector.tensor_copy(
-                rest[:, :, lo // PACK : hi // PACK].rearrange("p t (b r) j -> p b t r j", r=8),
-                raw[:].rearrange("p j (b t r) -> p b t r j", t=PACK, r=8)[:, :, 2:],
-            )
+            interleave(nc.scalar.copy, rest[:, 0, lo // PACK : hi // PACK], raw, 2)
+        s_rows = [project(w1_q[0], "s0", BANK // 2)]
+        for raw, (lo, hi) in zip(w1_raw, w1_parts):
+            interleave(nc.vector.tensor_copy, rest[:, 1, lo // PACK : hi // PACK], raw, 3)
         w1_q.append(quantize(second[:], "w1_1"))
         w1_q.extend(split(quantize(rest[:].rearrange("p t c j -> p (t c) j"), "w1_23")))
 
@@ -193,7 +192,7 @@ def tile_picked_tourney_none_p_kernel(
         s_rows.append(project(w1_q[3], "s3"))
         diffs.append(score_difference(s_rows[3], 3))
 
-        turned = [sums.tile([P, PACK, P], F32, name="turned%d" % block) for block in range(EARLY // P)]
+        turned = [sums.tile([P, EARLY // P, 2, P], F32, name="turned%d" % u) for u in range(2)]
         val_rows = []
         for t in range(PACK):
             gates(t, 0, EARLY)
@@ -206,10 +205,10 @@ def tile_picked_tourney_none_p_kernel(
             terms = [keep.tile([P, EARLY], F32, name="term%d_%d" % (t, side)) for side in range(2)]
             weigh(terms[0][:], left_sb, q_left, t, 0, EARLY)
             weigh(terms[1][:], right_sb, q_right, t, 0, EARLY)
-            for block, bank in enumerate(turned):
+            for block in range(EARLY // P):
                 for side, term in enumerate(terms):
                     nc.tensor.matmul(
-                        bank[:, t, :],
+                        turned[t // 2][:, block, t % 2, :],
                         term[:, block * P : (block + 1) * P],
                         identity[:],
                         start=side == 0,
@@ -219,23 +218,26 @@ def tile_picked_tourney_none_p_kernel(
 
         w3_codes, w3_scale = quantize(w3_grouped[:].rearrange("p (c t) -> p c t", t=PACK), "w3")
         late = V - EARLY
-        parts = keep.tile([P, PACK * 2 * late], F32, name="parts", align_bytes=64)
-        sides = parts[:].rearrange("p (t s v) -> p s t v", s=2, v=late)
+        parts = keep.tile([P, PACK * 2 * late + P], F32, name="parts", align_bytes=64)
+        sides = parts[:, : PACK * 2 * late].rearrange("p (t s v) -> p s t v", s=2, v=late)
         part_left, part_right = sides[:, 0], sides[:, 1]
-        for t in range(PACK):
+        for t in range(2):
             gates(t, EARLY, V)
+        words_back = psum.tile([P, EARLY // P, 2, P], F32, name="bank")
+        for u, bank in enumerate(turned):
+            rounded = keep.tile([P, EARLY // P, P, 2], BF16, name="rounded%d" % u)
+            nc.scalar.copy(rounded[:], bank[:].rearrange("v b e p -> v b p e"))
+            pairs = rounded[:].rearrange("v b p e -> v b (p e)").bitcast(F32)
+            for block in range(EARLY // P):
+                nc.tensor.transpose(words_back[:, block, u, :], pairs[:, block, :], identity[:])
+        gates(2, EARLY, V)
+        nc.scalar.activation(q_left[3][:, EARLY + P :], diffs[3][:, EARLY + P :], SIGMOID)
+        nc.scalar.activation(q_right[3][:, EARLY:], diffs[3][:, EARLY:], SIGMOID, scale=-1.0)
         for t in range(PACK - 1):
             weigh(part_left[:, t, :], left_sb, q_left, t, EARLY, V)
             weigh(part_right[:, t, :], right_sb, q_right, t, EARLY, V)
 
-        words_back = psum.tile([P, EARLY // P, 2, P], F32, name="bank")
-        for block, bank in enumerate(turned):
-            rounded = keep.tile([P, 2, P, 2], BF16, name="rounded%d" % block)
-            nc.scalar.copy(rounded[:], bank[:].rearrange("v (u e) p -> v u p e", e=2))
-            pairs = rounded[:].rearrange("v u p e -> v u (p e)").bitcast(F32)
-            for u in range(2):
-                nc.tensor.transpose(words_back[:, block, u, :], pairs[:, u, :], identity[:])
-        z_early = parts[:, (PACK - 1) * 2 * late :]
+        z_early = parts[:, (PACK - 1) * 2 * late + P :]
         nc.scalar.copy(
             z_early.rearrange("p (b v u) -> p b v u", v=P, u=2), words_back[:].rearrange("p b u v -> p b v u")
         )
@@ -281,11 +283,18 @@ def tile_picked_tourney_none_p_kernel(
                     nc.scalar.copy(result[:], bank[:])
                     nc.sync.dma_start(rows, result[:])
 
+        held_gate = keep.tile([P, P], F32, name="rounded1")
+        nc.scalar.activation(held_gate[:], diffs[3][:, EARLY : EARLY + P], SIGMOID)
         finish(z_early.bitcast(BF16).rearrange("p (v t) -> p v t", t=PACK), 0, EARLY)
         t = PACK - 1
         before = None
         for lo, hi in PIECES:
-            weigh(part_left[:, t, lo - EARLY : hi - EARLY], left_sb, q_left, t, lo, hi)
+            if before is None:
+                nc.vector.tensor_tensor(
+                    part_left[:, t, :P], val_rows[t][:].indirect(left_sb[:, lo // 16 : hi // 16]), held_gate[:], ALU.mult
+                )
+            else:
+                weigh(part_left[:, t, lo - EARLY : hi - EARLY], left_sb, q_left, t, lo, hi)
             if before is not None:
                 z = blend(*before)
             weigh(part_right[:, t, lo - EARLY : hi - EARLY], right_sb, q_right, t, lo, hi)

@@ -41,13 +41,13 @@ def tile_picked_tourney_none_p_kernel(
 
         scale_table = keep.tile([P, T], U8, name="scale_table")
         word_table = keep.tile([P, T], I32, name="word_table", tag="words_then_w3")
-        w1_parts = ((0, 3 * H // 4), (3 * H // 4, H))
+        w1_parts = ((0, H // 2), (H // 2, H))
         w1_raw = [keep.tile([P, PACK, hi - lo], F32, name="w1_raw%d" % lo) for lo, hi in w1_parts]
 
-        nc.vector.memset(scale_table[:, : 3 * T // 4].bitcast(I32), 0)
-        nc.gpsimd.memset(scale_table[:, 3 * T // 4 :].bitcast(I32), 0)
+        nc.vector.memset(scale_table[:].bitcast(I32), 0)
         identity = keep.tile([P, P], F32, name="identity")
-        make_identity(nc, identity[:])
+        nc.vector.memset(identity[:], 0.0)
+        make_identity(nc, identity[:], nomemset=True)
         nc.sync.dma_start(offs_sb[:], offs)
         words = x_words[0].rearrange("p n r -> p (n r)").bitcast(I32)
         nc.sync.dma_start(word_table[:, : T // 4], words[:, : T // 4])

@@ -20,6 +20,7 @@ P = 128
 PACK = 4
 BANK = 512
 HEAD = 768
+SCALAR_SHARE = 80
 EARLY = 256
 PIECES = ((256, 384), (384, 512))
 W3_CUTS = (0, 128, 256, 512)
@@ -41,8 +42,7 @@ def tile_picked_tourney_none_p_kernel(
 
         scale_table = keep.tile([P, T], U8, name="scale_table")
         word_table = keep.tile([P, T], I32, name="word_table", tag="words_then_w3")
-        w1_parts = ((0, H // 2), (H // 2, H))
-        w1_raw = [keep.tile([P, PACK, hi - lo], F32, name="w1_raw%d" % lo) for lo, hi in w1_parts]
+        w1_raw = keep.tile([P, PACK, H], F32, name="w1_raw")
 
         nc.vector.memset(scale_table[:].bitcast(I32), 0)
         identity = keep.tile([P, P], F32, name="identity")
@@ -55,8 +55,7 @@ def tile_picked_tourney_none_p_kernel(
         for r in range(4):
             nc.sync.dma_start(scale_table[r:P:32, :].bitcast(I32), x_scales[0, r:16:4, :].bitcast(I32))
         nc.sync.dma_start(word_table[:, T // 4 :], words[:, T // 4 :])
-        for raw, (lo, hi) in zip(w1_raw, w1_parts):
-            nc.sync.dma_start(raw[:], w1[:, lo:hi].rearrange("(p j) c -> p j c", j=PACK))
+        nc.sync.dma_start(w1_raw[:], w1.rearrange("(p j) c -> p j c", j=PACK))
         nc.sync.dma_start(left_sb[:], left)
         w2_raw = keep.tile([P, PACK, H], F32, name="w2_raw")
         nc.sync.dma_start(w2_raw[:], w2.rearrange("(p j) c -> p j c", j=PACK))
@@ -72,7 +71,7 @@ def tile_picked_tourney_none_p_kernel(
         def interleave(copy, grouped, raw, t):
             copy(
                 grouped.rearrange("p (b h i) j -> p b h j i", h=4, i=2),
-                raw[:].rearrange("p j (b t h i) -> p t b h j i", t=PACK, h=4, i=2)[:, t],
+                raw.rearrange("p j (b t h i) -> p t b h j i", t=PACK, h=4, i=2)[:, t],
             )
 
         def quantize(grouped, name):
@@ -86,9 +85,16 @@ def tile_picked_tourney_none_p_kernel(
 
         first = staged.tile([P, P, PACK], BF16, name="w1_first", offset=1536, align_bytes=64)
         second = keep.tile([P, P, PACK], BF16, name="w1_second", align_bytes=64)
-        for t, grouped in enumerate((first, second)):
-            for raw, (lo, hi) in zip(w1_raw, w1_parts):
-                interleave(nc.scalar.copy, grouped[:, lo // PACK : hi // PACK], raw, t)
+        interleave(nc.scalar.copy, first[:, :SCALAR_SHARE], w1_raw[:, :, : SCALAR_SHARE * PACK], 0)
+        nc.gpsimd.tensor_scalar(
+            first[:, SCALAR_SHARE:].rearrange("p (b r) j -> p b r j", r=8),
+            w1_raw[:, :, SCALAR_SHARE * PACK :].rearrange("p j (b t r) -> p t b r j", t=PACK, r=8)[:, 0],
+            1.0,
+            0.0,
+            ALU.mult,
+            ALU.add,
+        )
+        interleave(nc.scalar.copy, second[:], w1_raw[:], 1)
         w1_q = [quantize(first[:], "w1_0")]
         x_tail = staged.tile([P, S - HEAD], U32, name="x_tail", offset=2048, align_bytes=64)
         nc.vector.tensor_copy(x_tail[:], word_window.indirect(offs_sb[:, HEAD // 16 :]))
@@ -123,7 +129,7 @@ def tile_picked_tourney_none_p_kernel(
         def w2_pair(u):
             grouped = keep.tile([P, 2, P, PACK], BF16, name="w2_grouped%d" % u, align_bytes=64)
             for e in range(2):
-                interleave(nc.scalar.copy, grouped[:, e], w2_raw, 2 * u + e)
+                interleave(nc.scalar.copy, grouped[:, e], w2_raw[:], 2 * u + e)
             return split(quantize(grouped[:].rearrange("p t c j -> p (t c) j"), "w2_%d" % u))
 
         def split(weight):
@@ -174,11 +180,9 @@ def tile_picked_tourney_none_p_kernel(
             )
 
         rest = staged.tile([P, 2, P, PACK], BF16, name="w1_rest", offset=0, align_bytes=64)
-        for raw, (lo, hi) in zip(w1_raw, w1_parts):
-            interleave(nc.scalar.copy, rest[:, 0, lo // PACK : hi // PACK], raw, 2)
+        interleave(nc.scalar.copy, rest[:, 0], w1_raw[:], 2)
         s_rows = [project(w1_q[0], "s0", BANK // 2)]
-        for raw, (lo, hi) in zip(w1_raw, w1_parts):
-            interleave(nc.vector.tensor_copy, rest[:, 1, lo // PACK : hi // PACK], raw, 3)
+        interleave(nc.vector.tensor_copy, rest[:, 1], w1_raw[:], 3)
         w1_q.append(quantize(second[:], "w1_1"))
         w1_q.extend(split(quantize(rest[:].rearrange("p t c j -> p (t c) j"), "w1_23")))
 

@@ -1,7 +1,6 @@
 from contextlib import ExitStack
 
 import concourse.mybir as mybir
-from concourse.masks import make_identity
 
 K, T, S, V, N, H = 512, 2048, 1024, 512, 512, 512
 FLOPS = 2 * K * H * S * 2 + 2 * H * N * V
@@ -15,6 +14,7 @@ U8 = mybir.dt.uint8
 FP8X4 = mybir.dt.float8_e4m3fn_x4
 ALU = mybir.AluOpType
 SIGMOID = mybir.ActivationFunctionType.Sigmoid
+COPY = mybir.ActivationFunctionType.Copy
 
 P = 128
 PACK = 4
@@ -22,8 +22,7 @@ BANK = 512
 HEAD = 768
 SCALAR_SHARE = 80
 EARLY = 256
-PIECES = ((256, 384), (384, 512))
-W3_CUTS = (0, 128, 256, 512)
+LAST = 384
 
 
 def tile_picked_tourney_none_p_kernel(
@@ -33,8 +32,7 @@ def tile_picked_tourney_none_p_kernel(
     with ExitStack() as ctx:
         lists = ctx.enter_context(tc.tile_pool(name="lists", bufs=1))
         keep = ctx.enter_context(tc.tile_pool(name="keep", bufs=1))
-        psum = ctx.enter_context(tc.psum_pool(name="psum", bufs=6))
-        sums = ctx.enter_context(tc.psum_pool(name="sums", bufs=1))
+        psum = ctx.enter_context(tc.psum_pool(name="psum", bufs=8))
 
         offs_sb = lists.tile([P, S // 16], U16, name="offs_sb")
         left_sb = lists.tile([P, V // 16], U16, name="left_sb")
@@ -45,9 +43,9 @@ def tile_picked_tourney_none_p_kernel(
         w1_raw = keep.tile([P, PACK, H], F32, name="w1_raw")
 
         nc.vector.memset(scale_table[:].bitcast(I32), 0)
-        identity = keep.tile([P, P], F32, name="identity")
-        nc.vector.memset(identity[:], 0.0)
-        make_identity(nc, identity[:], nomemset=True)
+        warm = keep.tile([P, 2], F32, name="warm")
+        nc.gpsimd.memset(warm[:, :1], 0.0)
+        nc.scalar.activation(warm[:, 1:], warm[:, :1], SIGMOID)
         nc.sync.dma_start(offs_sb[:], offs)
         words = x_words[0].rearrange("p n r -> p (n r)").bitcast(I32)
         nc.sync.dma_start(word_table[:, : T // 4], words[:, : T // 4])
@@ -107,9 +105,9 @@ def tile_picked_tourney_none_p_kernel(
         def x_codes(lo, hi):
             return x_head[:, lo:hi] if hi <= HEAD else x_tail[:, lo - HEAD : hi - HEAD]
 
-        def project(weight, name, width=BANK):
+        def multiply(weight, width=BANK):
             codes, scale = weight
-            rows = keep.tile([P, S], F32, name=name)
+            banks = []
             for lo in range(0, S, width):
                 bank = psum.tile([P, width], F32, name="bank")
                 cuts = sorted({lo, lo + width} | ({HEAD} if lo < HEAD < lo + width else set()))
@@ -123,186 +121,181 @@ def tile_picked_tourney_none_p_kernel(
                         start=True,
                         stop=True,
                     )
-                nc.scalar.copy(rows[:, lo : lo + width], bank[:])
-            return rows
+                banks.append(bank)
+            return banks
 
-        def w2_pair(u):
-            grouped = keep.tile([P, 2, P, PACK], BF16, name="w2_grouped%d" % u, align_bytes=64)
-            for e in range(2):
-                interleave(nc.scalar.copy, grouped[:, e], w2_raw[:], 2 * u + e)
-            return split(quantize(grouped[:].rearrange("p t c j -> p (t c) j"), "w2_%d" % u))
+        def project(weight, name, copy, width=BANK):
+            rows = keep.tile([P, S], F32, name=name)
+            for n, bank in enumerate(multiply(weight, width)):
+                copy(rows[:, n * width : (n + 1) * width], bank[:])
+            return rows
 
         def split(weight):
             codes, scale = weight
-            return [(codes[:, u * P : (u + 1) * P], scale[:, u * P : (u + 1) * P]) for u in range(2)]
+            return [(codes[:, u * P : (u + 1) * P], scale[:, u * P : (u + 1) * P]) for u in range(codes.shape[1] // P)]
 
-        w3_grouped = keep.tile([P, N * PACK], BF16, name="w3_grouped", align_bytes=64)
+        def gpsimd_round(dst, src):
+            nc.gpsimd.tensor_scalar(dst, src, 1.0, 0.0, ALU.mult, ALU.add)
 
-        def w3_interleave(part):
-            lo, hi = W3_CUTS[part], W3_CUTS[part + 1]
-            nc.gpsimd.tensor_scalar(
-                w3_grouped[:, lo * PACK : hi * PACK].rearrange("p (c i t) -> p c t i", i=2, t=PACK),
+        def picked(rows, offsets, lo=0, hi=V):
+            return rows[:].indirect(offsets[:, lo // 16 : hi // 16])
+
+        def scalar_gather(dst, src):
+            nc.scalar.activation(dst, src, COPY)
+
+        def w3_views(grouped, lo, hi):
+            return (
+                grouped.rearrange("p (c i) t -> p c t i", i=2),
                 w3_raw[:, :, lo:hi].rearrange("p t (c i) -> p c t i", i=2),
-                1.0,
-                0.0,
-                ALU.mult,
-                ALU.add,
             )
 
-        def score_difference(s_rows, t):
-            low = keep.tile([P, V // 2], F32, name="s_right_low%d" % t)[:]
-            if t in (1, 2):
-                high = w3_grouped[:, W3_CUTS[t - 1] * PACK : W3_CUTS[t - 1] * PACK + V].bitcast(F32)
+        diff = keep.tile([P, PACK, V], F32, name="diff")
+        gate = keep.tile([P, PACK, V], F32, name="gate")
+        counter = keep.tile([P, 2, V], F32, name="counter")
+        spread = keep.tile([P, 2, V], F32, name="spread")
+        base = keep.tile([P, PACK, V], F32, name="base")
+        step = keep.tile([P, PACK, V], F32, name="step")
+
+        def right_scores(rows, t, gather):
+            if t == 1:
+                s_right = shared[:, : 2 * V].bitcast(F32)
             else:
-                high = keep.tile([P, V // 2], F32, name="s_right_high%d" % t)[:]
-            diff = keep.tile([P, V], F32, name="diff%d" % t)
-            halves = ((0, V // 2, low), (V // 2, V, high))
-            for lo, hi, s_right in halves:
-                nc.vector.tensor_copy(s_right, s_rows[:].indirect(right_sb[:, lo // 16 : hi // 16]))
-            for lo, hi, s_right in halves:
-                nc.vector.tensor_tensor(
-                    diff[:, lo:hi], s_rows[:].indirect(left_sb[:, lo // 16 : hi // 16]), s_right, ALU.subtract
-                )
-            if t in (1, 2):
-                w3_interleave(t - 1)
-            return diff
+                s_right = keep.tile([P, V], F32, name="s_right%d" % t)[:]
+            gather(s_right, picked(rows, right_sb))
+            return s_right
 
-        q_left = [keep.tile([P, V], F32, name="q_left%d" % t) for t in range(PACK)]
-        q_right = [keep.tile([P, V], F32, name="q_right%d" % t) for t in range(PACK)]
+        def difference(rows, s_right, t):
+            nc.vector.tensor_tensor(diff[:, t, :], picked(rows, left_sb), s_right, ALU.subtract)
 
-        def gates(t, lo, hi):
-            nc.scalar.activation(q_left[t][:, lo:hi], diffs[t][:, lo:hi], SIGMOID)
-            nc.scalar.activation(q_right[t][:, lo:hi], diffs[t][:, lo:hi], SIGMOID, scale=-1.0)
+        def both_gates(t):
+            nc.scalar.activation(gate[:, t, :], diff[:, t, :], SIGMOID)
+            nc.scalar.activation(counter[:, t, :], diff[:, t, :], SIGMOID, scale=-1.0)
 
-        def weigh(part, offsets, gate, t, lo, hi):
+        def weigh(rows, t):
+            nc.vector.tensor_tensor(step[:, t, :], picked(rows, left_sb), gate[:, t, :], ALU.mult)
+            nc.vector.tensor_tensor(base[:, t, :], picked(rows, right_sb), counter[:, t, :], ALU.mult)
+
+        def right_values(rows, t, lo, hi):
+            scalar_gather(base[:, t, lo:hi], picked(rows, right_sb, lo, hi))
+
+        def value_spread(rows, t, lo, hi):
             nc.vector.tensor_tensor(
-                part, val_rows[t][:].indirect(offsets[:, lo // 16 : hi // 16]), gate[t][:, lo:hi], ALU.mult
+                spread[:, t - 2, lo:hi], picked(rows, left_sb, lo, hi), base[:, t, lo:hi], ALU.subtract
             )
 
-        rest = staged.tile([P, 2, P, PACK], BF16, name="w1_rest", offset=0, align_bytes=64)
-        interleave(nc.scalar.copy, rest[:, 0], w1_raw[:], 2)
-        s_rows = [project(w1_q[0], "s0", BANK // 2)]
-        interleave(nc.vector.tensor_copy, rest[:, 1], w1_raw[:], 3)
-        w1_q.append(quantize(second[:], "w1_1"))
-        w1_q.extend(split(quantize(rest[:].rearrange("p t c j -> p (t c) j"), "w1_23")))
+        def late_gates(lo, hi):
+            nc.scalar.activation(gate[:, 2:, lo:hi], diff[:, 2:, lo:hi], SIGMOID)
 
-        diffs = [score_difference(s_rows[0], 0)]
-        s_rows.append(project(w1_q[1], "s1"))
-        diffs.append(score_difference(s_rows[1], 1))
-        w2_q = w2_pair(0)
-        s_rows.append(project(w1_q[2], "s2"))
-        diffs.append(score_difference(s_rows[2], 2))
-        w2_q.extend(w2_pair(1))
-        s_rows.append(project(w1_q[3], "s3"))
-        diffs.append(score_difference(s_rows[3], 3))
-
-        turned = [sums.tile([P, EARLY // P, 2, P], F32, name="turned%d" % u) for u in range(2)]
-        val_rows = []
-        for t in range(PACK):
-            gates(t, 0, EARLY)
-            val_rows.append(project(w2_q[t], "val%d" % t))
-        nc.scalar.copy(
-            w3_grouped[:, W3_CUTS[2] * PACK :].rearrange("p (c i t) -> p c t i", i=2, t=PACK),
-            w3_raw[:, :, W3_CUTS[2] :].rearrange("p t (c i) -> p c t i", i=2),
-        )
-        for t in range(PACK):
-            terms = [keep.tile([P, EARLY], F32, name="term%d_%d" % (t, side)) for side in range(2)]
-            weigh(terms[0][:], left_sb, q_left, t, 0, EARLY)
-            weigh(terms[1][:], right_sb, q_right, t, 0, EARLY)
-            for block in range(EARLY // P):
-                for side, term in enumerate(terms):
-                    nc.tensor.matmul(
-                        turned[t // 2][:, block, t % 2, :],
-                        term[:, block * P : (block + 1) * P],
-                        identity[:],
-                        start=side == 0,
-                        stop=side == 1,
-                        is_transpose=True,
-                    )
-
-        w3_codes, w3_scale = quantize(w3_grouped[:].rearrange("p (c t) -> p c t", t=PACK), "w3")
-        late = V - EARLY
-        parts = keep.tile([P, PACK * 2 * late + P], F32, name="parts", align_bytes=64)
-        sides = parts[:, : PACK * 2 * late].rearrange("p (t s v) -> p s t v", s=2, v=late)
-        part_left, part_right = sides[:, 0], sides[:, 1]
-        for t in range(2):
-            gates(t, EARLY, V)
-        words_back = psum.tile([P, EARLY // P, 2, P], F32, name="bank")
-        for u, bank in enumerate(turned):
-            rounded = keep.tile([P, EARLY // P, P, 2], BF16, name="rounded%d" % u)
-            nc.scalar.copy(rounded[:], bank[:].rearrange("v b e p -> v b p e"))
-            pairs = rounded[:].rearrange("v b p e -> v b (p e)").bitcast(F32)
-            for block in range(EARLY // P):
-                nc.tensor.transpose(words_back[:, block, u, :], pairs[:, block, :], identity[:])
-        gates(2, EARLY, V)
-        nc.scalar.activation(q_left[3][:, EARLY + P :], diffs[3][:, EARLY + P :], SIGMOID)
-        nc.scalar.activation(q_right[3][:, EARLY:], diffs[3][:, EARLY:], SIGMOID, scale=-1.0)
-        for t in range(PACK - 1):
-            weigh(part_left[:, t, :], left_sb, q_left, t, EARLY, V)
-            weigh(part_right[:, t, :], right_sb, q_right, t, EARLY, V)
-
-        z_early = parts[:, (PACK - 1) * 2 * late + P :]
-        nc.scalar.copy(
-            z_early.rearrange("p (b v u) -> p b v u", v=P, u=2), words_back[:].rearrange("p b u v -> p b v u")
-        )
-
-        out_rows = out.rearrange("(a p) v -> p a v", p=P)
+        def late_steps(lo, hi):
+            nc.vector.tensor_tensor(step[:, 2:, lo:hi], spread[:, :, lo:hi], gate[:, 2:, lo:hi], ALU.mult)
 
         def blend(lo, hi):
             z = keep.tile([P, hi - lo, PACK], BF16, name="z%d" % hi, align_bytes=64)
             nc.vector.tensor_tensor(
                 z[:].rearrange("p (c i) t -> p c t i", i=2),
-                part_left[:, :, lo - EARLY : hi - EARLY].rearrange("p t (c i) -> p c t i", i=2),
-                part_right[:, :, lo - EARLY : hi - EARLY].rearrange("p t (c i) -> p c t i", i=2),
+                base[:, :, lo:hi].rearrange("p t (c i) -> p c t i", i=2),
+                step[:, :, lo:hi].rearrange("p t (c i) -> p c t i", i=2),
                 ALU.add,
             )
             return z[:]
 
-        def finish(z, lo, hi):
-            width = hi - lo
-            z_codes, z_scale = quantize(z, "z%d" % lo)
-            blocks = 1 if lo == 0 else 2
-            for first in range(0, PACK, blocks):
-                bank = psum.tile([P, blocks, width], F32, name="bank")
-                for a in range(blocks):
-                    cols = slice((first + a) * P, (first + a + 1) * P)
-                    nc.tensor.matmul_mx(
-                        out=bank[:, a, :],
-                        lhsT=w3_codes[:, cols].bitcast(FP8X4),
-                        lhsT_scale=w3_scale[:, cols],
-                        rhs=z_codes.bitcast(FP8X4),
-                        rhs_scale=z_scale,
-                        start=True,
-                        stop=True,
-                    )
-                result = keep.tile([P, blocks, width], F32, name="result%d_%d" % (lo, first))
-                rows = out_rows[:, first : first + blocks, lo:hi]
-                if hi == V and first > 0:
-                    nc.vector.tensor_copy(result[:], bank[:])
-                    nc.sync.dma_start(rows, result[:])
-                elif hi == V:
-                    nc.scalar.copy(result[:], bank[:])
-                    nc.scalar.dma_start(rows, result[:])
-                else:
-                    nc.scalar.copy(result[:], bank[:])
-                    nc.sync.dma_start(rows, result[:])
+        out_rows = out.rearrange("(a p) v -> p a v", p=P)
 
-        held_gate = keep.tile([P, P], F32, name="rounded1")
-        nc.scalar.activation(held_gate[:], diffs[3][:, EARLY : EARLY + P], SIGMOID)
-        finish(z_early.bitcast(BF16).rearrange("p (v t) -> p v t", t=PACK), 0, EARLY)
-        t = PACK - 1
-        before = None
-        for lo, hi in PIECES:
-            if before is None:
-                nc.vector.tensor_tensor(
-                    part_left[:, t, :P], val_rows[t][:].indirect(left_sb[:, lo // 16 : hi // 16]), held_gate[:], ALU.mult
+        def finish(z_q, lo, hi, first, blocks):
+            z_codes, z_scale = z_q
+            bank = psum.tile([P, blocks, hi - lo], F32, name="bank")
+            for a in range(blocks):
+                codes, scale = w3_q[first + a]
+                nc.tensor.matmul_mx(
+                    out=bank[:, a, :],
+                    lhsT=codes.bitcast(FP8X4),
+                    lhsT_scale=scale,
+                    rhs=z_codes.bitcast(FP8X4),
+                    rhs_scale=z_scale,
+                    start=True,
+                    stop=True,
                 )
+            result = keep.tile([P, blocks, hi - lo], F32, name="result%d_%d" % (lo, first))
+            rows = out_rows[:, first : first + blocks, lo:hi]
+            if hi == V and first > 0:
+                nc.vector.tensor_copy(result[:], bank[:])
+                nc.sync.dma_start(rows, result[:])
+            elif hi == V:
+                nc.scalar.copy(result[:], bank[:])
+                nc.scalar.dma_start(rows, result[:])
             else:
-                weigh(part_left[:, t, lo - EARLY : hi - EARLY], left_sb, q_left, t, lo, hi)
-            if before is not None:
-                z = blend(*before)
-            weigh(part_right[:, t, lo - EARLY : hi - EARLY], right_sb, q_right, t, lo, hi)
-            if before is not None:
-                finish(z, *before)
-            before = (lo, hi)
-        finish(blend(*before), *before)
+                nc.scalar.copy(result[:], bank[:])
+                nc.sync.dma_start(rows, result[:])
+
+        rest = staged.tile([P, 2, P, PACK], BF16, name="w1_rest", offset=0, align_bytes=64)
+        interleave(nc.scalar.copy, rest[:, 0], w1_raw[:], 2)
+        s0 = project(w1_q[0], "s0", nc.scalar.copy, BANK // 2)
+        interleave(nc.vector.tensor_copy, rest[:, 1], w1_raw[:], 3)
+        w1_q.append(quantize(second[:], "w1_1"))
+        w1_q.extend(split(quantize(rest[:].rearrange("p t c j -> p (t c) j"), "w1_23")))
+
+        def w2_round(grouped, t):
+            gpsimd_round(
+                grouped.rearrange("p (b r) j -> p b r j", r=8),
+                w2_raw[:].rearrange("p j (b t r) -> p t b r j", t=PACK, r=8)[:, t],
+            )
+
+        w2_early = keep.tile([P, 2, P, PACK], BF16, name="w2_early", align_bytes=64)
+        shared = keep.tile([P, 3 * P * PACK], BF16, name="shared", align_bytes=64)
+        slots = shared[:].rearrange("p (u c j) -> p u c j", u=3, j=PACK)
+        interleave(nc.vector.tensor_copy, slots[:, 2], w2_raw[:], 3)
+        for e in range(2):
+            w2_round(w2_early[:, e], e)
+
+        r0 = right_scores(s0, 0, nc.vector.tensor_copy)
+        s1 = project(w1_q[1], "s1", nc.scalar.copy)
+        w2_q = split(quantize(w2_early[:].rearrange("p t c j -> p (t c) j"), "w2_01"))
+        difference(s0, r0, 0)
+        r1 = right_scores(s1, 1, scalar_gather)
+        s2 = project(w1_q[2], "s2", nc.scalar.copy)
+        difference(s1, r1, 1)
+        both_gates(0)
+        w2_round(slots[:, 1], 2)
+        gpsimd_round(*w3_views(slots[:, 0], 0, P))
+        v0 = project(w2_q[0], "s1", nc.vector.tensor_copy)
+        r2 = right_scores(s2, 2, scalar_gather)
+        w2_q.extend(split(quantize(slots[:, 1:].rearrange("p t c j -> p (t c) j"), "w2_23")))
+        weigh(v0, 0)
+        v1 = project(w2_q[1], "val1", nc.scalar.copy)
+        both_gates(1)
+        difference(s2, r2, 2)
+        s3 = project(w1_q[3], "s3", nc.scalar.copy)
+        weigh(v1, 1)
+        r3 = right_scores(s3, 3, scalar_gather)
+        v2 = project(w2_q[2], "val2", nc.scalar.copy)
+        difference(s3, r3, 3)
+        right_values(v2, 2, 0, EARLY)
+        v3 = project(w2_q[3], "val3", nc.scalar.copy)
+        value_spread(v2, 2, 0, EARLY)
+        right_values(v3, 3, 0, EARLY)
+        late_gates(0, EARLY)
+        value_spread(v3, 3, 0, EARLY)
+        w3_q = [quantize(slots[:, 0], "w3_low")]
+        right_values(v2, 2, EARLY, V)
+        late_steps(0, EARLY)
+        right_values(v3, 3, EARLY, V)
+        value_spread(v2, 2, EARLY, V)
+        z_early = blend(0, EARLY)
+        late_gates(EARLY, V)
+        w3_high = keep.tile([P, N - P, PACK], BF16, name="w3_high", align_bytes=64)
+        nc.scalar.copy(*w3_views(w3_high[:], P, N))
+        value_spread(v3, 3, EARLY, V)
+        early_q = quantize(z_early, "z_early")
+        finish(early_q, 0, EARLY, 0, 1)
+        late_steps(EARLY, LAST)
+        w3_q.extend(split(quantize(w3_high[:], "w3_high")))
+        for a in range(1, PACK):
+            finish(early_q, 0, EARLY, a, 1)
+        z_middle = blend(EARLY, LAST)
+        late_steps(LAST, V)
+        middle_q = quantize(z_middle, "z_middle")
+        for first in range(0, PACK, 2):
+            finish(middle_q, EARLY, LAST, first, 2)
+        last_q = quantize(blend(LAST, V), "z_last")
+        for first in range(0, PACK, 2):
+            finish(last_q, LAST, V, first, 2)

@@ -256,7 +256,6 @@ def tile_picked_tourney_none_p_kernel(
         difference(s1, r1, 1)
         both_gates(0)
         w2_round(slots[:, 1], 2)
-        gpsimd_round(*w3_views(slots[:, 0], 0, P))
         v0 = project(w2_q[0], "s1", nc.vector.tensor_copy)
         r2 = right_scores(s2, 2, scalar_gather)
         w2_q.extend(split(quantize(slots[:, 1:].rearrange("p t c j -> p (t c) j"), "w2_23")))
@@ -271,25 +270,28 @@ def tile_picked_tourney_none_p_kernel(
         difference(s3, r3, 3)
         right_values(v2, 2, 0, EARLY)
         v3 = project(w2_q[3], "val3", nc.scalar.copy)
+        w3_low = keep.tile([P, N // 2, PACK], BF16, name="w3_low", align_bytes=64)
+        nc.scalar.copy(*w3_views(w3_low[:], 0, N // 2))
         value_spread(v2, 2, 0, EARLY)
         right_values(v3, 3, 0, EARLY)
         late_gates(0, EARLY)
         value_spread(v3, 3, 0, EARLY)
-        w3_q = [quantize(slots[:, 0], "w3_low")]
+        w3_q = split(quantize(w3_low[:], "w3_low"))
         right_values(v2, 2, EARLY, V)
         late_steps(0, EARLY)
         right_values(v3, 3, EARLY, V)
         value_spread(v2, 2, EARLY, V)
         z_early = blend(0, EARLY)
         late_gates(EARLY, V)
-        w3_high = keep.tile([P, N - P, PACK], BF16, name="w3_high", align_bytes=64)
-        nc.scalar.copy(*w3_views(w3_high[:], P, N))
+        w3_high = keep.tile([P, N // 2, PACK], BF16, name="w3_high", align_bytes=64)
+        nc.scalar.copy(*w3_views(w3_high[:], N // 2, N))
         value_spread(v3, 3, EARLY, V)
         early_q = quantize(z_early, "z_early")
-        finish(early_q, 0, EARLY, 0, 1)
+        for a in range(2):
+            finish(early_q, 0, EARLY, a, 1)
         late_steps(EARLY, LAST)
         w3_q.extend(split(quantize(w3_high[:], "w3_high")))
-        for a in range(1, PACK):
+        for a in range(2, PACK):
             finish(early_q, 0, EARLY, a, 1)
         z_middle = blend(EARLY, LAST)
         late_steps(LAST, V)

@@ -125,7 +125,7 @@ def tile_picked_tourney_none_p_kernel(
             return banks
 
         def project(weight, name, copy, width=BANK):
-            rows = keep.tile([P, S], F32, name=name)
+            rows = keep.tile([P, S], F32, name=name, align_bytes=64)
             for n, bank in enumerate(multiply(weight, width)):
                 copy(rows[:, n * width : (n + 1) * width], bank[:])
             return rows
@@ -241,11 +241,10 @@ def tile_picked_tourney_none_p_kernel(
             )
 
         w2_early = keep.tile([P, 2, P, PACK], BF16, name="w2_early", align_bytes=64)
-        shared = keep.tile([P, 3 * P * PACK], BF16, name="shared", align_bytes=64)
-        slots = shared[:].rearrange("p (u c j) -> p u c j", u=3, j=PACK)
-        interleave(nc.vector.tensor_copy, slots[:, 2], w2_raw[:], 3)
-        for e in range(2):
-            w2_round(w2_early[:, e], e)
+        shared = keep.tile([P, 2 * P * PACK], BF16, name="shared", align_bytes=64)
+        slots = shared[:].rearrange("p (u c j) -> p u c j", u=2, j=PACK)
+        interleave(nc.vector.tensor_copy, w2_early[:, 0], w2_raw[:], 0)
+        w2_round(w2_early[:, 1], 1)
 
         r0 = right_scores(s0, 0, nc.vector.tensor_copy)
         s1 = project(w1_q[1], "s1", nc.scalar.copy)
@@ -255,10 +254,11 @@ def tile_picked_tourney_none_p_kernel(
         s2 = project(w1_q[2], "s2", nc.scalar.copy)
         difference(s1, r1, 1)
         both_gates(0)
-        w2_round(slots[:, 1], 2)
+        interleave(nc.vector.tensor_copy, slots[:, 1], w2_raw[:], 3)
+        w2_round(slots[:, 0], 2)
         v0 = project(w2_q[0], "s1", nc.vector.tensor_copy)
         r2 = right_scores(s2, 2, scalar_gather)
-        w2_q.extend(split(quantize(slots[:, 1:].rearrange("p t c j -> p (t c) j"), "w2_23")))
+        w2_q.extend(split(quantize(slots.rearrange("p t c j -> p (t c) j"), "w2_23")))
         weigh(v0, 0)
         v1 = project(w2_q[1], "val1", nc.scalar.copy)
         both_gates(1)
@@ -268,29 +268,28 @@ def tile_picked_tourney_none_p_kernel(
         r3 = right_scores(s3, 3, scalar_gather)
         v2 = project(w2_q[2], "val2", nc.scalar.copy)
         difference(s3, r3, 3)
-        right_values(v2, 2, 0, EARLY)
         v3 = project(w2_q[3], "val3", nc.scalar.copy)
-        w3_low = keep.tile([P, N // 2, PACK], BF16, name="w3_low", align_bytes=64)
-        nc.scalar.copy(*w3_views(w3_low[:], 0, N // 2))
-        value_spread(v2, 2, 0, EARLY)
+        right_values(v2, 2, 0, EARLY)
         right_values(v3, 3, 0, EARLY)
         late_gates(0, EARLY)
+        w3_grouped = keep.tile([P, 2, N // 2, PACK], BF16, name="s3", align_bytes=64)
+        nc.vector.tensor_copy(*w3_views(w3_grouped[:, 0], 0, N // 2))
+        value_spread(v2, 2, 0, EARLY)
         value_spread(v3, 3, 0, EARLY)
-        w3_q = split(quantize(w3_low[:], "w3_low"))
+        w3_q = split(quantize(w3_grouped[:, 0], "w3_low"))
         right_values(v2, 2, EARLY, V)
         late_steps(0, EARLY)
         right_values(v3, 3, EARLY, V)
         value_spread(v2, 2, EARLY, V)
         z_early = blend(0, EARLY)
         late_gates(EARLY, V)
-        w3_high = keep.tile([P, N // 2, PACK], BF16, name="w3_high", align_bytes=64)
-        nc.scalar.copy(*w3_views(w3_high[:], N // 2, N))
+        nc.scalar.copy(*w3_views(w3_grouped[:, 1], N // 2, N))
         value_spread(v3, 3, EARLY, V)
         early_q = quantize(z_early, "z_early")
         for a in range(2):
             finish(early_q, 0, EARLY, a, 1)
         late_steps(EARLY, LAST)
-        w3_q.extend(split(quantize(w3_high[:], "w3_high")))
+        w3_q.extend(split(quantize(w3_grouped[:, 1], "w3_high")))
         for a in range(2, PACK):
             finish(early_q, 0, EARLY, a, 1)
         z_middle = blend(EARLY, LAST)

@@ -268,28 +268,29 @@ def tile_picked_tourney_none_p_kernel(
         r3 = right_scores(s3, 3, scalar_gather)
         v2 = project(w2_q[2], "val2", nc.scalar.copy)
         difference(s3, r3, 3)
-        v3 = project(w2_q[3], "val3", nc.scalar.copy)
         right_values(v2, 2, 0, EARLY)
+        v3 = project(w2_q[3], "val3", nc.scalar.copy)
+        w3_low = keep.tile([P, N // 2, PACK], BF16, name="w3_low", align_bytes=64)
+        nc.scalar.copy(*w3_views(w3_low[:], 0, N // 2))
+        value_spread(v2, 2, 0, EARLY)
         right_values(v3, 3, 0, EARLY)
         late_gates(0, EARLY)
-        w3_grouped = keep.tile([P, 2, N // 2, PACK], BF16, name="s3", align_bytes=64)
-        nc.vector.tensor_copy(*w3_views(w3_grouped[:, 0], 0, N // 2))
-        value_spread(v2, 2, 0, EARLY)
         value_spread(v3, 3, 0, EARLY)
-        w3_q = split(quantize(w3_grouped[:, 0], "w3_low"))
+        w3_q = split(quantize(w3_low[:], "w3_low"))
         right_values(v2, 2, EARLY, V)
         late_steps(0, EARLY)
         right_values(v3, 3, EARLY, V)
         value_spread(v2, 2, EARLY, V)
         z_early = blend(0, EARLY)
         late_gates(EARLY, V)
-        nc.scalar.copy(*w3_views(w3_grouped[:, 1], N // 2, N))
+        w3_high = keep.tile([P, N // 2, PACK], BF16, name="w3_high", align_bytes=64)
+        nc.scalar.copy(*w3_views(w3_high[:], N // 2, N))
         value_spread(v3, 3, EARLY, V)
         early_q = quantize(z_early, "z_early")
         for a in range(2):
             finish(early_q, 0, EARLY, a, 1)
         late_steps(EARLY, LAST)
-        w3_q.extend(split(quantize(w3_grouped[:, 1], "w3_high")))
+        w3_q.extend(split(quantize(w3_high[:], "w3_high")))
         for a in range(2, PACK):
             finish(early_q, 0, EARLY, a, 1)
         z_middle = blend(EARLY, LAST)

@@ -21,6 +21,7 @@ PACK = 4
 BANK = 512
 HEAD = 768
 SCALAR_SHARE = 80
+GPSIMD_SHARE = 80
 EARLY = 256
 LAST = 384
 
@@ -72,9 +73,9 @@ def tile_picked_tourney_none_p_kernel(
                 raw.rearrange("p j (b t h i) -> p t b h j i", t=PACK, h=4, i=2)[:, t],
             )
 
-        def quantize(grouped, name):
+        def quantize(grouped, name, tag=None):
             width = grouped.shape[1]
-            codes = keep.tile([P, width], U32, name=name + "_codes", align_bytes=64)
+            codes = keep.tile([P, width], U32, name=name + "_codes", tag=tag or name + "_codes", align_bytes=64)
             scale = keep.tile([P, width], U8, name=name + "_scale", align_bytes=64)
             nc.vector.quantize_mx(
                 out=codes[:].bitcast(FP8X4), scales=scale[:], in_=grouped.rearrange("p c j -> p (c j)")
@@ -105,13 +106,13 @@ def tile_picked_tourney_none_p_kernel(
         def x_codes(lo, hi):
             return x_head[:, lo:hi] if hi <= HEAD else x_tail[:, lo - HEAD : hi - HEAD]
 
-        def multiply(weight, width=BANK):
+        def project(weight, name, copies, cuts=(0, BANK, S)):
             codes, scale = weight
-            banks = []
-            for lo in range(0, S, width):
-                bank = psum.tile([P, width], F32, name="bank")
-                cuts = sorted({lo, lo + width} | ({HEAD} if lo < HEAD < lo + width else set()))
-                for a, b in zip(cuts, cuts[1:]):
+            rows = keep.tile([P, S], F32, name=name, align_bytes=64)
+            for lo, hi, copy in zip(cuts, cuts[1:], copies):
+                bank = psum.tile([P, hi - lo], F32, name="bank")
+                inner = sorted({lo, hi} | ({HEAD} if lo < HEAD < hi else set()))
+                for a, b in zip(inner, inner[1:]):
                     nc.tensor.matmul_mx(
                         out=bank[:, a - lo : b - lo],
                         lhsT=codes.bitcast(FP8X4),
@@ -121,14 +122,11 @@ def tile_picked_tourney_none_p_kernel(
                         start=True,
                         stop=True,
                     )
-                banks.append(bank)
-            return banks
-
-        def project(weight, name, copy, width=BANK):
-            rows = keep.tile([P, S], F32, name=name, align_bytes=64)
-            for n, bank in enumerate(multiply(weight, width)):
-                copy(rows[:, n * width : (n + 1) * width], bank[:])
+                copy(rows[:, lo:hi], bank[:])
             return rows
+
+        on_scalar = (nc.scalar.copy, nc.scalar.copy)
+        on_vector = (nc.vector.tensor_copy, nc.vector.tensor_copy)
 
         def split(weight):
             codes, scale = weight
@@ -156,16 +154,21 @@ def tile_picked_tourney_none_p_kernel(
         base = keep.tile([P, PACK, V], F32, name="base")
         step = keep.tile([P, PACK, V], F32, name="step")
 
-        def right_scores(rows, t, gather):
+        def right_scores(rows, t, gather, width=V):
             if t == 1:
                 s_right = shared[:, : 2 * V].bitcast(F32)
             else:
-                s_right = keep.tile([P, V], F32, name="s_right%d" % t)[:]
-            gather(s_right, picked(rows, right_sb))
+                s_right = keep.tile([P, V], F32, name="s_right%d" % t, align_bytes=64)[:]
+            for lo in range(0, V, width):
+                gather(s_right[:, lo : lo + width], picked(rows, right_sb, lo, lo + width))
             return s_right
 
-        def difference(rows, s_right, t):
-            nc.vector.tensor_tensor(diff[:, t, :], picked(rows, left_sb), s_right, ALU.subtract)
+        def difference(rows, s_right, t, width=V):
+            for lo in range(0, V, width):
+                hi = lo + width
+                nc.vector.tensor_tensor(
+                    diff[:, t, lo:hi], picked(rows, left_sb, lo, hi), s_right[:, lo:hi], ALU.subtract
+                )
 
         def both_gates(t):
             nc.scalar.activation(gate[:, t, :], diff[:, t, :], SIGMOID)
@@ -186,8 +189,8 @@ def tile_picked_tourney_none_p_kernel(
         def late_gates(lo, hi):
             nc.scalar.activation(gate[:, 2:, lo:hi], diff[:, 2:, lo:hi], SIGMOID)
 
-        def late_steps(lo, hi):
-            nc.vector.tensor_tensor(step[:, 2:, lo:hi], spread[:, :, lo:hi], gate[:, 2:, lo:hi], ALU.mult)
+        def late_steps(lo, hi, t):
+            nc.vector.tensor_tensor(step[:, t, lo:hi], spread[:, t - 2, lo:hi], gate[:, t, lo:hi], ALU.mult)
 
         def blend(lo, hi):
             z = keep.tile([P, hi - lo, PACK], BF16, name="z%d" % hi, align_bytes=64)
@@ -229,47 +232,48 @@ def tile_picked_tourney_none_p_kernel(
 
         rest = staged.tile([P, 2, P, PACK], BF16, name="w1_rest", offset=0, align_bytes=64)
         interleave(nc.scalar.copy, rest[:, 0], w1_raw[:], 2)
-        s0 = project(w1_q[0], "s0", nc.scalar.copy, BANK // 2)
+        s0 = project(w1_q[0], "s0", on_scalar + on_scalar, range(0, S + 1, BANK // 2))
         interleave(nc.vector.tensor_copy, rest[:, 1], w1_raw[:], 3)
         w1_q.append(quantize(second[:], "w1_1"))
         w1_q.extend(split(quantize(rest[:].rearrange("p t c j -> p (t c) j"), "w1_23")))
 
-        def w2_round(grouped, t):
+        def w2_round(grouped, raw, t):
             gpsimd_round(
                 grouped.rearrange("p (b r) j -> p b r j", r=8),
-                w2_raw[:].rearrange("p j (b t r) -> p t b r j", t=PACK, r=8)[:, t],
+                raw.rearrange("p j (b t r) -> p t b r j", t=PACK, r=8)[:, t],
             )
 
         w2_early = keep.tile([P, 2, P, PACK], BF16, name="w2_early", align_bytes=64)
-        shared = keep.tile([P, 2 * P * PACK], BF16, name="shared", align_bytes=64)
-        slots = shared[:].rearrange("p (u c j) -> p u c j", u=2, j=PACK)
-        interleave(nc.vector.tensor_copy, w2_early[:, 0], w2_raw[:], 0)
-        w2_round(w2_early[:, 1], 1)
+        interleave(nc.scalar.copy, w2_early[:, 0], w2_raw[:], 0)
+        shared = keep.tile([P, V * 2 + (P - GPSIMD_SHARE) * PACK], BF16, name="shared", align_bytes=64)
+        w2_late = shared[:, V * 2 - (P + GPSIMD_SHARE) * PACK :].rearrange("p (u c j) -> p u c j", u=2, j=PACK)
+        w2_round(w2_late[:, 1, GPSIMD_SHARE:], w2_raw[:, :, GPSIMD_SHARE * PACK :], 2)
+        w2_round(w2_early[:, 1], w2_raw[:], 1)
 
-        r0 = right_scores(s0, 0, nc.vector.tensor_copy)
-        s1 = project(w1_q[1], "s1", nc.scalar.copy)
-        w2_q = split(quantize(w2_early[:].rearrange("p t c j -> p (t c) j"), "w2_01"))
-        difference(s0, r0, 0)
+        r0 = right_scores(s0, 0, nc.vector.tensor_copy, V // 2)
+        s1 = project(w1_q[1], "s1", on_scalar)
+        difference(s0, r0, 0, V // 2)
+        w2_q = split(quantize(w2_early[:].rearrange("p t c j -> p (t c) j"), "w2_01", tag="s_right0"))
         r1 = right_scores(s1, 1, scalar_gather)
-        s2 = project(w1_q[2], "s2", nc.scalar.copy)
+        s2 = project(w1_q[2], "s2", on_scalar)
         difference(s1, r1, 1)
         both_gates(0)
-        interleave(nc.vector.tensor_copy, slots[:, 1], w2_raw[:], 3)
-        w2_round(slots[:, 0], 2)
-        v0 = project(w2_q[0], "s1", nc.vector.tensor_copy)
+        w2_round(w2_late[:, 1, :GPSIMD_SHARE], w2_raw[:, :, : GPSIMD_SHARE * PACK], 2)
+        v0 = project(w2_q[0], "s1", on_vector)
+        interleave(nc.vector.tensor_copy, w2_late[:, 0], w2_raw[:], 3)
         r2 = right_scores(s2, 2, scalar_gather)
-        w2_q.extend(split(quantize(slots.rearrange("p t c j -> p (t c) j"), "w2_23")))
+        w2_q.extend(reversed(split(quantize(w2_late.rearrange("p t c j -> p (t c) j"), "w2_32"))))
         weigh(v0, 0)
-        v1 = project(w2_q[1], "val1", nc.scalar.copy)
+        v1 = project(w2_q[1], "val1", on_scalar)
         both_gates(1)
         difference(s2, r2, 2)
-        s3 = project(w1_q[3], "s3", nc.scalar.copy)
+        s3 = project(w1_q[3], "s3", on_scalar)
         weigh(v1, 1)
         r3 = right_scores(s3, 3, scalar_gather)
-        v2 = project(w2_q[2], "val2", nc.scalar.copy)
+        v2 = project(w2_q[2], "val2", on_scalar)
         difference(s3, r3, 3)
         right_values(v2, 2, 0, EARLY)
-        v3 = project(w2_q[3], "val3", nc.scalar.copy)
+        v3 = project(w2_q[3], "val3", on_scalar)
         w3_low = keep.tile([P, N // 2, PACK], BF16, name="w3_low", align_bytes=64)
         nc.scalar.copy(*w3_views(w3_low[:], 0, N // 2))
         value_spread(v2, 2, 0, EARLY)
@@ -278,7 +282,8 @@ def tile_picked_tourney_none_p_kernel(
         value_spread(v3, 3, 0, EARLY)
         w3_q = split(quantize(w3_low[:], "w3_low"))
         right_values(v2, 2, EARLY, V)
-        late_steps(0, EARLY)
+        for t in (2, 3):
+            late_steps(0, EARLY, t)
         right_values(v3, 3, EARLY, V)
         value_spread(v2, 2, EARLY, V)
         z_early = blend(0, EARLY)
@@ -289,12 +294,14 @@ def tile_picked_tourney_none_p_kernel(
         early_q = quantize(z_early, "z_early")
         for a in range(2):
             finish(early_q, 0, EARLY, a, 1)
-        late_steps(EARLY, LAST)
+        for t in (2, 3):
+            late_steps(EARLY, LAST, t)
         w3_q.extend(split(quantize(w3_high[:], "w3_high")))
         for a in range(2, PACK):
             finish(early_q, 0, EARLY, a, 1)
         z_middle = blend(EARLY, LAST)
-        late_steps(LAST, V)
+        for t in (2, 3):
+            late_steps(LAST, V, t)
         middle_q = quantize(z_middle, "z_middle")
         for first in range(0, PACK, 2):
             finish(middle_q, EARLY, LAST, first, 2)

@@ -272,26 +272,26 @@ def tile_picked_tourney_none_p_kernel(
         r3 = right_scores(s3, 3, scalar_gather)
         v2 = project(w2_q[2], "val2", on_scalar)
         difference(s3, r3, 3)
-        right_values(v2, 2, 0, EARLY)
         v3 = project(w2_q[3], "val3", on_scalar)
-        w3_low = keep.tile([P, N // 2, PACK], BF16, name="w3_low", align_bytes=64)
-        nc.scalar.copy(*w3_views(w3_low[:], 0, N // 2))
-        value_spread(v2, 2, 0, EARLY)
+        right_values(v2, 2, 0, EARLY)
         right_values(v3, 3, 0, EARLY)
         late_gates(0, EARLY)
+        value_spread(v2, 2, 0, EARLY)
         value_spread(v3, 3, 0, EARLY)
-        w3_q = split(quantize(w3_low[:], "w3_low"))
         right_values(v2, 2, EARLY, V)
         for t in (2, 3):
             late_steps(0, EARLY, t)
-        right_values(v3, 3, EARLY, V)
         value_spread(v2, 2, EARLY, V)
         z_early = blend(0, EARLY)
+        w3_low = keep.tile([P, N // 2, PACK], BF16, name="w3_low", align_bytes=64)
+        nc.scalar.copy(*w3_views(w3_low[:], 0, N // 2))
+        w3_q = split(quantize(w3_low[:], "w3_low"))
+        early_q = quantize(z_early, "z_early")
+        right_values(v3, 3, EARLY, V)
+        value_spread(v3, 3, EARLY, V)
         late_gates(EARLY, V)
         w3_high = keep.tile([P, N // 2, PACK], BF16, name="w3_high", align_bytes=64)
         nc.scalar.copy(*w3_views(w3_high[:], N // 2, N))
-        value_spread(v3, 3, EARLY, V)
-        early_q = quantize(z_early, "z_early")
         for a in range(2):
             finish(early_q, 0, EARLY, a, 1)
         for t in (2, 3):

@@ -24,6 +24,8 @@ SCALAR_SHARE = 80
 GPSIMD_SHARE = 80
 EARLY = 256
 LAST = 384
+TERM_PAD = 8
+ROW_PAD = 16
 
 
 def tile_picked_tourney_none_p_kernel(
@@ -98,10 +100,10 @@ def tile_picked_tourney_none_p_kernel(
         x_tail = staged.tile([P, S - HEAD], U32, name="x_tail", offset=2048, align_bytes=64)
         nc.vector.tensor_copy(x_tail[:], word_window.indirect(offs_sb[:, HEAD // 16 :]))
 
-        w3_raw = keep.tile([P, PACK, N], F32, name="w3_raw", tag="words_then_w3")
+        w3_raw = keep.tile([P, PACK, N + ROW_PAD], F32, name="w3_raw", tag="words_then_w3")
         w3_rows = w3.rearrange("(b t r) n -> t b r n", t=PACK, r=8)
         for t in range(PACK):
-            nc.sync.dma_start(w3_raw[:, t, :], w3_rows[t])
+            nc.sync.dma_start(w3_raw[:, t, :N], w3_rows[t])
 
         def x_codes(lo, hi):
             return x_head[:, lo:hi] if hi <= HEAD else x_tail[:, lo - HEAD : hi - HEAD]
@@ -151,8 +153,8 @@ def tile_picked_tourney_none_p_kernel(
         gate = keep.tile([P, PACK, V], F32, name="gate")
         counter = keep.tile([P, 2, V], F32, name="counter")
         spread = keep.tile([P, 2, V], F32, name="spread")
-        base = keep.tile([P, PACK, V], F32, name="base")
-        step = keep.tile([P, PACK, V], F32, name="step")
+        terms = keep.tile([P, 2 * PACK, V + TERM_PAD], F32, name="terms")
+        base, step = terms[:, :PACK, :V], terms[:, PACK:, :V]
 
         def right_scores(rows, t, gather, width=V):
             if t == 1:

@@ -19,13 +19,10 @@ COPY = mybir.ActivationFunctionType.Copy
 P = 128
 PACK = 4
 BANK = 512
-HEAD = 768
-SCALAR_SHARE = 80
-GPSIMD_SHARE = 80
+QUARTER = 256
 EARLY = 256
 LAST = 384
-TERM_PAD = 8
-ROW_PAD = 16
+ROW_BYTES = S * 4
 
 
 def tile_picked_tourney_none_p_kernel(
@@ -35,39 +32,40 @@ def tile_picked_tourney_none_p_kernel(
     with ExitStack() as ctx:
         lists = ctx.enter_context(tc.tile_pool(name="lists", bufs=1))
         keep = ctx.enter_context(tc.tile_pool(name="keep", bufs=1))
-        psum = ctx.enter_context(tc.psum_pool(name="psum", bufs=8))
+        placed = ctx.enter_context(tc.tile_pool(name="placed", bufs=1))
+        psum = ctx.enter_context(tc.psum_pool(name="psum", bufs=1))
 
         offs_sb = lists.tile([P, S // 16], U16, name="offs_sb")
         left_sb = lists.tile([P, V // 16], U16, name="left_sb")
         right_sb = lists.tile([P, V // 16], U16, name="right_sb")
 
         scale_table = keep.tile([P, T], U8, name="scale_table")
-        word_table = keep.tile([P, T], I32, name="word_table", tag="words_then_w3")
+        word_table = keep.tile([P, T], I32, name="word_table")
         w1_raw = keep.tile([P, PACK, H], F32, name="w1_raw")
+        w2_raw = keep.tile([P, PACK, H], F32, name="w2_raw")
+        w3_raw = keep.tile([P, PACK, N], F32, name="w3_raw")
 
         nc.vector.memset(scale_table[:].bitcast(I32), 0)
         warm = keep.tile([P, 2], F32, name="warm")
         nc.gpsimd.memset(warm[:, :1], 0.0)
         nc.scalar.activation(warm[:, 1:], warm[:, :1], SIGMOID)
+
+        w1_rows = w1.rearrange("(p j) c -> p j c", j=PACK)
+        nc.sync.dma_start(w1_raw[:, :2], w1_rows[:, :2])
         nc.sync.dma_start(offs_sb[:], offs)
-        words = x_words[0].rearrange("p n r -> p (n r)").bitcast(I32)
-        nc.sync.dma_start(word_table[:, : T // 4], words[:, : T // 4])
-        nc.sync.dma_start(right_sb[:], right)
         for r in range(4):
             nc.sync.dma_start(scale_table[r:P:32, :].bitcast(I32), x_scales[0, r:16:4, :].bitcast(I32))
-        nc.sync.dma_start(word_table[:, T // 4 :], words[:, T // 4 :])
-        nc.sync.dma_start(w1_raw[:], w1.rearrange("(p j) c -> p j c", j=PACK))
-        nc.sync.dma_start(left_sb[:], left)
-        w2_raw = keep.tile([P, PACK, H], F32, name="w2_raw")
+        nc.sync.dma_start(w1_raw[:, 2:], w1_rows[:, 2:])
+        nc.sync.dma_start(word_table[:], x_words[0].rearrange("p n r -> p (n r)").bitcast(I32))
         nc.sync.dma_start(w2_raw[:], w2.rearrange("(p j) c -> p j c", j=PACK))
+        nc.sync.dma_start(right_sb[:], right)
+        nc.sync.dma_start(left_sb[:], left)
+        w3_rows = w3.rearrange("(b t r) n -> t b r n", t=PACK, r=8)
+        for t in range(PACK):
+            nc.sync.dma_start(w3_raw[:, t, :], w3_rows[t])
 
         x_scale = keep.tile([P, S], U8, name="x_scale", align_bytes=64)
         nc.vector.tensor_copy(x_scale[:], scale_table[:].indirect(offs_sb[:]))
-
-        staged = ctx.enter_context(tc.tile_pool(name="staged", bufs=1))
-        word_window = word_table[:].bitcast(U32)
-        x_head = keep.tile([P, HEAD], U32, name="x_head", align_bytes=64)
-        nc.vector.tensor_copy(x_head[:], word_window.indirect(offs_sb[:, : HEAD // 16]))
 
         def interleave(copy, grouped, raw, t):
             copy(
@@ -84,115 +82,70 @@ def tile_picked_tourney_none_p_kernel(
             )
             return codes[:], scale[:]
 
-        first = staged.tile([P, P, PACK], BF16, name="w1_first", offset=1536, align_bytes=64)
-        second = keep.tile([P, P, PACK], BF16, name="w1_second", align_bytes=64)
-        interleave(nc.scalar.copy, first[:, :SCALAR_SHARE], w1_raw[:, :, : SCALAR_SHARE * PACK], 0)
-        nc.gpsimd.tensor_scalar(
-            first[:, SCALAR_SHARE:].rearrange("p (b r) j -> p b r j", r=8),
-            w1_raw[:, :, SCALAR_SHARE * PACK :].rearrange("p j (b t r) -> p t b r j", t=PACK, r=8)[:, 0],
-            1.0,
-            0.0,
-            ALU.mult,
-            ALU.add,
-        )
-        interleave(nc.scalar.copy, second[:], w1_raw[:], 1)
-        w1_q = [quantize(first[:], "w1_0")]
-        x_tail = staged.tile([P, S - HEAD], U32, name="x_tail", offset=2048, align_bytes=64)
-        nc.vector.tensor_copy(x_tail[:], word_window.indirect(offs_sb[:, HEAD // 16 :]))
-
-        w3_raw = keep.tile([P, PACK, N + ROW_PAD], F32, name="w3_raw", tag="words_then_w3")
-        w3_rows = w3.rearrange("(b t r) n -> t b r n", t=PACK, r=8)
-        for t in range(PACK):
-            nc.sync.dma_start(w3_raw[:, t, :N], w3_rows[t])
-
-        def x_codes(lo, hi):
-            return x_head[:, lo:hi] if hi <= HEAD else x_tail[:, lo - HEAD : hi - HEAD]
-
-        def project(weight, name, copies, cuts=(0, BANK, S)):
-            codes, scale = weight
-            rows = keep.tile([P, S], F32, name=name, align_bytes=64)
-            for lo, hi, copy in zip(cuts, cuts[1:], copies):
-                bank = psum.tile([P, hi - lo], F32, name="bank")
-                inner = sorted({lo, hi} | ({HEAD} if lo < HEAD < hi else set()))
-                for a, b in zip(inner, inner[1:]):
-                    nc.tensor.matmul_mx(
-                        out=bank[:, a - lo : b - lo],
-                        lhsT=codes.bitcast(FP8X4),
-                        lhsT_scale=scale,
-                        rhs=x_codes(a, b).bitcast(FP8X4),
-                        rhs_scale=x_scale[:, a:b],
-                        start=True,
-                        stop=True,
-                    )
-                copy(rows[:, lo:hi], bank[:])
-            return rows
-
-        on_scalar = (nc.scalar.copy, nc.scalar.copy)
-        on_vector = (nc.vector.tensor_copy, nc.vector.tensor_copy)
-
         def split(weight):
             codes, scale = weight
             return [(codes[:, u * P : (u + 1) * P], scale[:, u * P : (u + 1) * P]) for u in range(codes.shape[1] // P)]
 
-        def gpsimd_round(dst, src):
-            nc.gpsimd.tensor_scalar(dst, src, 1.0, 0.0, ALU.mult, ALU.add)
+        w1_low = keep.tile([P, 2, P, PACK], BF16, name="w1_low", align_bytes=64)
+        w1_high = keep.tile([P, 2, P, PACK], BF16, name="w1_high", align_bytes=64)
+        interleave(nc.scalar.copy, w1_low[:, 0], w1_raw[:], 0)
+        interleave(nc.scalar.copy, w1_low[:, 1], w1_raw[:], 1)
+        interleave(nc.scalar.copy, w1_high[:, 0], w1_raw[:], 2)
+        interleave(nc.vector.tensor_copy, w1_high[:, 1], w1_raw[:], 3)
+        w1_q = split(quantize(w1_low[:].rearrange("p t c j -> p (t c) j"), "w1_low"))
+        w1_q.extend(split(quantize(w1_high[:].rearrange("p t c j -> p (t c) j"), "w1_high")))
+
+        x_codes = keep.tile([P, S], U32, name="x_codes", align_bytes=64)
+        word_window = word_table[:].bitcast(U32)
+
+        def gather_words(lo, hi):
+            nc.vector.tensor_copy(x_codes[:, lo:hi], word_window.indirect(offs_sb[:, lo // 16 : hi // 16]))
+
+        def product(weight, lo, hi, bank_number):
+            codes, scale = weight
+            bank = psum.tile([P, hi - lo], F32, name="bank%d" % bank_number)
+            nc.tensor.matmul_mx(
+                out=bank[:],
+                lhsT=codes.bitcast(FP8X4),
+                lhsT_scale=scale,
+                rhs=x_codes[:, lo:hi].bitcast(FP8X4),
+                rhs_scale=x_scale[:, lo:hi],
+                start=True,
+                stop=True,
+            )
+            return bank
+
+        def project(copy, rows, weight, lo, hi, bank_number):
+            copy(rows[:, lo:hi], product(weight, lo, hi, bank_number)[:])
 
         def picked(rows, offsets, lo=0, hi=V):
             return rows[:].indirect(offsets[:, lo // 16 : hi // 16])
 
-        def scalar_gather(dst, src):
-            nc.scalar.activation(dst, src, COPY)
-
-        def w3_views(grouped, lo, hi):
-            return (
-                grouped.rearrange("p (c i) t -> p c t i", i=2),
-                w3_raw[:, :, lo:hi].rearrange("p t (c i) -> p c t i", i=2),
-            )
-
-        diff = keep.tile([P, PACK, V], F32, name="diff")
         gate = keep.tile([P, PACK, V], F32, name="gate")
-        counter = keep.tile([P, 2, V], F32, name="counter")
-        spread = keep.tile([P, 2, V], F32, name="spread")
-        terms = keep.tile([P, 2 * PACK, V + TERM_PAD], F32, name="terms")
-        base, step = terms[:, :PACK, :V], terms[:, PACK:, :V]
+        s_right = keep.tile([P, PACK, V], F32, name="s_right")
+        spread = keep.tile([P, PACK, V], F32, name="spread")
+        base = keep.tile([P, PACK, V], F32, name="base")
+        step = keep.tile([P, PACK, V], F32, name="step")
 
-        def right_scores(rows, t, gather, width=V):
-            if t == 1:
-                s_right = shared[:, : 2 * V].bitcast(F32)
-            else:
-                s_right = keep.tile([P, V], F32, name="s_right%d" % t, align_bytes=64)[:]
-            for lo in range(0, V, width):
-                gather(s_right[:, lo : lo + width], picked(rows, right_sb, lo, lo + width))
-            return s_right
+        def right_scores(rows, t):
+            nc.scalar.activation(s_right[:, t, :], picked(rows, right_sb), COPY)
 
-        def difference(rows, s_right, t, width=V):
-            for lo in range(0, V, width):
-                hi = lo + width
-                nc.vector.tensor_tensor(
-                    diff[:, t, lo:hi], picked(rows, left_sb, lo, hi), s_right[:, lo:hi], ALU.subtract
-                )
+        def difference(rows, t):
+            nc.vector.tensor_tensor(diff[:, t, :], picked(rows, left_sb), s_right[:, t, :], ALU.subtract)
 
-        def both_gates(t):
-            nc.scalar.activation(gate[:, t, :], diff[:, t, :], SIGMOID)
-            nc.scalar.activation(counter[:, t, :], diff[:, t, :], SIGMOID, scale=-1.0)
+        def right_values(rows, t, lo=0, hi=V):
+            nc.scalar.activation(base[:, t, lo:hi], picked(rows, right_sb, lo, hi), COPY)
 
-        def weigh(rows, t):
-            nc.vector.tensor_tensor(step[:, t, :], picked(rows, left_sb), gate[:, t, :], ALU.mult)
-            nc.vector.tensor_tensor(base[:, t, :], picked(rows, right_sb), counter[:, t, :], ALU.mult)
-
-        def right_values(rows, t, lo, hi):
-            scalar_gather(base[:, t, lo:hi], picked(rows, right_sb, lo, hi))
-
-        def value_spread(rows, t, lo, hi):
+        def value_spread(rows, t, lo=0, hi=V):
             nc.vector.tensor_tensor(
-                spread[:, t - 2, lo:hi], picked(rows, left_sb, lo, hi), base[:, t, lo:hi], ALU.subtract
+                spread[:, t, lo:hi], picked(rows, left_sb, lo, hi), base[:, t, lo:hi], ALU.subtract
             )
 
-        def late_gates(lo, hi):
-            nc.scalar.activation(gate[:, 2:, lo:hi], diff[:, 2:, lo:hi], SIGMOID)
+        def gates(first, lo, hi):
+            nc.scalar.activation(gate[:, first : first + 2, lo:hi], diff[:, first : first + 2, lo:hi], SIGMOID)
 
-        def late_steps(lo, hi, t):
-            nc.vector.tensor_tensor(step[:, t, lo:hi], spread[:, t - 2, lo:hi], gate[:, t, lo:hi], ALU.mult)
+        def late_step(lo, hi, t):
+            nc.vector.tensor_tensor(step[:, t, lo:hi], spread[:, t, lo:hi], gate[:, t, lo:hi], ALU.mult)
 
         def blend(lo, hi):
             z = keep.tile([P, hi - lo, PACK], BF16, name="z%d" % hi, align_bytes=64)
@@ -206,9 +159,9 @@ def tile_picked_tourney_none_p_kernel(
 
         out_rows = out.rearrange("(a p) v -> p a v", p=P)
 
-        def finish(z_q, lo, hi, first, blocks):
+        def finish(z_q, lo, hi, first, blocks, bank_number):
             z_codes, z_scale = z_q
-            bank = psum.tile([P, blocks, hi - lo], F32, name="bank")
+            bank = psum.tile([P, blocks, hi - lo], F32, name="bank%d" % bank_number)
             for a in range(blocks):
                 codes, scale = w3_q[first + a]
                 nc.tensor.matmul_mx(
@@ -232,81 +185,103 @@ def tile_picked_tourney_none_p_kernel(
                 nc.scalar.copy(result[:], bank[:])
                 nc.sync.dma_start(rows, result[:])
 
-        rest = staged.tile([P, 2, P, PACK], BF16, name="w1_rest", offset=0, align_bytes=64)
-        interleave(nc.scalar.copy, rest[:, 0], w1_raw[:], 2)
-        s0 = project(w1_q[0], "s0", on_scalar + on_scalar, range(0, S + 1, BANK // 2))
-        interleave(nc.vector.tensor_copy, rest[:, 1], w1_raw[:], 3)
-        w1_q.append(quantize(second[:], "w1_1"))
-        w1_q.extend(split(quantize(rest[:].rearrange("p t c j -> p (t c) j"), "w1_23")))
+        on_scalar, on_vector = nc.scalar.copy, nc.vector.tensor_copy
 
-        def w2_round(grouped, raw, t):
-            gpsimd_round(
-                grouped.rearrange("p (b r) j -> p b r j", r=8),
-                raw.rearrange("p j (b t r) -> p t b r j", t=PACK, r=8)[:, t],
+        s0 = keep.tile([P, S], F32, name="s0", align_bytes=64)
+        s1 = keep.tile([P, S], F32, name="s1", align_bytes=64)
+        for u in range(2):
+            gather_words(u * QUARTER, (u + 1) * QUARTER)
+            project(on_scalar, s0, w1_q[0], u * QUARTER, (u + 1) * QUARTER, 2 * u)
+            project(on_scalar, s1, w1_q[1], u * QUARTER, (u + 1) * QUARTER, 2 * u + 1)
+        for u in range(2, 4):
+            gather_words(u * QUARTER, (u + 1) * QUARTER)
+            project(on_scalar, s0, w1_q[0], u * QUARTER, (u + 1) * QUARTER, u + 2)
+        right_scores(s0, 0)
+
+        w2_low = keep.tile([P, 2, P, PACK], BF16, name="w2_low", align_bytes=64)
+        w2_high = keep.tile([P, 2, P, PACK], BF16, name="w2_high", align_bytes=64)
+        interleave(on_vector, w2_low[:, 0], w2_raw[:], 0)
+        interleave(on_vector, w2_low[:, 1], w2_raw[:], 1)
+        w2_q = [quantize(w2_low[:, 0], "w2_0", tag="diff")]
+        interleave(on_vector, w2_high[:, 0], w2_raw[:], 2)
+        w2_q.append(quantize(w2_low[:, 1], "w2_1"))
+        interleave(on_vector, w2_high[:, 1], w2_raw[:], 3)
+
+        v0 = placed.tile([P, S], F32, name="v0", offset=ROW_BYTES // 2, align_bytes=64)
+        v1 = keep.tile([P, S], F32, name="v1", align_bytes=64)
+        project(on_vector, v0, w2_q[0], 0, BANK, 7)
+        w2_q.extend(split(quantize(w2_high[:].rearrange("p t c j -> p (t c) j"), "w2_high")))
+        project(on_scalar, s1, w1_q[1], BANK, S, 7)
+        right_scores(s1, 1)
+        project(on_vector, v0, w2_q[0], BANK, S, 0)
+        project(on_vector, v1, w2_q[1], 0, BANK, 1)
+        project(on_vector, v1, w2_q[1], BANK, S, 2)
+        diff = keep.tile([P, PACK, V], F32, name="diff", align_bytes=64)
+        difference(s0, 0)
+        right_values(v0, 0)
+        difference(s1, 1)
+        right_values(v1, 1)
+        value_spread(v0, 0)
+        gates(0, 0, V)
+        value_spread(v1, 1)
+        nc.gpsimd.tensor_tensor(step[:, :2, :], spread[:, :2, :], gate[:, :2, :], ALU.mult)
+
+        s2 = placed.tile([P, S], F32, name="s2", offset=0, align_bytes=64)
+        s3 = placed.tile([P, S], F32, name="s3", offset=ROW_BYTES, align_bytes=64)
+        v2 = keep.tile([P, S], F32, name="v2", tag="s1", align_bytes=64)
+        v3 = keep.tile([P, S], F32, name="v3", align_bytes=64)
+        project(on_vector, s2, w1_q[2], 0, BANK, 7)
+        project(on_vector, s2, w1_q[2], BANK, S, 0)
+        project(on_vector, s3, w1_q[3], 0, BANK, 1)
+        project(on_vector, s3, w1_q[3], BANK, S, 2)
+        project(on_scalar, v2, w2_q[2], 0, BANK, 3)
+        project(on_scalar, v2, w2_q[2], BANK, S, 4)
+        project(on_scalar, v3, w2_q[3], 0, BANK, 3)
+        right_scores(s2, 2)
+        difference(s2, 2)
+        right_scores(s3, 3)
+        difference(s3, 3)
+        project(on_scalar, v3, w2_q[3], BANK, S, 2)
+
+        def round_w3(lo, hi, name):
+            grouped = placed.tile(
+                [P, hi - lo, PACK], BF16, name=name, offset=ROW_BYTES + lo * PACK * 2, align_bytes=64
             )
+            nc.scalar.copy(
+                grouped[:].rearrange("p (c i) t -> p c t i", i=2),
+                w3_raw[:, :, lo:hi].rearrange("p t (c i) -> p c t i", i=2),
+            )
+            return grouped[:]
 
-        w2_early = keep.tile([P, 2, P, PACK], BF16, name="w2_early", align_bytes=64)
-        interleave(nc.scalar.copy, w2_early[:, 0], w2_raw[:], 0)
-        shared = keep.tile([P, V * 2 + (P - GPSIMD_SHARE) * PACK], BF16, name="shared", align_bytes=64)
-        w2_late = shared[:, V * 2 - (P + GPSIMD_SHARE) * PACK :].rearrange("p (u c j) -> p u c j", u=2, j=PACK)
-        w2_round(w2_late[:, 1, GPSIMD_SHARE:], w2_raw[:, :, GPSIMD_SHARE * PACK :], 2)
-        w2_round(w2_early[:, 1], w2_raw[:], 1)
-
-        r0 = right_scores(s0, 0, nc.vector.tensor_copy, V // 2)
-        s1 = project(w1_q[1], "s1", on_scalar)
-        difference(s0, r0, 0, V // 2)
-        w2_q = split(quantize(w2_early[:].rearrange("p t c j -> p (t c) j"), "w2_01", tag="s_right0"))
-        r1 = right_scores(s1, 1, scalar_gather)
-        s2 = project(w1_q[2], "s2", on_scalar)
-        difference(s1, r1, 1)
-        both_gates(0)
-        w2_round(w2_late[:, 1, :GPSIMD_SHARE], w2_raw[:, :, : GPSIMD_SHARE * PACK], 2)
-        v0 = project(w2_q[0], "s1", on_vector)
-        interleave(nc.vector.tensor_copy, w2_late[:, 0], w2_raw[:], 3)
-        r2 = right_scores(s2, 2, scalar_gather)
-        w2_q.extend(reversed(split(quantize(w2_late.rearrange("p t c j -> p (t c) j"), "w2_32"))))
-        weigh(v0, 0)
-        v1 = project(w2_q[1], "val1", on_scalar)
-        both_gates(1)
-        difference(s2, r2, 2)
-        s3 = project(w1_q[3], "s3", on_scalar)
-        weigh(v1, 1)
-        r3 = right_scores(s3, 3, scalar_gather)
-        v2 = project(w2_q[2], "val2", on_scalar)
-        difference(s3, r3, 3)
-        v3 = project(w2_q[3], "val3", on_scalar)
         right_values(v2, 2, 0, EARLY)
         right_values(v3, 3, 0, EARLY)
-        late_gates(0, EARLY)
+        gates(2, 0, EARLY)
         value_spread(v2, 2, 0, EARLY)
         value_spread(v3, 3, 0, EARLY)
         right_values(v2, 2, EARLY, V)
         for t in (2, 3):
-            late_steps(0, EARLY, t)
+            late_step(0, EARLY, t)
         value_spread(v2, 2, EARLY, V)
         z_early = blend(0, EARLY)
-        w3_low = keep.tile([P, N // 2, PACK], BF16, name="w3_low", align_bytes=64)
-        nc.scalar.copy(*w3_views(w3_low[:], 0, N // 2))
-        w3_q = split(quantize(w3_low[:], "w3_low"))
+        w3_q = split(quantize(round_w3(0, N // 2, "w3_low"), "w3_low"))
         early_q = quantize(z_early, "z_early")
         right_values(v3, 3, EARLY, V)
         value_spread(v3, 3, EARLY, V)
-        late_gates(EARLY, V)
-        w3_high = keep.tile([P, N // 2, PACK], BF16, name="w3_high", align_bytes=64)
-        nc.scalar.copy(*w3_views(w3_high[:], N // 2, N))
+        gates(2, EARLY, V)
+        w3_high = round_w3(N // 2, N, "w3_high")
         for a in range(2):
-            finish(early_q, 0, EARLY, a, 1)
+            finish(early_q, 0, EARLY, a, 1, a)
         for t in (2, 3):
-            late_steps(EARLY, LAST, t)
-        w3_q.extend(split(quantize(w3_high[:], "w3_high")))
+            late_step(EARLY, LAST, t)
+        w3_q.extend(split(quantize(w3_high, "w3_high")))
         for a in range(2, PACK):
-            finish(early_q, 0, EARLY, a, 1)
+            finish(early_q, 0, EARLY, a, 1, a)
         z_middle = blend(EARLY, LAST)
         for t in (2, 3):
-            late_steps(LAST, V, t)
+            late_step(LAST, V, t)
         middle_q = quantize(z_middle, "z_middle")
         for first in range(0, PACK, 2):
-            finish(middle_q, EARLY, LAST, first, 2)
+            finish(middle_q, EARLY, LAST, first, 2, 4 + first // 2)
         last_q = quantize(blend(LAST, V), "z_last")
         for first in range(0, PACK, 2):
-            finish(last_q, LAST, V, first, 2)
+            finish(last_q, LAST, V, first, 2, 6 + first // 2)

@@ -20,6 +20,8 @@ P = 128
 PACK = 4
 BANK = 512
 QUARTER = 256
+GPSIMD_SHARE = 32
+GPSIMD_STEPS = 896
 EARLY = 256
 LAST = 384
 ROW_BYTES = S * 4
@@ -71,6 +73,16 @@ def tile_picked_tourney_none_p_kernel(
             copy(
                 grouped.rearrange("p (b h i) j -> p b h j i", h=4, i=2),
                 raw.rearrange("p j (b t h i) -> p t b h j i", t=PACK, h=4, i=2)[:, t],
+            )
+
+        def gpsimd_interleave(grouped, raw, t):
+            nc.gpsimd.tensor_scalar(
+                grouped.rearrange("p (b r) j -> p b r j", r=8),
+                raw.rearrange("p j (b t r) -> p t b r j", t=PACK, r=8)[:, t],
+                1.0,
+                0.0,
+                ALU.mult,
+                ALU.add,
             )
 
         def quantize(grouped, name, tag=None):
@@ -189,59 +201,64 @@ def tile_picked_tourney_none_p_kernel(
 
         s0 = keep.tile([P, S], F32, name="s0", align_bytes=64)
         s1 = keep.tile([P, S], F32, name="s1", align_bytes=64)
-        for u in range(2):
+        for u in range(3):
             gather_words(u * QUARTER, (u + 1) * QUARTER)
             project(on_scalar, s0, w1_q[0], u * QUARTER, (u + 1) * QUARTER, 2 * u)
             project(on_scalar, s1, w1_q[1], u * QUARTER, (u + 1) * QUARTER, 2 * u + 1)
-        for u in range(2, 4):
-            gather_words(u * QUARTER, (u + 1) * QUARTER)
-            project(on_scalar, s0, w1_q[0], u * QUARTER, (u + 1) * QUARTER, u + 2)
+        gather_words(S - QUARTER, S)
+        project(on_scalar, s0, w1_q[0], S - QUARTER, S, 6)
         right_scores(s0, 0)
 
-        w2_low = keep.tile([P, 2, P, PACK], BF16, name="w2_low", align_bytes=64)
-        w2_high = keep.tile([P, 2, P, PACK], BF16, name="w2_high", align_bytes=64)
-        interleave(on_vector, w2_low[:, 0], w2_raw[:], 0)
-        interleave(on_vector, w2_low[:, 1], w2_raw[:], 1)
-        w2_q = [quantize(w2_low[:, 0], "w2_0", tag="diff")]
-        interleave(on_vector, w2_high[:, 0], w2_raw[:], 2)
-        w2_q.append(quantize(w2_low[:, 1], "w2_1"))
-        interleave(on_vector, w2_high[:, 1], w2_raw[:], 3)
+        tile_width = P * PACK
+        w2_rounded = keep.tile([P, 2 * tile_width], BF16, name="w2_rounded", align_bytes=64)
+        w2_first = s1[:, S - QUARTER :].bitcast(BF16).rearrange("p (c j) -> p c j", j=PACK)
+        w2_second = w2_rounded[:, GPSIMD_SHARE * PACK : GPSIMD_SHARE * PACK + tile_width].rearrange("p (c j) -> p c j", j=PACK)
+        w2_high = w2_rounded[:].rearrange("p (t c j) -> p t c j", t=2, j=PACK)
+        interleave(on_vector, w2_first, w2_raw[:], 0)
+        interleave(on_vector, w2_second, w2_raw[:], 1)
+        w2_q = [quantize(w2_first, "w2_0", tag="diff")]
+        interleave(on_vector, w2_high[:, 1, GPSIMD_SHARE:], w2_raw[:, :, GPSIMD_SHARE * PACK :], 3)
+        w2_q.append(quantize(w2_second, "w2_1"))
+        gpsimd_interleave(w2_high[:, 0], w2_raw[:], 2)
+        gpsimd_interleave(w2_high[:, 1, :GPSIMD_SHARE], w2_raw[:, :, : GPSIMD_SHARE * PACK], 3)
 
         v0 = placed.tile([P, S], F32, name="v0", offset=ROW_BYTES // 2, align_bytes=64)
         v1 = keep.tile([P, S], F32, name="v1", align_bytes=64)
-        project(on_vector, v0, w2_q[0], 0, BANK, 7)
-        w2_q.extend(split(quantize(w2_high[:].rearrange("p t c j -> p (t c) j"), "w2_high")))
-        project(on_scalar, s1, w1_q[1], BANK, S, 7)
+        project(on_vector, s1, w1_q[1], S - QUARTER, S, 7)
         right_scores(s1, 1)
-        project(on_vector, v0, w2_q[0], BANK, S, 0)
-        project(on_vector, v1, w2_q[1], 0, BANK, 1)
-        project(on_vector, v1, w2_q[1], BANK, S, 2)
+        project(on_vector, v0, w2_q[0], 0, BANK, 0)
+        project(on_vector, v0, w2_q[0], BANK, S, 1)
+        project(on_vector, v1, w2_q[1], 0, BANK, 2)
         diff = keep.tile([P, PACK, V], F32, name="diff", align_bytes=64)
         difference(s0, 0)
         right_values(v0, 0)
+        project(on_scalar, v1, w2_q[1], BANK, S, 3)
+        w2_q.extend(split(quantize(w2_high.rearrange("p t c j -> p (t c) j"), "w2_high")))
         difference(s1, 1)
         right_values(v1, 1)
         value_spread(v0, 0)
         gates(0, 0, V)
         value_spread(v1, 1)
-        nc.gpsimd.tensor_tensor(step[:, :2, :], spread[:, :2, :], gate[:, :2, :], ALU.mult)
+        flat = [rows[:].rearrange("p t v -> p (t v)")[:, :GPSIMD_STEPS] for rows in (step, spread, gate)]
+        nc.gpsimd.tensor_tensor(*flat, ALU.mult)
 
         s2 = placed.tile([P, S], F32, name="s2", offset=0, align_bytes=64)
         s3 = placed.tile([P, S], F32, name="s3", offset=ROW_BYTES, align_bytes=64)
         v2 = keep.tile([P, S], F32, name="v2", tag="s1", align_bytes=64)
-        v3 = keep.tile([P, S], F32, name="v3", align_bytes=64)
-        project(on_vector, s2, w1_q[2], 0, BANK, 7)
-        project(on_vector, s2, w1_q[2], BANK, S, 0)
-        project(on_vector, s3, w1_q[3], 0, BANK, 1)
-        project(on_vector, s3, w1_q[3], BANK, S, 2)
-        project(on_scalar, v2, w2_q[2], 0, BANK, 3)
-        project(on_scalar, v2, w2_q[2], BANK, S, 4)
-        project(on_scalar, v3, w2_q[3], 0, BANK, 3)
+        v3 = keep.tile([P, S], F32, name="v3", tag="v1", align_bytes=64)
+        project(on_vector, s2, w1_q[2], 0, BANK, 0)
+        project(on_vector, s2, w1_q[2], BANK, S, 1)
+        project(on_vector, s3, w1_q[3], 0, BANK, 2)
+        project(on_vector, s3, w1_q[3], BANK, S, 3)
+        project(on_scalar, v2, w2_q[2], 0, BANK, 4)
+        project(on_scalar, v2, w2_q[2], BANK, S, 5)
+        project(on_scalar, v3, w2_q[3], 0, BANK, 6)
+        late_step(GPSIMD_STEPS - V, V, 1)
         right_scores(s2, 2)
         difference(s2, 2)
         right_scores(s3, 3)
         difference(s3, 3)
-        project(on_scalar, v3, w2_q[3], BANK, S, 2)
+        project(on_scalar, v3, w2_q[3], BANK, S, 3)
 
         def round_w3(lo, hi, name):
             grouped = placed.tile(

@@ -20,8 +20,7 @@ P = 128
 PACK = 4
 BANK = 512
 QUARTER = 256
-GPSIMD_SHARE = 32
-GPSIMD_STEPS = 896
+GPSIMD_STEPS = 768
 EARLY = 256
 LAST = 384
 ROW_BYTES = S * 4
@@ -99,13 +98,13 @@ def tile_picked_tourney_none_p_kernel(
             return [(codes[:, u * P : (u + 1) * P], scale[:, u * P : (u + 1) * P]) for u in range(codes.shape[1] // P)]
 
         w1_low = keep.tile([P, 2, P, PACK], BF16, name="w1_low", align_bytes=64)
-        w1_high = keep.tile([P, 2, P, PACK], BF16, name="w1_high", align_bytes=64)
+        rounded = keep.tile([P, 3, P, PACK], BF16, name="rounded", align_bytes=64)
+        w1_high, w2_high = rounded[:, :2], rounded[:, 1:]
         interleave(nc.scalar.copy, w1_low[:, 0], w1_raw[:], 0)
         interleave(nc.scalar.copy, w1_low[:, 1], w1_raw[:], 1)
         interleave(nc.scalar.copy, w1_high[:, 0], w1_raw[:], 2)
         interleave(nc.vector.tensor_copy, w1_high[:, 1], w1_raw[:], 3)
         w1_q = split(quantize(w1_low[:].rearrange("p t c j -> p (t c) j"), "w1_low"))
-        w1_q.extend(split(quantize(w1_high[:].rearrange("p t c j -> p (t c) j"), "w1_high")))
 
         x_codes = keep.tile([P, S], U32, name="x_codes", align_bytes=64)
         word_window = word_table[:].bitcast(U32)
@@ -171,9 +170,9 @@ def tile_picked_tourney_none_p_kernel(
 
         out_rows = out.rearrange("(a p) v -> p a v", p=P)
 
-        def finish(z_q, lo, hi, first, blocks, bank_number):
+        def final_products(z_q, first, blocks, bank_number):
             z_codes, z_scale = z_q
-            bank = psum.tile([P, blocks, hi - lo], F32, name="bank%d" % bank_number)
+            bank = psum.tile([P, blocks, z_codes.shape[1]], F32, name="bank%d" % bank_number)
             for a in range(blocks):
                 codes, scale = w3_q[first + a]
                 nc.tensor.matmul_mx(
@@ -185,17 +184,13 @@ def tile_picked_tourney_none_p_kernel(
                     start=True,
                     stop=True,
                 )
-            result = keep.tile([P, blocks, hi - lo], F32, name="result%d_%d" % (lo, first))
-            rows = out_rows[:, first : first + blocks, lo:hi]
-            if hi == V and first > 0:
-                nc.vector.tensor_copy(result[:], bank[:])
-                nc.sync.dma_start(rows, result[:])
-            elif hi == V:
-                nc.scalar.copy(result[:], bank[:])
-                nc.scalar.dma_start(rows, result[:])
-            else:
-                nc.scalar.copy(result[:], bank[:])
-                nc.sync.dma_start(rows, result[:])
+            return bank
+
+        def store(copy, queue, bank, lo, first):
+            blocks, width = bank.shape[1:]
+            result = keep.tile([P, blocks, width], F32, name="result%d_%d" % (lo, first))
+            copy(result[:], bank[:])
+            queue.dma_start(out_rows[:, first : first + blocks, lo : lo + width], result[:])
 
         on_scalar, on_vector = nc.scalar.copy, nc.vector.tensor_copy
 
@@ -209,18 +204,15 @@ def tile_picked_tourney_none_p_kernel(
         project(on_scalar, s0, w1_q[0], S - QUARTER, S, 6)
         right_scores(s0, 0)
 
-        tile_width = P * PACK
-        w2_rounded = keep.tile([P, 2 * tile_width], BF16, name="w2_rounded", align_bytes=64)
+        w2_second = keep.tile([P, P, PACK], BF16, name="w2_second", align_bytes=64)
         w2_first = s1[:, S - QUARTER :].bitcast(BF16).rearrange("p (c j) -> p c j", j=PACK)
-        w2_second = w2_rounded[:, GPSIMD_SHARE * PACK : GPSIMD_SHARE * PACK + tile_width].rearrange("p (c j) -> p c j", j=PACK)
-        w2_high = w2_rounded[:].rearrange("p (t c j) -> p t c j", t=2, j=PACK)
         interleave(on_vector, w2_first, w2_raw[:], 0)
-        interleave(on_vector, w2_second, w2_raw[:], 1)
+        interleave(on_vector, w2_second[:], w2_raw[:], 1)
         w2_q = [quantize(w2_first, "w2_0", tag="diff")]
-        interleave(on_vector, w2_high[:, 1, GPSIMD_SHARE:], w2_raw[:, :, GPSIMD_SHARE * PACK :], 3)
-        w2_q.append(quantize(w2_second, "w2_1"))
+        interleave(on_vector, w2_high[:, 1], w2_raw[:], 3)
+        w2_q.append(quantize(w2_second[:], "w2_1"))
+        w1_q.extend(split(quantize(w1_high.rearrange("p t c j -> p (t c) j"), "w1_high", tag="w2_second")))
         gpsimd_interleave(w2_high[:, 0], w2_raw[:], 2)
-        gpsimd_interleave(w2_high[:, 1, :GPSIMD_SHARE], w2_raw[:, :, : GPSIMD_SHARE * PACK], 3)
 
         v0 = placed.tile([P, S], F32, name="v0", offset=ROW_BYTES // 2, align_bytes=64)
         v1 = keep.tile([P, S], F32, name="v1", align_bytes=64)
@@ -287,18 +279,19 @@ def tile_picked_tourney_none_p_kernel(
         gates(2, EARLY, V)
         w3_high = round_w3(N // 2, N, "w3_high")
         for a in range(2):
-            finish(early_q, 0, EARLY, a, 1, a)
+            store(on_scalar, nc.sync, final_products(early_q, a, 1, a), 0, a)
         for t in (2, 3):
             late_step(EARLY, LAST, t)
         w3_q.extend(split(quantize(w3_high, "w3_high")))
         for a in range(2, PACK):
-            finish(early_q, 0, EARLY, a, 1, a)
+            store(on_scalar, nc.sync, final_products(early_q, a, 1, a), 0, a)
         z_middle = blend(EARLY, LAST)
         for t in (2, 3):
             late_step(LAST, V, t)
         middle_q = quantize(z_middle, "z_middle")
-        for first in range(0, PACK, 2):
-            finish(middle_q, EARLY, LAST, first, 2, 4 + first // 2)
+        store(on_scalar, nc.sync, final_products(middle_q, 0, 2, 4), EARLY, 0)
+        middle_bank = final_products(middle_q, 2, 2, 5)
         last_q = quantize(blend(LAST, V), "z_last")
-        for first in range(0, PACK, 2):
-            finish(last_q, LAST, V, first, 2, 6 + first // 2)
+        store(on_vector, nc.sync, middle_bank, EARLY, 2)
+        store(on_scalar, nc.scalar, final_products(last_q, 0, 2, 6), LAST, 0)
+        store(on_vector, nc.sync, final_products(last_q, 2, 2, 7), LAST, 2)

@@ -20,7 +20,7 @@ P = 128
 PACK = 4
 BANK = 512
 QUARTER = 256
-GPSIMD_STEPS = 768
+GPSIMD_SHARE = 32
 EARLY = 256
 LAST = 384
 ROW_BYTES = S * 4
@@ -98,8 +98,11 @@ def tile_picked_tourney_none_p_kernel(
             return [(codes[:, u * P : (u + 1) * P], scale[:, u * P : (u + 1) * P]) for u in range(codes.shape[1] // P)]
 
         w1_low = keep.tile([P, 2, P, PACK], BF16, name="w1_low", align_bytes=64)
-        rounded = keep.tile([P, 3, P, PACK], BF16, name="rounded", align_bytes=64)
-        w1_high, w2_high = rounded[:, :2], rounded[:, 1:]
+        tile_width = P * PACK
+        vector_share = (P - GPSIMD_SHARE) * PACK
+        rounded = keep.tile([P, 2 * tile_width + vector_share], BF16, name="rounded", align_bytes=64)
+        w1_high = rounded[:, : 2 * tile_width].rearrange("p (t c j) -> p t c j", t=2, j=PACK)
+        w2_high = rounded[:, vector_share:].rearrange("p (t c j) -> p t c j", t=2, j=PACK)
         interleave(nc.scalar.copy, w1_low[:, 0], w1_raw[:], 0)
         interleave(nc.scalar.copy, w1_low[:, 1], w1_raw[:], 1)
         interleave(nc.scalar.copy, w1_high[:, 0], w1_raw[:], 2)
@@ -209,10 +212,11 @@ def tile_picked_tourney_none_p_kernel(
         interleave(on_vector, w2_first, w2_raw[:], 0)
         interleave(on_vector, w2_second[:], w2_raw[:], 1)
         w2_q = [quantize(w2_first, "w2_0", tag="diff")]
-        interleave(on_vector, w2_high[:, 1], w2_raw[:], 3)
         w2_q.append(quantize(w2_second[:], "w2_1"))
+        interleave(on_vector, w2_high[:, 1, GPSIMD_SHARE:], w2_raw[:, :, GPSIMD_SHARE * PACK :], 3)
         w1_q.extend(split(quantize(w1_high.rearrange("p t c j -> p (t c) j"), "w1_high", tag="w2_second")))
         gpsimd_interleave(w2_high[:, 0], w2_raw[:], 2)
+        gpsimd_interleave(w2_high[:, 1, :GPSIMD_SHARE], w2_raw[:, :, : GPSIMD_SHARE * PACK], 3)
 
         v0 = placed.tile([P, S], F32, name="v0", offset=ROW_BYTES // 2, align_bytes=64)
         v1 = keep.tile([P, S], F32, name="v1", align_bytes=64)
@@ -220,10 +224,10 @@ def tile_picked_tourney_none_p_kernel(
         right_scores(s1, 1)
         project(on_vector, v0, w2_q[0], 0, BANK, 0)
         project(on_vector, v0, w2_q[0], BANK, S, 1)
-        project(on_vector, v1, w2_q[1], 0, BANK, 2)
         diff = keep.tile([P, PACK, V], F32, name="diff", align_bytes=64)
         difference(s0, 0)
         right_values(v0, 0)
+        project(on_scalar, v1, w2_q[1], 0, BANK, 2)
         project(on_scalar, v1, w2_q[1], BANK, S, 3)
         w2_q.extend(split(quantize(w2_high.rearrange("p t c j -> p (t c) j"), "w2_high")))
         difference(s1, 1)
@@ -231,8 +235,7 @@ def tile_picked_tourney_none_p_kernel(
         value_spread(v0, 0)
         gates(0, 0, V)
         value_spread(v1, 1)
-        flat = [rows[:].rearrange("p t v -> p (t v)")[:, :GPSIMD_STEPS] for rows in (step, spread, gate)]
-        nc.gpsimd.tensor_tensor(*flat, ALU.mult)
+        nc.gpsimd.tensor_tensor(step[:, :2, :], spread[:, :2, :], gate[:, :2, :], ALU.mult)
 
         s2 = placed.tile([P, S], F32, name="s2", offset=0, align_bytes=64)
         s3 = placed.tile([P, S], F32, name="s3", offset=ROW_BYTES, align_bytes=64)
@@ -245,7 +248,6 @@ def tile_picked_tourney_none_p_kernel(
         project(on_scalar, v2, w2_q[2], 0, BANK, 4)
         project(on_scalar, v2, w2_q[2], BANK, S, 5)
         project(on_scalar, v3, w2_q[3], 0, BANK, 6)
-        late_step(GPSIMD_STEPS - V, V, 1)
         right_scores(s2, 2)
         difference(s2, 2)
         right_scores(s3, 3)

@@ -106,7 +106,7 @@ def tile_picked_tourney_none_p_kernel(
         interleave(nc.scalar.copy, w1_low[:, 0], w1_raw[:], 0)
         interleave(nc.scalar.copy, w1_low[:, 1], w1_raw[:], 1)
         interleave(nc.scalar.copy, w1_high[:, 0], w1_raw[:], 2)
-        interleave(nc.vector.tensor_copy, w1_high[:, 1], w1_raw[:], 3)
+        interleave(nc.scalar.copy, w1_high[:, 1], w1_raw[:], 3)
         w1_q = split(quantize(w1_low[:].rearrange("p t c j -> p (t c) j"), "w1_low"))
 
         x_codes = keep.tile([P, S], U32, name="x_codes", align_bytes=64)
@@ -136,16 +136,20 @@ def tile_picked_tourney_none_p_kernel(
             return rows[:].indirect(offsets[:, lo // 16 : hi // 16])
 
         gate = keep.tile([P, PACK, V], F32, name="gate")
-        s_right = keep.tile([P, PACK, V], F32, name="s_right")
+        reused = keep.tile([P, 3 * 2 * V], BF16, name="reused", align_bytes=64)
+        s_right_1 = keep.tile([P, V], F32, name="s_right_1")
+        s_right = [reused[:, u * 2 * V : (u + 1) * 2 * V].bitcast(F32) for u in range(3)]
+        s_right = [s_right[0], s_right_1[:], s_right[2], s_right[1]]
+        w3_rounded = reused[:, V : V + N * PACK].rearrange("p (c t) -> p c t", t=PACK)
         spread = keep.tile([P, PACK, V], F32, name="spread")
         base = keep.tile([P, PACK, V], F32, name="base")
         step = keep.tile([P, PACK, V], F32, name="step")
 
         def right_scores(rows, t):
-            nc.scalar.activation(s_right[:, t, :], picked(rows, right_sb), COPY)
+            nc.scalar.activation(s_right[t], picked(rows, right_sb), COPY)
 
         def difference(rows, t):
-            nc.vector.tensor_tensor(diff[:, t, :], picked(rows, left_sb), s_right[:, t, :], ALU.subtract)
+            nc.vector.tensor_tensor(diff[:, t, :], picked(rows, left_sb), s_right[t], ALU.subtract)
 
         def right_values(rows, t, lo=0, hi=V):
             nc.scalar.activation(base[:, t, lo:hi], picked(rows, right_sb, lo, hi), COPY)
@@ -195,6 +199,12 @@ def tile_picked_tourney_none_p_kernel(
             copy(result[:], bank[:])
             queue.dma_start(out_rows[:, first : first + blocks, lo : lo + width], result[:])
 
+        def round_w3(copy, lo, hi):
+            copy(
+                w3_rounded[:, lo:hi].rearrange("p (c i) t -> p c t i", i=2),
+                w3_raw[:, :, lo:hi].rearrange("p t (c i) -> p c t i", i=2),
+            )
+
         on_scalar, on_vector = nc.scalar.copy, nc.vector.tensor_copy
 
         s0 = keep.tile([P, S], F32, name="s0", align_bytes=64)
@@ -224,12 +234,13 @@ def tile_picked_tourney_none_p_kernel(
         right_scores(s1, 1)
         project(on_vector, v0, w2_q[0], 0, BANK, 0)
         project(on_vector, v0, w2_q[0], BANK, S, 1)
+        project(on_vector, v1, w2_q[1], 0, BANK, 2)
         diff = keep.tile([P, PACK, V], F32, name="diff", align_bytes=64)
         difference(s0, 0)
         right_values(v0, 0)
-        project(on_scalar, v1, w2_q[1], 0, BANK, 2)
         project(on_scalar, v1, w2_q[1], BANK, S, 3)
         w2_q.extend(split(quantize(w2_high.rearrange("p t c j -> p (t c) j"), "w2_high")))
+        round_w3(on_vector, 0, P)
         difference(s1, 1)
         right_values(v1, 1)
         value_spread(v0, 0)
@@ -254,16 +265,6 @@ def tile_picked_tourney_none_p_kernel(
         difference(s3, 3)
         project(on_scalar, v3, w2_q[3], BANK, S, 3)
 
-        def round_w3(lo, hi, name):
-            grouped = placed.tile(
-                [P, hi - lo, PACK], BF16, name=name, offset=ROW_BYTES + lo * PACK * 2, align_bytes=64
-            )
-            nc.scalar.copy(
-                grouped[:].rearrange("p (c i) t -> p c t i", i=2),
-                w3_raw[:, :, lo:hi].rearrange("p t (c i) -> p c t i", i=2),
-            )
-            return grouped[:]
-
         right_values(v2, 2, 0, EARLY)
         right_values(v3, 3, 0, EARLY)
         gates(2, 0, EARLY)
@@ -274,18 +275,19 @@ def tile_picked_tourney_none_p_kernel(
             late_step(0, EARLY, t)
         value_spread(v2, 2, EARLY, V)
         z_early = blend(0, EARLY)
-        w3_q = split(quantize(round_w3(0, N // 2, "w3_low"), "w3_low"))
+        round_w3(on_scalar, N // 2, N)
+        w3_q = [None, None] + split(quantize(w3_rounded[:, N // 2 :], "w3_high"))
         early_q = quantize(z_early, "z_early")
         right_values(v3, 3, EARLY, V)
         value_spread(v3, 3, EARLY, V)
         gates(2, EARLY, V)
-        w3_high = round_w3(N // 2, N, "w3_high")
-        for a in range(2):
+        round_w3(on_scalar, P, N // 2)
+        for a in range(2, PACK):
             store(on_scalar, nc.sync, final_products(early_q, a, 1, a), 0, a)
         for t in (2, 3):
             late_step(EARLY, LAST, t)
-        w3_q.extend(split(quantize(w3_high, "w3_high")))
-        for a in range(2, PACK):
+        w3_q[:2] = split(quantize(w3_rounded[:, : N // 2], "w3_low"))
+        for a in range(2):
             store(on_scalar, nc.sync, final_products(early_q, a, 1, a), 0, a)
         z_middle = blend(EARLY, LAST)
         for t in (2, 3):

@@ -21,6 +21,7 @@ PACK = 4
 BANK = 512
 QUARTER = 256
 GPSIMD_SHARE = 32
+GPSIMD_STEPS = 256
 EARLY = 256
 LAST = 384
 ROW_BYTES = S * 4
@@ -159,8 +160,8 @@ def tile_picked_tourney_none_p_kernel(
                 spread[:, t, lo:hi], picked(rows, left_sb, lo, hi), base[:, t, lo:hi], ALU.subtract
             )
 
-        def gates(first, lo, hi):
-            nc.scalar.activation(gate[:, first : first + 2, lo:hi], diff[:, first : first + 2, lo:hi], SIGMOID)
+        def gates(first, tiles, lo, hi):
+            nc.scalar.activation(gate[:, first : first + tiles, lo:hi], diff[:, first : first + tiles, lo:hi], SIGMOID)
 
         def late_step(lo, hi, t):
             nc.vector.tensor_tensor(step[:, t, lo:hi], spread[:, t, lo:hi], gate[:, t, lo:hi], ALU.mult)
@@ -219,55 +220,57 @@ def tile_picked_tourney_none_p_kernel(
 
         w2_second = keep.tile([P, P, PACK], BF16, name="w2_second", align_bytes=64)
         w2_first = s1[:, S - QUARTER :].bitcast(BF16).rearrange("p (c j) -> p c j", j=PACK)
-        interleave(on_vector, w2_first, w2_raw[:], 0)
-        interleave(on_vector, w2_second[:], w2_raw[:], 1)
-        w2_q = [quantize(w2_first, "w2_0", tag="diff")]
-        w2_q.append(quantize(w2_second[:], "w2_1"))
+        interleave(on_vector, w2_first, w2_raw[:], 1)
+        interleave(on_vector, w2_second[:], w2_raw[:], 0)
+        w2_q = [None, quantize(w2_first, "w2_1", tag="diff")]
+        w2_q[0] = quantize(w2_second[:], "w2_0")
         interleave(on_vector, w2_high[:, 1, GPSIMD_SHARE:], w2_raw[:, :, GPSIMD_SHARE * PACK :], 3)
         w1_q.extend(split(quantize(w1_high.rearrange("p t c j -> p (t c) j"), "w1_high", tag="w2_second")))
         gpsimd_interleave(w2_high[:, 0], w2_raw[:], 2)
         gpsimd_interleave(w2_high[:, 1, :GPSIMD_SHARE], w2_raw[:, :, : GPSIMD_SHARE * PACK], 3)
 
-        v0 = placed.tile([P, S], F32, name="v0", offset=ROW_BYTES // 2, align_bytes=64)
-        v1 = keep.tile([P, S], F32, name="v1", align_bytes=64)
+        v1 = placed.tile([P, S], F32, name="v1", offset=ROW_BYTES // 2, align_bytes=64)
+        v0 = keep.tile([P, S], F32, name="v0", align_bytes=64)
         project(on_vector, s1, w1_q[1], S - QUARTER, S, 7)
         right_scores(s1, 1)
-        project(on_vector, v0, w2_q[0], 0, BANK, 0)
-        project(on_vector, v0, w2_q[0], BANK, S, 1)
-        project(on_vector, v1, w2_q[1], 0, BANK, 2)
+        project(on_vector, v1, w2_q[1], 0, BANK, 0)
+        project(on_vector, v1, w2_q[1], BANK, S, 1)
+        project(on_vector, v0, w2_q[0], 0, BANK, 2)
         diff = keep.tile([P, PACK, V], F32, name="diff", align_bytes=64)
         difference(s0, 0)
-        right_values(v0, 0)
-        project(on_scalar, v1, w2_q[1], BANK, S, 3)
+        project(on_scalar, v0, w2_q[0], BANK, S, 3)
+        right_values(v1, 1)
         w2_q.extend(split(quantize(w2_high.rearrange("p t c j -> p (t c) j"), "w2_high")))
         round_w3(on_vector, 0, P)
         difference(s1, 1)
-        right_values(v1, 1)
-        value_spread(v0, 0)
-        gates(0, 0, V)
+        right_values(v0, 0)
         value_spread(v1, 1)
-        nc.gpsimd.tensor_tensor(step[:, :2, :], spread[:, :2, :], gate[:, :2, :], ALU.mult)
+        gates(0, 1, 0, V)
+        value_spread(v0, 0)
+        nc.gpsimd.tensor_tensor(step[:, 0, :], spread[:, 0, :], gate[:, 0, :], ALU.mult)
 
-        s2 = placed.tile([P, S], F32, name="s2", offset=0, align_bytes=64)
-        s3 = placed.tile([P, S], F32, name="s3", offset=ROW_BYTES, align_bytes=64)
-        v2 = keep.tile([P, S], F32, name="v2", tag="s1", align_bytes=64)
-        v3 = keep.tile([P, S], F32, name="v3", tag="v1", align_bytes=64)
-        project(on_vector, s2, w1_q[2], 0, BANK, 0)
-        project(on_vector, s2, w1_q[2], BANK, S, 1)
-        project(on_vector, s3, w1_q[3], 0, BANK, 2)
-        project(on_vector, s3, w1_q[3], BANK, S, 3)
-        project(on_scalar, v2, w2_q[2], 0, BANK, 4)
-        project(on_scalar, v2, w2_q[2], BANK, S, 5)
-        project(on_scalar, v3, w2_q[3], 0, BANK, 6)
+        s3 = placed.tile([P, S], F32, name="s3", offset=0, align_bytes=64)
+        v2 = placed.tile([P, S], F32, name="v2", offset=ROW_BYTES, align_bytes=64)
+        s2 = keep.tile([P, S], F32, name="s2", tag="s1", align_bytes=64)
+        v3 = keep.tile([P, S], F32, name="v3", tag="v0", align_bytes=64)
+        project(on_vector, s3, w1_q[3], 0, BANK, 0)
+        project(on_vector, s3, w1_q[3], BANK, S, 1)
+        project(on_scalar, s2, w1_q[2], 0, BANK, 4)
+        project(on_scalar, s2, w1_q[2], BANK, S, 5)
+        gates(1, 1, 0, V)
+        nc.gpsimd.tensor_tensor(step[:, 1, :GPSIMD_STEPS], spread[:, 1, :GPSIMD_STEPS], gate[:, 1, :GPSIMD_STEPS], ALU.mult)
+        project(on_vector, v2, w2_q[2], 0, BANK, 2)
+        project(on_vector, v2, w2_q[2], BANK, S, 3)
+        late_step(GPSIMD_STEPS, V, 1)
         right_scores(s2, 2)
         difference(s2, 2)
         right_scores(s3, 3)
         difference(s3, 3)
-        project(on_scalar, v3, w2_q[3], BANK, S, 3)
-
+        project(on_scalar, v3, w2_q[3], 0, BANK, 6)
+        project(on_scalar, v3, w2_q[3], BANK, S, 7)
         right_values(v2, 2, 0, EARLY)
         right_values(v3, 3, 0, EARLY)
-        gates(2, 0, EARLY)
+        gates(2, 2, 0, EARLY)
         value_spread(v2, 2, 0, EARLY)
         value_spread(v3, 3, 0, EARLY)
         right_values(v2, 2, EARLY, V)
@@ -280,7 +283,7 @@ def tile_picked_tourney_none_p_kernel(
         early_q = quantize(z_early, "z_early")
         right_values(v3, 3, EARLY, V)
         value_spread(v3, 3, EARLY, V)
-        gates(2, EARLY, V)
+        gates(2, 2, EARLY, V)
         round_w3(on_scalar, P, N // 2)
         for a in range(2, PACK):
             store(on_scalar, nc.sync, final_products(early_q, a, 1, a), 0, a)

@@ -20,7 +20,6 @@ P = 128
 PACK = 4
 BANK = 512
 QUARTER = 256
-GPSIMD_SHARE = 32
 GPSIMD_STEPS = 256
 EARLY = 256
 LAST = 384
@@ -99,11 +98,8 @@ def tile_picked_tourney_none_p_kernel(
             return [(codes[:, u * P : (u + 1) * P], scale[:, u * P : (u + 1) * P]) for u in range(codes.shape[1] // P)]
 
         w1_low = keep.tile([P, 2, P, PACK], BF16, name="w1_low", align_bytes=64)
-        tile_width = P * PACK
-        vector_share = (P - GPSIMD_SHARE) * PACK
-        rounded = keep.tile([P, 2 * tile_width + vector_share], BF16, name="rounded", align_bytes=64)
-        w1_high = rounded[:, : 2 * tile_width].rearrange("p (t c j) -> p t c j", t=2, j=PACK)
-        w2_high = rounded[:, vector_share:].rearrange("p (t c j) -> p t c j", t=2, j=PACK)
+        rounded = keep.tile([P, 3, P, PACK], BF16, name="rounded", align_bytes=64)
+        w1_high, w2_high = rounded[:, :2], rounded[:, 1:]
         interleave(nc.scalar.copy, w1_low[:, 0], w1_raw[:], 0)
         interleave(nc.scalar.copy, w1_low[:, 1], w1_raw[:], 1)
         interleave(nc.scalar.copy, w1_high[:, 0], w1_raw[:], 2)
@@ -141,7 +137,7 @@ def tile_picked_tourney_none_p_kernel(
         s_right_1 = keep.tile([P, V], F32, name="s_right_1")
         s_right = [reused[:, u * 2 * V : (u + 1) * 2 * V].bitcast(F32) for u in range(3)]
         s_right = [s_right[0], s_right_1[:], s_right[2], s_right[1]]
-        w3_rounded = reused[:, V : V + N * PACK].rearrange("p (c t) -> p c t", t=PACK)
+        w3_rounded = reused[:, 2 * V : 2 * V + N * PACK].rearrange("p (c t) -> p c t", t=PACK)
         spread = keep.tile([P, PACK, V], F32, name="spread")
         base = keep.tile([P, PACK, V], F32, name="base")
         step = keep.tile([P, PACK, V], F32, name="step")
@@ -210,28 +206,24 @@ def tile_picked_tourney_none_p_kernel(
 
         s0 = keep.tile([P, S], F32, name="s0", align_bytes=64)
         s1 = keep.tile([P, S], F32, name="s1", align_bytes=64)
-        for u in range(3):
+        for u in range(PACK):
             gather_words(u * QUARTER, (u + 1) * QUARTER)
             project(on_scalar, s0, w1_q[0], u * QUARTER, (u + 1) * QUARTER, 2 * u)
             project(on_scalar, s1, w1_q[1], u * QUARTER, (u + 1) * QUARTER, 2 * u + 1)
-        gather_words(S - QUARTER, S)
-        project(on_scalar, s0, w1_q[0], S - QUARTER, S, 6)
         right_scores(s0, 0)
 
         w2_second = keep.tile([P, P, PACK], BF16, name="w2_second", align_bytes=64)
-        w2_first = s1[:, S - QUARTER :].bitcast(BF16).rearrange("p (c j) -> p c j", j=PACK)
-        interleave(on_vector, w2_first, w2_raw[:], 1)
+        w2_first = keep.tile([P, P, PACK], BF16, name="w2_first", align_bytes=64)
+        interleave(on_vector, w2_first[:], w2_raw[:], 1)
         interleave(on_vector, w2_second[:], w2_raw[:], 0)
-        w2_q = [None, quantize(w2_first, "w2_1", tag="diff")]
+        w2_q = [None, quantize(w2_first[:], "w2_1", tag="diff")]
         w2_q[0] = quantize(w2_second[:], "w2_0")
-        interleave(on_vector, w2_high[:, 1, GPSIMD_SHARE:], w2_raw[:, :, GPSIMD_SHARE * PACK :], 3)
-        w1_q.extend(split(quantize(w1_high.rearrange("p t c j -> p (t c) j"), "w1_high", tag="w2_second")))
+        interleave(on_vector, w2_high[:, 1], w2_raw[:], 3)
+        w1_q.extend(split(quantize(w1_high.rearrange("p t c j -> p (t c) j"), "w1_high", tag="w2_first")))
         gpsimd_interleave(w2_high[:, 0], w2_raw[:], 2)
-        gpsimd_interleave(w2_high[:, 1, :GPSIMD_SHARE], w2_raw[:, :, : GPSIMD_SHARE * PACK], 3)
 
         v1 = placed.tile([P, S], F32, name="v1", offset=ROW_BYTES // 2, align_bytes=64)
         v0 = keep.tile([P, S], F32, name="v0", align_bytes=64)
-        project(on_vector, s1, w1_q[1], S - QUARTER, S, 7)
         right_scores(s1, 1)
         project(on_vector, v1, w2_q[1], 0, BANK, 0)
         project(on_vector, v1, w2_q[1], BANK, S, 1)
@@ -241,7 +233,6 @@ def tile_picked_tourney_none_p_kernel(
         project(on_scalar, v0, w2_q[0], BANK, S, 3)
         right_values(v1, 1)
         w2_q.extend(split(quantize(w2_high.rearrange("p t c j -> p (t c) j"), "w2_high")))
-        round_w3(on_vector, 0, P)
         difference(s1, 1)
         right_values(v0, 0)
         value_spread(v1, 1)
@@ -278,27 +269,26 @@ def tile_picked_tourney_none_p_kernel(
             late_step(0, EARLY, t)
         value_spread(v2, 2, EARLY, V)
         z_early = blend(0, EARLY)
-        round_w3(on_scalar, N // 2, N)
-        w3_q = [None, None] + split(quantize(w3_rounded[:, N // 2 :], "w3_high"))
+        round_w3(on_scalar, 0, N // 2)
+        w3_q = split(quantize(w3_rounded[:, : N // 2], "w3_low"))
         early_q = quantize(z_early, "z_early")
         right_values(v3, 3, EARLY, V)
         value_spread(v3, 3, EARLY, V)
         gates(2, 2, EARLY, V)
-        round_w3(on_scalar, P, N // 2)
-        for a in range(2, PACK):
+        round_w3(on_scalar, N // 2, N)
+        for a in range(2):
             store(on_scalar, nc.sync, final_products(early_q, a, 1, a), 0, a)
         for t in (2, 3):
             late_step(EARLY, LAST, t)
-        w3_q[:2] = split(quantize(w3_rounded[:, : N // 2], "w3_low"))
-        for a in range(2):
+        w3_q.extend(split(quantize(w3_rounded[:, N // 2 :], "w3_high")))
+        for a in range(2, PACK):
             store(on_scalar, nc.sync, final_products(early_q, a, 1, a), 0, a)
         z_middle = blend(EARLY, LAST)
         for t in (2, 3):
             late_step(LAST, V, t)
         middle_q = quantize(z_middle, "z_middle")
         store(on_scalar, nc.sync, final_products(middle_q, 0, 2, 4), EARLY, 0)
-        middle_bank = final_products(middle_q, 2, 2, 5)
+        store(on_scalar, nc.sync, final_products(middle_q, 2, 2, 5), EARLY, 2)
         last_q = quantize(blend(LAST, V), "z_last")
-        store(on_vector, nc.sync, middle_bank, EARLY, 2)
         store(on_scalar, nc.scalar, final_products(last_q, 0, 2, 6), LAST, 0)
         store(on_vector, nc.sync, final_products(last_q, 2, 2, 7), LAST, 2)

@@ -165,9 +165,9 @@ def tile_picked_tourney_none_p_kernel(
         def blend(lo, hi):
             z = keep.tile([P, hi - lo, PACK], BF16, name="z%d" % hi, align_bytes=64)
             nc.vector.tensor_tensor(
-                z[:].rearrange("p (c i) t -> p c t i", i=2),
-                base[:, :, lo:hi].rearrange("p t (c i) -> p c t i", i=2),
-                step[:, :, lo:hi].rearrange("p t (c i) -> p c t i", i=2),
+                z[:].rearrange("p (c i) t -> p c t i", i=4),
+                base[:, :, lo:hi].rearrange("p t (c i) -> p c t i", i=4),
+                step[:, :, lo:hi].rearrange("p t (c i) -> p c t i", i=4),
                 ALU.add,
             )
             return z[:]

@@ -290,5 +290,6 @@ def tile_picked_tourney_none_p_kernel(
         store(on_scalar, nc.sync, final_products(middle_q, 0, 2, 4), EARLY, 0)
         store(on_scalar, nc.sync, final_products(middle_q, 2, 2, 5), EARLY, 2)
         last_q = quantize(blend(LAST, V), "z_last")
-        store(on_scalar, nc.scalar, final_products(last_q, 0, 2, 6), LAST, 0)
-        store(on_vector, nc.sync, final_products(last_q, 2, 2, 7), LAST, 2)
+        for a in range(PACK):
+            copy, queue = (on_vector, nc.sync) if a % 2 else (on_scalar, nc.scalar)
+            store(copy, queue, final_products(last_q, a, 1, (6 + a) % 8), LAST, a)

from contextlib import ExitStack

import concourse.mybir as mybir

K, T, S, V, N, H = 512, 2048, 1024, 512, 512, 512
FLOPS = 2 * K * H * S * 2 + 2 * H * N * V

F32 = mybir.dt.float32
BF16 = mybir.dt.bfloat16
I32 = mybir.dt.int32
U32 = mybir.dt.uint32
U16 = mybir.dt.uint16
U8 = mybir.dt.uint8
FP8X4 = mybir.dt.float8_e4m3fn_x4
ALU = mybir.AluOpType
SIGMOID = mybir.ActivationFunctionType.Sigmoid
COPY = mybir.ActivationFunctionType.Copy

P = 128
PACK = 4
BANK = 512
QUARTER = 256
GPSIMD_STEPS = 256
EARLY = 256
LAST = 384
ROW_BYTES = S * 4


def tile_picked_tourney_none_p_kernel(
    tc, x_words, x_scales, w1, w2, w3, offs, left, right, out
):
    nc = tc.nc
    with ExitStack() as ctx:
        lists = ctx.enter_context(tc.tile_pool(name="lists", bufs=1))
        keep = ctx.enter_context(tc.tile_pool(name="keep", bufs=1))
        placed = ctx.enter_context(tc.tile_pool(name="placed", bufs=1))
        psum = ctx.enter_context(tc.psum_pool(name="psum", bufs=1))

        offs_sb = lists.tile([P, S // 16], U16, name="offs_sb")
        left_sb = lists.tile([P, V // 16], U16, name="left_sb")
        right_sb = lists.tile([P, V // 16], U16, name="right_sb")

        scale_table = keep.tile([P, T], U8, name="scale_table")
        word_table = keep.tile([P, T], I32, name="word_table")
        w1_raw = keep.tile([P, PACK, H], F32, name="w1_raw")
        w2_raw = keep.tile([P, PACK, H], F32, name="w2_raw")
        w3_raw = keep.tile([P, PACK, N], F32, name="w3_raw")

        nc.vector.memset(scale_table[:].bitcast(I32), 0)
        warm = keep.tile([P, 2], F32, name="warm")
        nc.gpsimd.memset(warm[:, :1], 0.0)
        nc.scalar.activation(warm[:, 1:], warm[:, :1], SIGMOID)

        w1_rows = w1.rearrange("(p j) c -> p j c", j=PACK)
        nc.sync.dma_start(w1_raw[:, :2], w1_rows[:, :2])
        nc.sync.dma_start(offs_sb[:], offs)
        for r in range(4):
            nc.sync.dma_start(scale_table[r:P:32, :].bitcast(I32), x_scales[0, r:16:4, :].bitcast(I32))
        nc.sync.dma_start(w1_raw[:, 2:], w1_rows[:, 2:])
        nc.sync.dma_start(word_table[:], x_words[0].rearrange("p n r -> p (n r)").bitcast(I32))
        nc.sync.dma_start(w2_raw[:], w2.rearrange("(p j) c -> p j c", j=PACK))
        nc.sync.dma_start(right_sb[:], right)
        nc.sync.dma_start(left_sb[:], left)
        w3_rows = w3.rearrange("(b t r) n -> t b r n", t=PACK, r=8)
        for t in range(PACK):
            nc.sync.dma_start(w3_raw[:, t, :], w3_rows[t])

        x_scale = keep.tile([P, S], U8, name="x_scale", align_bytes=64)
        nc.vector.tensor_copy(x_scale[:], scale_table[:].indirect(offs_sb[:]))

        def interleave(copy, grouped, raw, t):
            copy(
                grouped.rearrange("p (b h i) j -> p b h j i", h=4, i=2),
                raw.rearrange("p j (b t h i) -> p t b h j i", t=PACK, h=4, i=2)[:, t],
            )

        def gpsimd_interleave(grouped, raw, t):
            nc.gpsimd.tensor_scalar(
                grouped.rearrange("p (b r) j -> p b r j", r=8),
                raw.rearrange("p j (b t r) -> p t b r j", t=PACK, r=8)[:, t],
                1.0,
                0.0,
                ALU.mult,
                ALU.add,
            )

        def quantize(grouped, name, tag=None):
            width = grouped.shape[1]
            codes = keep.tile([P, width], U32, name=name + "_codes", tag=tag or name + "_codes", align_bytes=64)
            scale = keep.tile([P, width], U8, name=name + "_scale", align_bytes=64)
            nc.vector.quantize_mx(
                out=codes[:].bitcast(FP8X4), scales=scale[:], in_=grouped.rearrange("p c j -> p (c j)")
            )
            return codes[:], scale[:]

        def split(weight):
            codes, scale = weight
            return [(codes[:, u * P : (u + 1) * P], scale[:, u * P : (u + 1) * P]) for u in range(codes.shape[1] // P)]

        w1_low = keep.tile([P, 2, P, PACK], BF16, name="w1_low", align_bytes=64)
        rounded = keep.tile([P, 3, P, PACK], BF16, name="rounded", align_bytes=64)
        w1_high, w2_high = rounded[:, :2], rounded[:, 1:]
        interleave(nc.scalar.copy, w1_low[:, 0], w1_raw[:], 0)
        interleave(nc.scalar.copy, w1_low[:, 1], w1_raw[:], 1)
        interleave(nc.scalar.copy, w1_high[:, 0], w1_raw[:], 2)
        interleave(nc.scalar.copy, w1_high[:, 1], w1_raw[:], 3)
        w1_q = split(quantize(w1_low[:].rearrange("p t c j -> p (t c) j"), "w1_low"))

        x_codes = keep.tile([P, S], U32, name="x_codes", align_bytes=64)
        word_window = word_table[:].bitcast(U32)

        def gather_words(lo, hi):
            nc.vector.tensor_copy(x_codes[:, lo:hi], word_window.indirect(offs_sb[:, lo // 16 : hi // 16]))

        def product(weight, lo, hi, bank_number):
            codes, scale = weight
            bank = psum.tile([P, hi - lo], F32, name="bank%d" % bank_number)
            nc.tensor.matmul_mx(
                out=bank[:],
                lhsT=codes.bitcast(FP8X4),
                lhsT_scale=scale,
                rhs=x_codes[:, lo:hi].bitcast(FP8X4),
                rhs_scale=x_scale[:, lo:hi],
                start=True,
                stop=True,
            )
            return bank

        def project(copy, rows, weight, lo, hi, bank_number):
            copy(rows[:, lo:hi], product(weight, lo, hi, bank_number)[:])

        def picked(rows, offsets, lo=0, hi=V):
            return rows[:].indirect(offsets[:, lo // 16 : hi // 16])

        gate = keep.tile([P, PACK, V], F32, name="gate")
        reused = keep.tile([P, 3 * 2 * V], BF16, name="reused", align_bytes=64)
        s_right_1 = keep.tile([P, V], F32, name="s_right_1")
        s_right = [reused[:, u * 2 * V : (u + 1) * 2 * V].bitcast(F32) for u in range(3)]
        s_right = [s_right[0], s_right_1[:], s_right[2], s_right[1]]
        w3_rounded = reused[:, 2 * V : 2 * V + N * PACK].rearrange("p (c t) -> p c t", t=PACK)
        spread = keep.tile([P, PACK, V], F32, name="spread")
        base = keep.tile([P, PACK, V], F32, name="base")
        step = keep.tile([P, PACK, V], F32, name="step")

        def right_scores(rows, t):
            nc.scalar.activation(s_right[t], picked(rows, right_sb), COPY)

        def difference(rows, t):
            nc.vector.tensor_tensor(diff[:, t, :], picked(rows, left_sb), s_right[t], ALU.subtract)

        def right_values(rows, t, lo=0, hi=V):
            nc.scalar.activation(base[:, t, lo:hi], picked(rows, right_sb, lo, hi), COPY)

        def value_spread(rows, t, lo=0, hi=V):
            nc.vector.tensor_tensor(
                spread[:, t, lo:hi], picked(rows, left_sb, lo, hi), base[:, t, lo:hi], ALU.subtract
            )

        def gates(first, tiles, lo, hi):
            nc.scalar.activation(gate[:, first : first + tiles, lo:hi], diff[:, first : first + tiles, lo:hi], SIGMOID)

        def late_step(lo, hi, t):
            nc.vector.tensor_tensor(step[:, t, lo:hi], spread[:, t, lo:hi], gate[:, t, lo:hi], ALU.mult)

        def blend(lo, hi):
            z = keep.tile([P, hi - lo, PACK], BF16, name="z%d" % hi, align_bytes=64)
            nc.vector.tensor_tensor(
                z[:].rearrange("p (c i) t -> p c t i", i=4),
                base[:, :, lo:hi].rearrange("p t (c i) -> p c t i", i=4),
                step[:, :, lo:hi].rearrange("p t (c i) -> p c t i", i=4),
                ALU.add,
            )
            return z[:]

        out_rows = out.rearrange("(a p) v -> p a v", p=P)

        def final_products(z_q, first, blocks, bank_number):
            z_codes, z_scale = z_q
            bank = psum.tile([P, blocks, z_codes.shape[1]], F32, name="bank%d" % bank_number)
            for a in range(blocks):
                codes, scale = w3_q[first + a]
                nc.tensor.matmul_mx(
                    out=bank[:, a, :],
                    lhsT=codes.bitcast(FP8X4),
                    lhsT_scale=scale,
                    rhs=z_codes.bitcast(FP8X4),
                    rhs_scale=z_scale,
                    start=True,
                    stop=True,
                )
            return bank

        def store(copy, queue, bank, lo, first):
            blocks, width = bank.shape[1:]
            result = keep.tile([P, blocks, width], F32, name="result%d_%d" % (lo, first))
            copy(result[:], bank[:])
            queue.dma_start(out_rows[:, first : first + blocks, lo : lo + width], result[:])

        def round_w3(copy, lo, hi):
            copy(
                w3_rounded[:, lo:hi].rearrange("p (c i) t -> p c t i", i=2),
                w3_raw[:, :, lo:hi].rearrange("p t (c i) -> p c t i", i=2),
            )

        on_scalar, on_vector = nc.scalar.copy, nc.vector.tensor_copy

        s0 = keep.tile([P, S], F32, name="s0", align_bytes=64)
        s1 = keep.tile([P, S], F32, name="s1", align_bytes=64)
        for u in range(PACK):
            gather_words(u * QUARTER, (u + 1) * QUARTER)
            project(on_scalar, s0, w1_q[0], u * QUARTER, (u + 1) * QUARTER, 2 * u)
            project(on_scalar, s1, w1_q[1], u * QUARTER, (u + 1) * QUARTER, 2 * u + 1)
        right_scores(s0, 0)

        w2_second = keep.tile([P, P, PACK], BF16, name="w2_second", align_bytes=64)
        w2_first = keep.tile([P, P, PACK], BF16, name="w2_first", align_bytes=64)
        interleave(on_vector, w2_first[:], w2_raw[:], 1)
        interleave(on_vector, w2_second[:], w2_raw[:], 0)
        w2_q = [None, quantize(w2_first[:], "w2_1", tag="diff")]
        w2_q[0] = quantize(w2_second[:], "w2_0")
        interleave(on_vector, w2_high[:, 1], w2_raw[:], 3)
        w1_q.extend(split(quantize(w1_high.rearrange("p t c j -> p (t c) j"), "w1_high", tag="w2_first")))
        gpsimd_interleave(w2_high[:, 0], w2_raw[:], 2)

        v1 = placed.tile([P, S], F32, name="v1", offset=ROW_BYTES // 2, align_bytes=64)
        v0 = keep.tile([P, S], F32, name="v0", align_bytes=64)
        right_scores(s1, 1)
        project(on_vector, v1, w2_q[1], 0, BANK, 0)
        project(on_vector, v1, w2_q[1], BANK, S, 1)
        project(on_vector, v0, w2_q[0], 0, BANK, 2)
        diff = keep.tile([P, PACK, V], F32, name="diff", align_bytes=64)
        difference(s0, 0)
        project(on_scalar, v0, w2_q[0], BANK, S, 3)
        right_values(v1, 1)
        w2_q.extend(split(quantize(w2_high.rearrange("p t c j -> p (t c) j"), "w2_high")))
        difference(s1, 1)
        right_values(v0, 0)
        value_spread(v1, 1)
        gates(0, 1, 0, V)
        value_spread(v0, 0)
        nc.gpsimd.tensor_tensor(step[:, 0, :], spread[:, 0, :], gate[:, 0, :], ALU.mult)

        s3 = placed.tile([P, S], F32, name="s3", offset=0, align_bytes=64)
        v2 = placed.tile([P, S], F32, name="v2", offset=ROW_BYTES, align_bytes=64)
        s2 = keep.tile([P, S], F32, name="s2", tag="s1", align_bytes=64)
        v3 = keep.tile([P, S], F32, name="v3", tag="v0", align_bytes=64)
        project(on_vector, s3, w1_q[3], 0, BANK, 0)
        project(on_vector, s3, w1_q[3], BANK, S, 1)
        project(on_scalar, s2, w1_q[2], 0, BANK, 4)
        project(on_scalar, s2, w1_q[2], BANK, S, 5)
        gates(1, 1, 0, V)
        nc.gpsimd.tensor_tensor(step[:, 1, :GPSIMD_STEPS], spread[:, 1, :GPSIMD_STEPS], gate[:, 1, :GPSIMD_STEPS], ALU.mult)
        project(on_vector, v2, w2_q[2], 0, BANK, 2)
        project(on_vector, v2, w2_q[2], BANK, S, 3)
        late_step(GPSIMD_STEPS, V, 1)
        right_scores(s2, 2)
        difference(s2, 2)
        right_scores(s3, 3)
        difference(s3, 3)
        project(on_scalar, v3, w2_q[3], 0, BANK, 6)
        project(on_scalar, v3, w2_q[3], BANK, S, 7)
        right_values(v2, 2, 0, EARLY)
        right_values(v3, 3, 0, EARLY)
        gates(2, 2, 0, EARLY)
        value_spread(v2, 2, 0, EARLY)
        value_spread(v3, 3, 0, EARLY)
        right_values(v2, 2, EARLY, V)
        for t in (2, 3):
            late_step(0, EARLY, t)
        value_spread(v2, 2, EARLY, V)
        z_early = blend(0, EARLY)
        round_w3(on_scalar, 0, N // 2)
        w3_q = split(quantize(w3_rounded[:, : N // 2], "w3_low"))
        early_q = quantize(z_early, "z_early")
        right_values(v3, 3, EARLY, V)
        value_spread(v3, 3, EARLY, V)
        gates(2, 2, EARLY, V)
        round_w3(on_scalar, N // 2, N)
        for a in range(2):
            store(on_scalar, nc.sync, final_products(early_q, a, 1, a), 0, a)
        for t in (2, 3):
            late_step(EARLY, LAST, t)
        w3_q.extend(split(quantize(w3_rounded[:, N // 2 :], "w3_high")))
        for a in range(2, PACK):
            store(on_scalar, nc.sync, final_products(early_q, a, 1, a), 0, a)
        z_middle = blend(EARLY, LAST)
        for t in (2, 3):
            late_step(LAST, V, t)
        middle_q = quantize(z_middle, "z_middle")
        store(on_scalar, nc.sync, final_products(middle_q, 0, 2, 4), EARLY, 0)
        store(on_scalar, nc.sync, final_products(middle_q, 2, 2, 5), EARLY, 2)
        last_q = quantize(blend(LAST, V), "z_last")
        for a in range(PACK):
            copy, queue = (on_vector, nc.sync) if a % 2 else (on_scalar, nc.scalar)
            store(copy, queue, final_products(last_q, a, 1, (6 + a) % 8), LAST, a)
